import numpy as np, ml_dtypes
CORES = [6,15,38,47]
N = 4
BF = ml_dtypes.bfloat16
T, NC, GY, W, H, HW = 512, 2048, 32, 128, 64, 8192
LZ, ZS, UN, P = 8192, 2, 32, 3
def poses(rng, a, b):
    p = np.zeros((N, 8, 6), np.int64); p[..., 0] = a; p[..., 1] = b
    p[..., 2] = rng.integers(-4000, 4001, (N, 8)) - (256 * a + 4 * GY * b)
    p[..., 3] = rng.integers(-4000, 4001, (N, 8)) + 16384 - (4 * GY * a - 256 * b)
    p[..., 4] = rng.integers(-5 * H, 5 * H + 1, (N, 8)); p[..., 5] = rng.integers(LZ // 16, LZ // 3, (N, 8))
    return p.astype(np.int32)
def image(v):
    return v.astype(np.float32).astype(BF)
def setup_inputs(rng):
    w = rng.random((N, 1)) * 2 * np.pi; j = rng.integers(-2, 3, (2, N, 8))
    a = np.clip(np.rint(64 * np.cos(w)).astype(np.int64) + j[0], -64, 64); b = np.clip(np.rint(64 * np.sin(w)).astype(np.int64) + j[1], -64, 64)
    v = rng.integers(-31, 32, (N, 16, HW)); v[:, :2] = rng.integers(-12, 13, (N, 2, HW)); v[:, 15] = rng.integers(0, 256, (N, HW))
    return {"cam": image(v), "lens": rng.integers(0, 1024, (N, 8, LZ)).astype(np.int32), "pose": poses(rng, a, b)}
def setup_inputs_ends(rng):
    d = setup_inputs(rng); p = d["pose"]; e = d["lens"]; top = 32768 - 512 * (GY - 1)
    p[..., 0] = 64; p[..., 1] = 0; p[..., 2] = rng.integers(-2000, 2001, (N, 8)) - 16384; p[..., 5] = LZ
    p[..., 3] = rng.permuted(np.tile(np.array([0, -1, top - 1, top]), (N, 2, 1)), axis=2).reshape(N, 8)
    e[:] = np.where(rng.random(e.shape) < 0.75, e, rng.choice(np.array([0, 1, 4095]), e.shape))
    e[:, :, 0] = rng.integers(1, 256, (N, 8)); e[:, :, LZ - 1] = rng.integers(1, 256, (N, 8)); e[:, 4:] = 1024
    p[:, 4, 4] = -2 * H - 1; p[:, 5, 4] = 2 * H; p[:, 6, 4] = 2 * H - 1; p[:, 7, 4] = -2 * H
    p[:, 6, 2] = 384 - 16384; p[:, 7, 2] = -16384
    return d
def setup_inputs_ties(rng):
    d = setup_inputs(rng); a = 16 * rng.integers(1, 4, (N, 8)) * rng.choice(np.array([-1, 1]), (N, 8)); b = 16 * rng.integers(-2, 3, (N, 8))
    p = poses(rng, a, b); p[..., 3] = p[..., 3] & -128
    p[..., 5] = rng.permuted(np.tile(UN * np.array([0, 1, 32, 64]), (N, 2, 1)), axis=2).reshape(N, 8)
    d["pose"] = p; return d
def setup_inputs_one(rng):
    d = setup_inputs(rng); d["lens"][:, :4] = 0; d["pose"][:, :2, 5] = LZ
    v = d["cam"].astype(np.float32); v[:, :2] = rng.choice(np.array([-31, 31]), (N, 2, HW)); d["cam"] = image(v); return d
def setup_inputs_blind(rng):
    d = setup_inputs(rng); q = rng.permutation(N); p = d["pose"]
    p[q[0], :, 0] = 64; p[q[0], :, 1] = 0; p[q[0], :, 3] = -49152; p[q[1], :, 5] = 0
    v = d["cam"].astype(np.float32); v[q[2], 15] = 0; d["cam"] = image(v); return d
def setup_inputs_spread(rng):
    d = setup_inputs(rng); p = d["pose"]
    v = rng.integers(-31, 32, (N, 16, HW)); v = np.sign(v) * (np.abs(v) >> rng.integers(0, 6, (N, 1, HW))); v[:, 15] = rng.integers(0, 256, (N, HW)) >> rng.integers(0, 3, (N, HW))
    d["cam"] = image(v); d["lens"] = (rng.integers(0, 4096, (N, 8, LZ)) >> rng.integers(0, 8, (N, 8, LZ))).astype(np.int32)
    y = rng.integers(-4095, 4096, (N, 8)); p[..., 4] = np.sign(y) * (np.abs(y) >> rng.integers(0, 8, (N, 8)))
    p[..., 5] = rng.integers(LZ // 4, LZ + 1, (N, 8)) >> rng.integers(0, 6, (N, 8)); return d
def check_inputs(d):
    bad = []; c = d["cam"].astype(np.float32); p = d["pose"].astype(np.int64); e = d["lens"]
    if not (np.isfinite(c).all() and (c == np.floor(c)).all()): bad.append("whole numbers in cam")
    if not (np.abs(c[:, :15]) <= 31).all(): bad.append("features")
    if not ((c[:, 15] >= 0) & (c[:, 15] <= 255)).all(): bad.append("depth")
    if not ((e >= 0) & (e <= 4095)).all(): bad.append("lens")
    if not (np.abs(p[..., 0:2]) <= 64).all(): bad.append("turning numbers")
    if not (np.abs(p[..., 2:4]) <= 49152).all(): bad.append("offsets")
    if not (np.abs(p[..., 4]) <= 4095).all(): bad.append("height")
    if not ((p[..., 5] >= 0) & (p[..., 5] <= LZ)).all(): bad.append("tolerance")
    return bad
def reference(cam, lens, pose):
    c = np.arange(NC); sx = np.zeros(NC, np.int64); sy = np.zeros(NC, np.int64)
    im = np.concatenate([cam.astype(np.float32), np.zeros((N, 16, 1), np.float32)], 2).astype(np.int64)
    for k in range(P):
        gx = 8 * (c & 63) + sx; gy = 8 * (c >> 6) + sy; s = np.zeros((16, NC), np.int64)
        for r in range(N):
            for g in range(8):
                a, b, tx, tz, h, tol = [int(v) for v in pose[r, g]]
                x = (a * gx + b * gy + tx) >> 5; z = (a * gy - b * gx + tz) >> ZS
                near = (z >= 0) & (z < LZ); m = lens[r, g][np.where(near, z, 0)].astype(np.int64)
                u = ((x * m) >> 12) + W // 2; v = ((h * m) >> 12) + H // 2
                seen = near & (u >= 0) & (u < W) & (v >= 0) & (v < H)
                t = im[r][:, np.where(seen, W * v + u, HW)]
                s += t * (np.abs(UN * t[15] - z) <= tol)
        sx = np.minimum(np.maximum(s[0], -31), 31); sy = np.minimum(np.maximum(s[1], -31), 31)
    y = np.ascontiguousarray(s.reshape(16, N, T).transpose(1, 0, 2)).astype(np.float32)
    return {"y": y}

@@ -1,0 +1,535 @@
+from concourse.bass import DstId, RemoteDMATransfer
+from concourse.mybir import AluOpType as A, ActivationFunctionType as F
+
+N = 4
+HW = 8192
+PAD = 128
+WC = HW + 2 * PAD
+NP = 16
+PIECE = WC // NP
+BIG = float(1 << 22)
+CFG = dict(GV=30, ZS=4, ZG=2, FOLD=False, TRIES=2500, SEED=1)
+b16, f32, f16, i32, u16 = "bfloat16", "float32", "float16", "int32", "uint16"
+
+SCRATCH = {}
+for _d, _w, _names in (
+    (b16, WC, "W1 W2"), (b16, HW, "C3"), (i32, 512, "L"), (b16, 512, "Lhi Llo Lv"), (i32, 8, "Pi"),
+    (f32, 8, "Pf S4 S32 S8 hc c1 c2 stmp"), (f32, 128, "ones I32 GO Qr GOq KX KY Ta Tb Tc Td NB A8 mk M0 M1"),
+    (b16, 128, "Ib I128 Ibig WZ0 WZ1 WD"), (f16, 128, "I16"), (f32, 64, "NB2 MT wtmp"), (f32, 24, "LAB"),
+    (i32, 128, "mi mj"), (i32, 16, "gi gj"), (b16, 16, "GSEL SEL1"), (b16, 32, "SEL2"), (b16, 64, "WX Rs"),
+    (b16, 256, "ZR LAND"), (f16, 256, "LY Ys"),
+    (f32, 128, "RZ0 RZ1 RX0 RX1 RDa0 RDa1 RDb0 RDb1 D00 D01 Fo0 Fo1"), (b16, 128, "SP0 SP1"),
+    (f32, 64, "X00 X01 t0 t1 au0 au1 Xk0 Xk1 keep0 keep1"), (u16, 64, "zoff0 zoff1 off0 off1 offb0 offb1"),
+    (i32, 64, "xi0 xi1"), (b16, 64, "pen0 pen1"), (b16, 1024, "G0 G1"),
+):
+    for _n in _names.split():
+        SCRATCH[_n] = ("sbuf", [128, _w], _d)
+for _h in "01":
+    for _n in ("Bu", "Bv", "Bd"):
+        SCRATCH[_n + _h] = ("sbuf", [128, 17, 8], b16)
+    for _n in ("Pp", "Pq"):
+        SCRATCH[_n + _h] = ("sbuf", [128, 8, 2, 8], b16)
+    for _n in "ABCD":
+        SCRATCH["ps" + _n + _h] = ("psum", [128, 512], f32)
+
+DMAS = ["dL", "dP", "dC3", "dC", "dHi", "dLo", "dV", "dWa", "dWb", "dYa0", "dYb0", "dYa1", "dYb1"]
+SEMAPHORES = ["sV", "sS", "sP", "sG", "sent"] + ["arr%d_%d" % (k, r) for k in range(6) for r in range(N)] + DMAS
+
+
+def build(g, core, T, topo):
+    rank = T.rank_of(core)
+    ops, res, banks, cur = [], {}, {}, [0]
+    V, S, PE = g.vector, g.scalar, g.tensor
+    GV = CFG["GV"]
+
+    def op(eng, fn, cost, r=(), w=(), b=None, after=(), sem=None, val=0):
+        k = len(ops)
+        deps = set(after)
+        for x in r:
+            st = res.setdefault(x, [None, []])
+            if st[0] is not None:
+                deps.add(st[0])
+        for x in w:
+            st = res.setdefault(x, [None, []])
+            if st[0] is not None:
+                deps.add(st[0])
+            deps.update(st[1])
+        for x in r:
+            res[x][1].append(k)
+        for x in w:
+            res[x] = [k, []]
+        if b is not None:
+            st = banks.setdefault(b, [None, [], []])
+            if st[0] == eng:
+                deps.update(st[2])
+                if eng == "P":
+                    deps.add(st[1][-1])
+                st[1].append(k)
+            else:
+                deps.update(st[1])
+                banks[b] = [eng, [k], st[1]]
+        deps.discard(k)
+        ops.append(dict(eng=eng, fn=fn, cost=cost, deps=deps, sem=sem, val=val, half=cur[0], tag=(list(w) + [b])[0]))
+        return k
+
+    def ts(out, in0, s1, s2, o0, o1, n, r, w, b=None):
+        if o1 is None:
+            return op("V", lambda: V.tensor_scalar(out, in0, s1, None, o0), ("v", n), r, w, b)
+        return op("V", lambda: V.tensor_scalar(out, in0, s1, s2, o0, o1), ("v", n), r, w, b)
+
+    def tt(out, a, c, o, n, r, w, b=None):
+        return op("V", lambda: V.tensor_tensor(out, a, c, o), ("v", n), r, w, b)
+
+    def cpy(out, a, n, r, w, b=None):
+        return op("V", lambda: V.tensor_copy(out, a), ("v", n), r, w, b)
+
+    def fill(ap, c, n, w):
+        return op("V", lambda: V.memset(ap, c), ("v", n), (), w)
+
+    def act(out, a, n, r, w, b=None, bias=0.0, scale=1.0, f=F.Identity):
+        return op("S", lambda: S.activation(out, a, f, bias=bias, scale=scale), ("v", n), r, w, b)
+
+    def mm(lst, cyc, r, b, after=()):
+        def fn():
+            last = None
+            for o, l, x, st, sp in lst:
+                last = PE.matmul(o, l, x, st, sp)
+            return last
+        return op("P", fn, ("p", cyc), r, (), b, after)
+
+    def iota(out, pat, base, cm, n, w, flt=True):
+        if flt:
+            return op("G", lambda: g.iota(out, pat, base, cm, allow_small_or_imprecise_dtypes=True), ("g", n), (), w)
+        return op("G", lambda: g.iota(out, pat, base, cm), ("g", n), (), w)
+
+    def asel(out, a, pat, cm, n, r, w):
+        return op("G", lambda: g.affine_select(out, a, pat, A.is_equal, 0.0, 0, cm), ("g", n), r, w)
+
+    def dma(q, sem, pairs, kb, r, w, after=()):
+        e = g.sync if q == "Y" else S
+
+        def fn():
+            for o, i in pairs:
+                e.dma_start(o, i).then_inc(T.sem[sem], 16)
+        return op(q, fn, ("d", len(pairs), kb), r, w, None, after, sem, 16 * len(pairs))
+
+    def gather(eng, out, win, offs, cols, r, w):
+        src = win[:, 0:WC].indirect(offs)
+        if eng == "V":
+            return op("V", lambda: V.tensor_copy(out, src), ("i", 16 * cols), r, w)
+        return op("S", lambda: S.activation(out, src, F.Copy), ("i", 16 * cols), r, w)
+
+    peers = [(rank + d) % N for d in (1, 2, 3)]
+    dst = {}
+    mask = -1
+    for p in peers:
+        rid, pid, _se = topo.addr(T.cores[p])
+        dst[p] = (rid, pid)
+        mask &= topo.mask(core, T.cores[p])
+    neng = bin(mask).count("1")
+    sent = [0]
+    r8 = lambda t, a=0, b=128: t[0:8, a:b]
+    r16 = lambda t, a=0, b=128: t[0:16, a:b]
+
+    dma("Y", "dL", [(T.L[:], T.lens[:])], 256, (), ["L"])
+    dma("S", "dP", [(r8(T.Pi, 0, 6), T.pose[:])], 0, (), ["Pi"])
+    dma("Y", "dC3", [(T.C3[0:2, :], T.cam[0:2, :]), (T.C3[2:3, :], T.cam[15:16, :])], 48, (), ["C3"])
+
+    zn = ["Wz%d" % k for k in range(NP)]
+    fill(T.W1[:, 0:PIECE], 0.0, PIECE // 2, [zn[0]])
+    iota(T.ones[:], [[0, 128]], 1, 0, 128, ["ones"])
+    asel(r8(T.GO), r8(T.ones), [[1, 8], [0, 16]], -1, 128, ["ones"], ["GO"])
+    for k in range(1, NP):
+        piece = T.W1[:, k * PIECE:(k + 1) * PIECE]
+        if k <= CFG["ZS"]:
+            act(piece, T.W1[:, 0:PIECE], PIECE, [zn[0]], [zn[k]])
+        elif k <= CFG["ZS"] + CFG["ZG"]:
+            iota(piece, [[0, PIECE]], 0, 0, PIECE, [zn[k]])
+        else:
+            fill(piece, 0.0, PIECE // 2, [zn[k]])
+
+    iota(r8(T.KX), [[0, 16], [64, 8]], 0, 0, 128, ["KX"])
+    iota(r8(T.KY), [[64, 4], [8, 4], [0, 8]], 0, 0, 128, ["KY"])
+    iota(r8(T.Qr), [[0, 8], [1, 16]], 0, 0, 128, ["Qr"])
+    asel(r8(T.GOq), r8(T.Qr), [[1, 8], [0, 16]], -1, 128, ["Qr"], ["GOq"])
+    asel(T.I32[:], T.ones[:], [[-1, 128]], 1, 128, ["ones"], ["I32"])
+    GT, GTc = T.GO[0:8, ::2], T.GOq[0:8, ::2]
+
+    Pf = r8(T.Pf, 0, 6)
+    cpy(Pf, r8(T.Pi, 0, 6), 6, ["Pi"], ["Pf"])
+    mm([(T.psB1[:, 128:134], r8(T.GO), Pf, True, True)], 256, ["GO", "Pf"], "B1")
+    act(T.hc[:, 0:6], T.psB1[:, 128:134], 6, (), ["hc"], "B1", scale=1.0 / 4096)
+
+    cpy(T.psA1[:], T.L[:], 512, ["L"], (), "A1")
+    act(T.Lv[:], T.psA1[:], 512, ["hc"], ["Lv"], "A1", scale=T.hc[:, 4:5], bias=191.5 + 1.0 / 8192)
+    cpy(T.Lhi[:], T.L[:], 512, ["L"], ["Lhi"])
+    tt(T.Llo[:], T.psA1[:], T.Lhi[:], A.subtract, 512, ["Lhi"], ["Llo"], "A1")
+    dma("Y", "dHi", [(T.W1[3::16, PAD:PAD + HW], T.Lhi[:])], 128, zn + ["Lhi"], ["Whi"])
+    dma("S", "dV", [(T.W1[5::16, PAD:PAD + HW], T.Lv[:])], 128, zn + ["Lv"], ["Wv"])
+    dma("Y", "dLo", [(T.W1[4::16, PAD:PAD + HW], T.Llo[:])], 128, zn + ["Llo"], ["Wlo"])
+    dma("Y", "dC", [(T.W1[16 * a:16 * a + 3, PAD:PAD + HW], T.C3[0:3, :]) for a in range(8)], 384, zn + ["C3"], ["Wc"])
+    win1 = zn + ["Whi", "Wlo", "Wv", "Wc"]
+
+    act(r8(T.S4, 0, 6), Pf, 6, ["Pf"], ["S4"], scale=0.25)
+    act(r8(T.S32, 0, 6), Pf, 6, ["Pf"], ["S32"], scale=1.0 / 32)
+    act(r8(T.S8, 0, 6), Pf, 6, ["Pf"], ["S8"], scale=8.0)
+    act(r8(T.Ta), r8(T.KY), 128, ["KY", "S4"], ["Ta"], scale=r8(T.S4, 0, 1), bias=r8(T.S4, 3, 4))
+    ts(r8(T.Tb), r8(T.KX), r8(T.S4, 1, 2), -(PAD - 0.375), A.mult, A.add, 128, ["KX", "S4"], ["Tb"])
+    tt(r8(T.RZ0), r8(T.Ta), r8(T.Tb), A.subtract, 256, ["Ta", "Tb"], ["RZ0"])
+    act(r8(T.RZ1), r8(T.RZ0), 128, ["RZ0", "S8"], ["RZ1"], bias=r8(T.S8, 0, 1))
+    ts(r8(T.NB2, 0, 64), r8(T.ones, 0, 64), r8(T.Pf, 1, 2), -2.0, A.mult, A.mult, 64, ["ones", "Pf"], ["NB2"])
+    act(r8(T.Tc), r8(T.KX), 128, ["KX", "S32"], ["Tc"], scale=r8(T.S32, 0, 1), bias=r8(T.S32, 2, 3))
+    ts(r8(T.Td), r8(T.KY), r8(T.S32, 1, 2), -31.0 / 64, A.mult, A.add, 128, ["KY", "S32"], ["Td"])
+    tt(r8(T.RX0), r8(T.Tc), r8(T.Td), A.add, 256, ["Tc", "Td"], ["RX0"])
+    act(r8(T.RX1), r8(T.RX0), 128, ["RX0", "Pf"], ["RX1"], bias=r8(T.Pf, 1, 2))
+    ts(r8(T.NB), r8(T.ones), r8(T.Pf, 1, 2), -1.0, A.mult, A.mult, 128, ["ones", "Pf"], ["NB"])
+    ts(r8(T.A8), r8(T.ones), r8(T.Pf, 0, 1), 0.125, A.mult, A.mult, 128, ["ones", "Pf"], ["A8"])
+    act(r8(T.c1, 0, 6), Pf, 6, ["Pf"], ["c1"], scale=-1.0, bias=-(PAD + 0.5))
+    act(r8(T.c2, 0, 6), Pf, 6, ["Pf"], ["c2"], bias=-(PAD - 0.5))
+
+    cpy(T.Ib[:], T.I32[:], 128, ["I32"], ["Ib"])
+    act(T.I128[:], T.I32[:], 128, ["I32"], ["I128"], scale=128.0)
+    tt(T.stmp[:], T.I32[:, 3::16], T.I32[:, 4::16], A.add, 16, ["I32"], ["stmp"])
+    ts(T.SEL1[:, 0:8], T.stmp[:], 1.0 / 4096, None, A.mult, None, 8, ["stmp"], ["SEL1a"])
+    act(T.SEL1[:, 8:16], T.I32[:, 5::16], 8, ["I32"], ["SEL1b"])
+    act(T.SEL2[:, 0:8], T.I32[:, 2::16], 8, ["I32"], ["SEL2a"], scale=-32.0)
+    act(T.SEL2[:, 8:16], T.I32[:, 2::16], 8, ["I32"], ["SEL2b"], scale=32.0)
+    act(T.SEL2[:, 16:24], T.I32[:, 0::16], 8, ["I32"], ["SEL2c"])
+    act(T.SEL2[:, 24:32], T.I32[:, 1::16], 8, ["I32"], ["SEL2d"])
+    sel2 = ["SEL2a", "SEL2b", "SEL2c", "SEL2d"]
+    fill(r16(T.ZR, 0, 256), 0.0, 128, ["ZR"])
+    for nm in ("Bu0", "Bv0", "Bu1", "Bv1"):
+        fill(T[nm][:], 0.0, 68, [nm])
+
+    def late_setup():
+        iota(r16(T.mi), [[0, 8], [-1, 16]], 16, 1, 128, ["mi"], False)
+        ts(r16(T.mj), r16(T.mi), 7, None, A.bitwise_and, None, 128, ["mi"], ["mj"])
+        ts(r16(T.M0), r16(T.mj), 0.0, 0.25, A.is_equal, A.mult, 128, ["mj"], ["M0"])
+        act(r16(T.MT, 0, 64), r16(T.M0, 0, 64), 64, ["M0"], ["MT"])
+        iota(r16(T.mk), [[0, 8], [1, 2], [0, 8]], 0, 0, 128, ["mk"])
+        tt(r16(T.M1), r16(T.M0), r16(T.mk), A.mult, 256, ["M0", "mk"], ["M1"])
+        tt(r16(T.M0), r16(T.M0), r16(T.M1), A.subtract, 256, ["M1"], ["M0"])
+        act(r8(T.LAB, 0, 8), r8(T.NB, 0, 8), 8, ["NB"], ["LABa"])
+        act(r8(T.LAB, 8, 16), r8(T.A8, 0, 8), 8, ["A8"], ["LABb"], scale=8.0)
+        act(r8(T.LAB, 16, 24), r8(T.NB, 0, 8), 8, ["NB"], ["LABc"], scale=-1.0)
+        ps, MT = T.psB0, r16(T.MT, 0, 64)
+        mm([(r16(ps, 128, 256), r8(T.LAB, 0, 16), r8(T.GO), True, True),
+            (r16(ps, 256, 320), r8(T.LAB, 8, 24), GT, True, True)], 768, ["LABa", "LABb", "LABc", "GO"], "B0")
+        tt(r16(T.WZ0), r16(ps, 128, 256), r16(T.M0), A.mult, 128, ["M0"], ["WZ0"], "B0")
+        tt(r16(T.WZ1), r16(ps, 128, 256), r16(T.M1), A.mult, 128, ["M1"], ["WZ1"], "B0")
+        tt(r16(T.WD, 0, 64), ps[0:16, 128:256:2], MT, A.mult, 64, ["MT"], ["WDa"], "B0")
+        tt(r16(T.wtmp, 0, 64), r16(ps, 256, 320), MT, A.mult, 64, ["MT"], ["wtmp"], "B0")
+        act(r16(T.WX, 0, 64), r16(T.wtmp, 0, 64), 64, ["wtmp"], ["WX"], scale=0.125)
+        act(r16(T.WD, 64, 128), r16(T.WD, 0, 64), 64, ["WDa"], ["WDb"], scale=-1.0)
+
+    def last_setup():
+        fill(T.W2[:, 0:PAD], 0.0, 64, ["W2a"])
+        fill(T.W2[:, PAD + HW:WC], 0.0, 64, ["W2b"])
+        act(T.Ibig[:], T.I32[:], 128, ["I32"], ["Ibig"], scale=BIG)
+        cpy(T.I16[:], T.I32[:], 128, ["I32"], ["I16"])
+        iota(T.gi[:], [[-1, 16]], 16, 1, 16, ["gi"], False)
+        ts(T.gj[:], T.gi[:], 15, None, A.bitwise_and, None, 16, ["gi"], ["gj"])
+        ts(T.GSEL[:], T.gj[:], 0.0, None, A.is_equal, None, 16, ["gj"], ["GSEL"])
+        for nm in ("Bd0", "Bd1"):
+            fill(T[nm][:], 0.0, 68, [nm])
+
+    arrived = {}
+    senders = peers[::-1]
+
+    def half_pass(p, h):
+        cur[0] = h
+        n = lambda s: "%s%d" % (s, h)
+        B = lambda s: T[n(s)]
+        pA, pB, pC, pD = B("psA"), B("psB"), B("psC"), B("psD")
+        bA, bB, bC, bD = n("A"), n("B"), n("C"), n("D")
+        G = B("G")
+        psZ, psX = pB[:, 0:64], pC[:, 0:64]
+        mm([(psZ, r8(T.GO), B("RZ")[0:8, ::2], True, False),
+            (psZ, r8(T.GOq), r8(T.NB2, 0, 64), False, p == 0)], 512, ["GO", "GOq", n("RZ"), "NB2"], bB)
+        if p == 0:
+            mm([(psX, r8(B("RX")), GT, True, False), (psX, r8(T.A8), GTc, False, True)], 512,
+               ["GO", "GOq", n("RX"), "A8"], bC)
+            cpy(B("xi")[:], psX, 64, (), [n("xi")], bC)
+            act(B("X0")[:], psX, 64, (), [n("X0")], bC)
+            act(r8(B("RDa")), r8(B("RZ")), 128, [n("RZ"), "c1"], [n("RDa")], bias=r8(T.c1, 5, 6))
+            act(r8(B("RDb")), r8(B("RZ")), 128, [n("RZ"), "c2"], [n("RDb")], bias=r8(T.c2, 5, 6))
+            mm([(pD[:, 256:320], r8(B("RDa")), GT, True, False), (pD[:, 256:320], r8(T.NB), GTc, False, True),
+                (pD[:, 320:384], r8(B("RDb")), GT, True, False), (pD[:, 320:384], r8(T.NB), GTc, False, True)],
+               1024, ["GO", "GOq", n("RDa"), n("RDb"), "NB"], bD)
+            act(B("D0")[:, 0:64], pD[:, 256:320], 64, (), [n("D0a")], bD)
+            act(B("D0")[:, 64:128], pD[:, 320:384], 64, (), [n("D0b")], bD, scale=-1.0)
+        mm([(pD[:, 0:256], r16(T.ZR), r16(T.ZR, 0, 256), True, False)], 256, ["ZR"], bD)
+        mm([(pD[:, 0:128], T.I32[:], B("D0")[:], False, False)], 512, ["I32", n("D0a"), n("D0b")], bD)
+        if p > 0:
+            s = 2 * (p - 1) + h
+            psS = r16(pA)
+            if CFG["FOLD"]:
+                P = B("Pp" if p == 1 else "Pq")
+                mm([(psS, P[:, a, :, :], T.Ib[:], a == 0, False) for a in range(8)], 1024, ["Pa%d" % s, "Pb%d" % s, "Ib"], bA)
+            else:
+                mm([(psS, T.Rs[:, 16 * s:16 * s + 16], T.Ib[:], True, False)], 128, ["Rs%d" % s, "Ib"], bA)
+            for j, q in enumerate(senders):
+                mm([(psS, T.LAND[:, 16 * (N * s + q):16 * (N * s + q) + 16], T.Ib[:], False, j == 2)],
+                   128, ["Ib"], bA, [arrived[(p - 1, h)][j]])
+            SP = B("SP")
+            ts(r16(SP), psS, -31.0, 31.0, A.max, A.min, 128, (), [n("SP")], bA)
+            mm([(psZ, r16(T.WZ0), SP[0:16, 0::2], False, False), (psZ, r16(T.WZ1), SP[0:16, 1::2], False, True)],
+               128, ["WZ0", "WZ1", n("SP")], bB)
+            mm([(psX, r16(SP), r16(T.WX, 0, 64), True, True)], 64, ["WX", n("SP")], bC)
+            tt(B("xi")[:], psX, B("X0")[:], A.add, 64, [n("X0")], [n("xi")], bC)
+            mm([(pD[:, 0:128], r16(SP), r16(T.WD), False, False)], 128, ["WDa", "WDb", n("SP")], bD)
+
+        ts(B("zoff")[:], psZ, 0.0, float(WC - 1), A.max, A.min, 64, (), [n("zoff")], bB)
+        gather("V", G[:, 0:16 * GV], T.W1, B("zoff")[:, 0:GV], GV, win1 + [n("zoff")], [n("Ga")])
+        gather("S", G[:, 16 * GV:1024], T.W1, B("zoff")[:, GV:64], 64 - GV, win1 + [n("zoff")], [n("Gb")])
+        mm([(pC[:, 128 + c:256:8], G[:, c::8], T.SEL1[:], True, True) for c in range(8)], 512,
+           [n("Ga"), n("Gb"), "SEL1a", "SEL1b"], bC)
+        tt(B("t")[:], pC[:, 128:192], B("xi")[:], A.mult, 64, [n("xi")], [n("t")], bC)
+        act(B("Bv")[:, 1::2, :], pC[:, 192:256], 64, (), [n("Bv")], bC, bias=-160.0)
+        ts(B("Bu")[:, 1::2, :], B("t")[:], 191.5 + 1.0 / 8192, 128.0, A.add, A.max, 64, [n("t")], [n("Bu")])
+
+        def turn(ps, buf, ident, first, last):
+            return [(ps, buf[:, 1:17, :], ident[:, 0::2], first, False), (ps, buf[:, 0:16, :], ident[:, 1::2], False, last)]
+        psO = pA[:, 128:192]
+        mm(turn(psO, B("Bu"), T.Ib, True, False) + turn(psO, B("Bv"), T.I128, False, True), 256,
+           [n("Bu"), n("Bv"), "Ib", "I128"], bA)
+        ts(B("off")[:], psO, 0.0, float(WC - 1), A.max, A.min, 64, (), [n("off")], bA)
+        gather("V", G[:, 0:16 * GV], T.W1, B("off")[:, 0:GV], GV, win1 + [n("off")], [n("Ga")])
+        act(B("au")[:], B("t")[:], 64, [n("t")], [n("au")], bias=1.0 / 8192, f=F.Abs)
+        act(B("pen")[:], B("au")[:], 64, [n("au")], [n("pen")], scale=float(1 << 23), bias=-float(1 << 29), f=F.Relu)
+        gather("S", G[:, 16 * GV:1024], T.W1, B("off")[:, GV:64], 64 - GV, win1 + [n("off")], [n("Gb")])
+        mm([(pD[:, 0:64], T.I128[:], B("pen")[:], False, False)], 64, ["I128", n("pen")], bD)
+        if p == 2:
+            psO2 = pA[:, 256:320]
+            mm(turn(psO2, B("Bu"), T.Ib, True, False) + turn(psO2, B("Bv"), T.I128, False, False), 256,
+               [n("Bu"), n("Bv"), "Ib", "I128"], bA)
+        wd = 128 if p == 2 else 256
+        mm([(pD[:, c:wd:8], G[:, c::8], T.SEL2[:, 0:wd // 8], False, c == 7) for c in range(8)], 512,
+           [n("Ga"), n("Gb")] + sel2, bD)
+        ts(B("Xk")[:], pD[:, 0:64], 0.0, -1.0e9, A.is_gt, A.mult, 64, (), [n("Xk")], bD)
+        if p < 2:
+            s = 2 * p + h
+            tt(B("keep")[:], pD[:, 64:128], B("Xk")[:], A.is_le, 64, [n("Xk")], [n("keep")], bD)
+            P = B("Pp" if p == 0 else "Pq")
+            pa, pb = "Pa%d" % s, "Pb%d" % s
+            tt(P[:, :, 0, :], pD[:, 128:192], B("keep")[:], A.mult, 64, [n("keep")], [pa], bD)
+            tt(P[:, :, 1, :], pD[:, 192:256], B("keep")[:], A.mult, 64, [n("keep")], [pb], bD)
+            if CFG["FOLD"]:
+                srcs, alu, rd = [P[:, a, :, :] for a in range(8)], 1, [pa, pb]
+            else:
+                psR = pA[:, 192:208]
+                mm([(psR, T.Ib[:], P[:, a, :, :], a == 0, a == 7) for a in range(8)], 512, [pa, pb, "Ib"], bA)
+                srcs, alu, rd = [T.Rs[:, 16 * s:16 * s + 16]], 0, ["Rs%d" % s]
+                act(srcs[0], psR, 16, (), rd, bA)
+            c0 = 16 * (N * s + rank)
+
+            def send():
+                g.remote_dma_fused([RemoteDMATransfer(
+                    dst_ids=[DstId(rid=dst[q][0], pnc=dst[q][1]) for q in peers], dma_engine_mask=mask,
+                    remote_sem=T.sem["arr%d_%d" % (s, rank)], srcs=srcs, dsts=[T.LAND[:, c0:c0 + 16] for q in peers],
+                    alu_op=alu)], local_sem=T.sem.sent)
+            sent[0] += neng
+            k = op("G", send, ("r",), rd, (), sem="none")
+            arrived[(p, h)] = [op("-", None, ("c", j + 1), after=[k], sem="arr%d_%d" % (s, q), val=neng)
+                               for j, q in enumerate(senders)]
+            return
+        tt(B("Bd")[:, 1::2, :], pD[:, 64:128], B("Xk")[:], A.is_gt, 64, [n("Xk")], [n("Bd")], bD)
+        mm(turn(psO2, B("Bd"), T.Ibig, False, True), 128, [n("Bd"), "Ibig"], bA)
+        ts(B("offb")[:], psO2, 0.0, float(WC - 1), A.max, A.min, 64, (), [n("offb")], bA)
+        win2 = ["W2a", "W2b", "W2c", "W2d", n("offb"), n("Gz")]
+        s = 4 + h
+        arr = []
+        plan = [(peers[0], "V", pC, 256, bC), (peers[1], "S", pB, 64, bB), (peers[2], "V", pD, 384, bD), (rank, "S", pA, 320, bA)]
+        op("-", None, ("c", 0), (), [n("Ga"), n("Gb"), n("Gz")])
+        for j, (q, eng, pb, c0, bk) in enumerate(plan):
+            gather(eng, G[:, 256 * q:256 * q + 256], T.W2, B("offb")[:, 16 * q:16 * q + 16], 16, win2, [n("Gq%d" % q)])
+            mm([(pb[:, c0 + 16 * e:c0 + 16 * e + 16], G[:, 256 * q + 128 * e:256 * q + 128 * e + 128], T.GSEL[:], True, True)
+                for e in range(2)], 128, [n("Gq%d" % q), "GSEL"], bk)
+            y0 = 32 * (N * h + q)
+            cpy(T.Ys[:, y0:y0 + 32], pb[:, c0:c0 + 32], 32, (), [n("Ys%d_" % q)], bk)
+            if q != rank:
+                l0 = 32 * (N * h + rank)
+
+                def send1(q=q, y0=y0, l0=l0):
+                    g.remote_dma(T.LY[:, l0:l0 + 32], T.Ys[:, y0:y0 + 32], T.sem["arr%d_%d" % (s, rank)], T.sem.sent,
+                                 dst[q][1], dst[q][0], mask)
+                sent[0] += neng
+                k = op("G", send1, ("r",), [n("Ys%d_" % q)], (), sem="none")
+                arr.append(op("-", None, ("c", 1), after=[k], sem="arr%d_%d" % (s, senders[j]), val=neng))
+        psF = pA[0:32, 384:512]
+        y0 = 32 * (N * h + rank)
+        mm([(psF, T.Ys[:, y0:y0 + 32], T.I16[:], True, False)], 128, [n("Ys%d_" % rank), "I16"], bA)
+        for j, q in enumerate(senders):
+            mm([(psF, T.LY[:, 32 * (N * h + q):32 * (N * h + q) + 32], T.I16[:], False, j == 2)], 128, ["I16"], bA, [arr[j]])
+        cpy(B("Fo")[0:32, :], psF, 128, (), [n("Fo")], bA)
+        dma("Y", n("dYa"), [(T.y[:, 256 * h:256 * h + 128], B("Fo")[0:16, :])], 8, [n("Fo")], ())
+        dma("S", n("dYb"), [(T.y[:, 256 * h + 128:256 * h + 256], B("Fo")[16:32, :])], 8, [n("Fo")], ())
+
+    half_pass(0, 0)
+    half_pass(0, 1)
+    cur[0] = 0
+    dma("Y", "dWa", [(T.W2[16 * a:16 * a + 16, PAD:PAD + HW], T.cam[:]) for a in range(4)], 1024, win1, ["W2c"])
+    late_setup()
+    half_pass(1, 0)
+    half_pass(1, 1)
+    cur[0] = 0
+    dma("Y", "dWb", [(T.W2[16 * a:16 * a + 16, PAD:PAD + HW], T.cam[:]) for a in range(4, 8)], 1024, (), ["W2d"],
+        [arrived[(0, 1)][2]])
+    last_setup()
+    half_pass(2, 0)
+    half_pass(2, 1)
+    return ops, sent[0]
+
+
+PLANS = [
+    dict(hop=0.09, cyc=0.00104, gat=1.56, pe=0.0006, dl=2.0, dk=0.004, ri=0.5, rl=2.4, rr=0.7),
+    dict(hop=0.05, cyc=0.00085, gat=1.1, pe=0.00045, dl=1.5, dk=0.003, ri=0.3, rl=1.6, rr=0.4),
+    dict(hop=0.15, cyc=0.0012, gat=2.0, pe=0.001, dl=2.3, dk=0.005, ri=0.8, rl=3.0, rr=1.1),
+    dict(hop=0.15, cyc=0.0009, gat=1.2, pe=0.0008, dl=2.0, dk=0.004, ri=0.8, rl=3.0, rr=1.0),
+    dict(hop=0.06, cyc=0.0012, gat=2.0, pe=0.0005, dl=1.8, dk=0.004, ri=0.4, rl=1.8, rr=0.5),
+]
+
+
+def price(ops, q):
+    out = []
+    for o in ops:
+        c = o["cost"]
+        out.append({"v": lambda: (0.04 + max(c[1], 64) * q["cyc"], 0.0), "i": lambda: (0.06 + c[1] * q["gat"] * q["cyc"], 0.0),
+                    "p": lambda: (0.03 + c[1] * q["pe"], 0.0), "g": lambda: (0.17 + 2 * c[1] * q["cyc"], 0.0),
+                    "d": lambda: (0.1 * c[1], q["dl"] + c[2] * q["dk"]), "r": lambda: (q["ri"], 0.0),
+                    "c": lambda: (0.0, q["rl"] + c[1] * q["rr"] if c[1] else 0.0)}[c[0]]())
+    return out
+
+
+def replay(ops, order, cost, hop):
+    done, start, free = [0.0] * len(ops), [0.0] * len(ops), {}
+    for k in order:
+        e = ops[k]["eng"]
+        t = 0.0 if e == "-" else free.get(e, 0.0)
+        for d in ops[k]["deps"]:
+            t = max(t, done[d] + (0.0 if e == "-" or ops[d]["eng"] == e == "P" else hop))
+        start[k] = t
+        free[e] = t + cost[k][0]
+        done[k] = t + cost[k][0] + cost[k][1]
+    return max(done), start, done
+
+
+def lay_once(ops, kids, cost, hop, bias, look, noise):
+    n = len(ops)
+    tail = [0.0] * n
+    for k in range(n - 1, -1, -1):
+        tail[k] = cost[k][0] + cost[k][1] + max([hop + tail[c] for c in kids[k]] + [0.0])
+    tail = [tail[k] - bias * ops[k]["half"] + noise[k] for k in range(n)]
+    left = [len(o["deps"]) for o in ops]
+    ready = [k for k in range(n) if left[k] == 0]
+    done, free, order, at = [0.0] * n, {}, [], {k: 0.0 for k in ready}
+    while ready:
+        e = {k: at[k] if ops[k]["eng"] == "-" else max(at[k], free.get(ops[k]["eng"], 0.0)) for k in ready}
+        k0 = min(ready, key=lambda k: (e[k], -tail[k]))
+        near = [k for k in ready if ops[k]["eng"] == ops[k0]["eng"] and e[k] <= e[k0] + look * cost[k0][0]]
+        k = max(near, key=lambda j: tail[j])
+        ready.remove(k)
+        eng = ops[k]["eng"]
+        free[eng] = e[k] + cost[k][0]
+        done[k] = free[eng] + cost[k][1]
+        order.append(k)
+        for c in kids[k]:
+            left[c] -= 1
+            if left[c] == 0:
+                ec = ops[c]["eng"]
+                at[c] = max(done[d] + (0.0 if ec == "-" or ops[d]["eng"] == ec == "P" else hop) for d in ops[c]["deps"])
+                ready.append(c)
+    return order
+
+
+LAID = {}
+
+
+def lay_out(ops):
+    if "order" in LAID:
+        return LAID["order"]
+    n = len(ops)
+    kids = [[] for _ in range(n)]
+    for k, o in enumerate(ops):
+        for d in o["deps"]:
+            kids[d].append(k)
+    costs = [price(ops, q) for q in PLANS]
+    state = [CFG["SEED"]]
+
+    def rnd():
+        state[0] = (state[0] * 6364136223846793005 + 1442695040888963407) % (1 << 64)
+        return (state[0] >> 11) / float(1 << 53)
+    best = None
+    for it in range(CFG["TRIES"]):
+        if best is None or it < CFG["TRIES"] // 5:
+            amp = 0.6 * rnd()
+            par = (0 if rnd() < 0.5 else int(rnd() * len(PLANS)), 5.0 * rnd(), 1.2 * rnd(), [amp * rnd() for _k in range(n)])
+        else:
+            p0, share = best[3], 0.15 * rnd()
+            par = (p0[0], max(0.0, p0[1] + 0.3 * (rnd() - 0.5)), max(0.0, p0[2] + 0.1 * (rnd() - 0.5)),
+                   [x + 1.5 * (rnd() - 0.5) if rnd() < share else x for x in p0[3]])
+        order = lay_once(ops, kids, costs[par[0]], PLANS[par[0]]["hop"], par[1], par[2], par[3])
+        ends = [replay(ops, order, costs[j], q["hop"])[0] for j, q in enumerate(PLANS)]
+        score = sum(ends) + ends[0]
+        if best is None or score <= best[0]:
+            best = (score, order, ends, par)
+    LAID["order"], LAID["ends"] = best[1], best[2]
+    return best[1]
+
+
+def rank_program(g, core, T, topo):
+    if T.rank_of(core) is None:
+        return
+    ops, sent = build(g, core, T, topo)
+    order = lay_out(ops)
+    queue = {"V": g.vector, "S": g.scalar, "P": g.tensor, "G": g, "Y": g.sync}
+    count = {"sV": 0, "sS": 0, "sP": 0, "sG": 0}
+    token, waited, totals = {}, {}, {}
+
+    def needs(k, eng):
+        out = []
+        for d in ops[k]["deps"]:
+            od = ops[d]
+            if od["eng"] == "-" and od["sem"] is None:
+                out += needs(d, eng)
+            elif not (od["eng"] == eng == "P" or od["sem"] == "none"):
+                out.append(d)
+        return out
+    wanted = set()
+    for k in order:
+        if ops[k]["eng"] != "-":
+            wanted.update(needs(k, ops[k]["eng"]))
+    for k in order:
+        o = ops[k]
+        eng = o["eng"]
+        if eng == "-":
+            if o["sem"] is not None:
+                token[k] = (o["sem"], o["val"])
+                totals[o["sem"]] = o["val"]
+            continue
+        want = {}
+        for d in needs(k, eng):
+            s, v = token[d]
+            want[s] = max(want.get(s, 0), v)
+        for s in sorted(want):
+            if waited.get((eng, s), 0) < want[s]:
+                queue[eng].wait_ge(T.sem[s], want[s])
+                waited[(eng, s)] = want[s]
+        ins = o["fn"]()
+        if o["sem"] is None:
+            if k in wanted:
+                s = "s" + eng
+                count[s] += 1
+                ins.then_inc(T.sem[s], 1)
+                token[k] = (s, count[s])
+        elif o["sem"] != "none":
+            token[k] = (o["sem"], o["val"])
+            totals[o["sem"]] = o["val"]
+    totals.update(count)
+    totals["sent"] = sent
+    seen = {}
+    for (e, s), v in waited.items():
+        seen[s] = max(seen.get(s, 0), v)
+    for s in totals:
+        if totals[s] > seen.get(s, 0):
+            g.wait_ge(T.sem[s], totals[s])

@@ -7,53 +7,55 @@ PAD = 128
 WC = HW + 2 * PAD
 NP = 16
 PIECE = WC // NP
-BIG = float(1 << 22)
-CFG = dict(GV=30, ZS=4, ZG=2, FOLD=False, TRIES=2500, SEED=1)
+KR = 112
+MAGIC = 1.5 * (1 << 23)
+COL0 = MAGIC + 128 * 160 - 64 - PAD
+MAGIC8 = 8 * MAGIC
+ORDER = [
+    "O z0 z1 R x0 x1 K l0 k0 k1 t0 l1 m0 n0 i0 t1 S Q W n1 u0 r0 s0 i1 m1 w0 u1 r1 s1 w1",
+    "a0 b0 c0 d0 a1 z0 k0 l0 x0 b1 c1 t0 n0 d1 m0 i0 z1 k1 u0 l1 r0 s0 x1 t1 w0 n1 m1 i1 u1 r1 s1 w1",
+    "a0 b0 c0 d0 a1 z0 k0 k1 l0 b1 x0 t0 c1 n0 d1 m0 i0 z1 u0 r0 l1 s0 x1 t1 f0 m1 n1 i1 g0 F0 u1 r1 s1 f1 G0 F1 g1 G1 e0 E0 e1 E1",
+]
+CFG = dict(GL=((34, 24), (32, 34), (32, 24)), GI=((28, 44), (24, 32), (28, 34)), ZS=5, ZG=2, W2=(3, 3, 2))
 b16, f32, f16, i32, u16 = "bfloat16", "float32", "float16", "int32", "uint16"
 
 SCRATCH = {}
 for _d, _w, _names in (
     (b16, WC, "W1 W2"), (b16, HW, "C3"), (i32, 512, "L"), (b16, 512, "Lhi Llo Lv"), (i32, 8, "Pi"),
-    (f32, 8, "Pf S4 S32 S8 hc c1 c2 stmp"), (f32, 128, "ones I32 GO Qr GOq KX KY Ta Tb Tc Td NB A8 mk M0 M1"),
-    (b16, 128, "Ib I128 Ibig WZ0 WZ1 WD"), (f16, 128, "I16"), (f32, 64, "NB2 MT wtmp"), (f32, 24, "LAB"),
-    (i32, 128, "mi mj"), (i32, 16, "gi gj"), (b16, 16, "GSEL SEL1"), (b16, 32, "SEL2"), (b16, 64, "WX Rs"),
-    (b16, 256, "ZR LAND"), (f16, 256, "LY Ys"),
-    (f32, 128, "RZ0 RZ1 RX0 RX1 RDa0 RDa1 RDb0 RDb1 D00 D01 Fo0 Fo1"), (b16, 128, "SP0 SP1"),
-    (f32, 64, "X00 X01 t0 t1 au0 au1 Xk0 Xk1 keep0 keep1"), (u16, 64, "zoff0 zoff1 off0 off1 offb0 offb1"),
-    (i32, 64, "xi0 xi1"), (b16, 64, "pen0 pen1"), (b16, 1024, "G0 G1"),
+    (f32, 8, "Pf hc stmp hcol"), (b16, 128, "ones mask GO GO2 Ib Pr Pm Ineg WK WN WX WT"), (f32, 128, "I17"),
+    (b16, 16, "GSEL GSEL4 GSEL2"), (b16, 192, "D3"), (f16, 256, "LY Ys"), (b16, 320, "D5 P50 P51"),
+    (f32, 96, "Fo0 Fo1"), (f32, 136, "OF0 OF1"), (u16, 64, "zoff0 zoff1 off0 off1 offb0 offb1"), (b16, 1024, "G0 G1 H0 H1"),
+    (b16, 64, "SQ0 SQ1"), (f32, 192, "DX0 DX1 O10 O11 O30 O31"),
 ):
     for _n in _names.split():
         SCRATCH[_n] = ("sbuf", [128, _w], _d)
+for _n, _s in (("LAB", [16, 16]), ("SEL1", [8, 3]), ("SEL2", [8, 5]), ("SEL3", [8, 3]), ("PAT", [64, 5]), ("PC", [64, 3]),
+               ("RZ", [4, 136]), ("WZ", [17, 16]), ("SP0", [17, 8]), ("SP1", [17, 8]), ("Rs", [4, 48]), ("LAND", [4, 80])):
+    SCRATCH[_n] = ("sbuf", [128] + _s, b16)
 for _h in "01":
-    for _n in ("Bu", "Bv", "Bd"):
-        SCRATCH[_n + _h] = ("sbuf", [128, 17, 8], b16)
-    for _n in ("Pp", "Pq"):
-        SCRATCH[_n + _h] = ("sbuf", [128, 8, 2, 8], b16)
-    for _n in "ABCD":
-        SCRATCH["ps" + _n + _h] = ("psum", [128, 512], f32)
+    SCRATCH["psA" + _h] = ("psum", [128, 512], f32)
+    SCRATCH["psB" + _h] = ("psum", [128, 64, 8], f32)
+    SCRATCH["psC" + _h] = ("psum", [128, 512], f32)
+    SCRATCH["psD" + _h] = ("psum", [128, 512], f32)
 
-DMAS = ["dL", "dP", "dC3", "dC", "dHi", "dLo", "dV", "dWa", "dWb", "dYa0", "dYb0", "dYa1", "dYb1"]
+DMAS = ["dL", "dP", "dC3", "dC", "dHi", "dLo", "dV", "dW0", "dW1", "dW2", "dY0", "dY1"]
 SEMAPHORES = ["sV", "sS", "sP", "sG", "sent"] + ["arr%d_%d" % (k, r) for k in range(6) for r in range(N)] + DMAS
 
 
 def build(g, core, T, topo):
     rank = T.rank_of(core)
-    ops, res, banks, cur = [], {}, {}, [0]
+    ops, res, banks = [], {}, {}
     V, S, PE = g.vector, g.scalar, g.tensor
-    GV = CFG["GV"]
 
     def op(eng, fn, cost, r=(), w=(), b=None, after=(), sem=None, val=0):
         k = len(ops)
         deps = set(after)
         for x in r:
-            st = res.setdefault(x, [None, []])
-            if st[0] is not None:
-                deps.add(st[0])
+            deps.add(res[x][0])
         for x in w:
-            st = res.setdefault(x, [None, []])
-            if st[0] is not None:
-                deps.add(st[0])
-            deps.update(st[1])
+            if x in res:
+                deps.add(res[x][0])
+                deps.update(res[x][1])
         for x in r:
             res[x][1].append(k)
         for x in w:
@@ -62,32 +64,34 @@ def build(g, core, T, topo):
             st = banks.setdefault(b, [None, [], []])
             if st[0] == eng:
                 deps.update(st[2])
-                if eng == "P":
-                    deps.add(st[1][-1])
                 st[1].append(k)
             else:
                 deps.update(st[1])
                 banks[b] = [eng, [k], st[1]]
         deps.discard(k)
-        ops.append(dict(eng=eng, fn=fn, cost=cost, deps=deps, sem=sem, val=val, half=cur[0], tag=(list(w) + [b])[0]))
+        ops.append(dict(eng=eng, fn=fn, cost=cost, deps=deps, sem=sem, val=val, tag=(list(w) + [b])[0]))
         return k
 
     def ts(out, in0, s1, s2, o0, o1, n, r, w, b=None):
-        if o1 is None:
-            return op("V", lambda: V.tensor_scalar(out, in0, s1, None, o0), ("v", n), r, w, b)
         return op("V", lambda: V.tensor_scalar(out, in0, s1, s2, o0, o1), ("v", n), r, w, b)
 
-    def tt(out, a, c, o, n, r, w, b=None):
-        return op("V", lambda: V.tensor_tensor(out, a, c, o), ("v", n), r, w, b)
+    def tt(out, a, c, o, n, r, w, b=None, after=()):
+        return op("V", lambda: V.tensor_tensor(out, a, c, o), ("v", n), r, w, b, after)
 
     def cpy(out, a, n, r, w, b=None):
         return op("V", lambda: V.tensor_copy(out, a), ("v", n), r, w, b)
 
-    def fill(ap, c, n, w):
-        return op("V", lambda: V.memset(ap, c), ("v", n), (), w)
+    def fill(ap, c, n, w, r=()):
+        return op("V", lambda: V.memset(ap, c), ("v", n), r, w)
+
+    def scan(out, d0, d1, o0, o1, n, r, w, b):
+        return op("V", lambda: V.tensor_tensor_scan(out, d0, d1, 0.0, o0, o1), ("v", n), r, w, b)
 
     def act(out, a, n, r, w, b=None, bias=0.0, scale=1.0, f=F.Identity):
         return op("S", lambda: S.activation(out, a, f, bias=bias, scale=scale), ("v", n), r, w, b)
+
+    def sfill(out, c, n, w, r=(), p1=128):
+        return act(out, T.W1[0:p1, 0:n], n, ["Wz0"] + list(r), w, bias=c)
 
     def mm(lst, cyc, r, b, after=()):
         def fn():
@@ -97,13 +101,11 @@ def build(g, core, T, topo):
             return last
         return op("P", fn, ("p", cyc), r, (), b, after)
 
-    def iota(out, pat, base, cm, n, w, flt=True):
-        if flt:
-            return op("G", lambda: g.iota(out, pat, base, cm, allow_small_or_imprecise_dtypes=True), ("g", n), (), w)
-        return op("G", lambda: g.iota(out, pat, base, cm), ("g", n), (), w)
+    def iota(out, pat, base, cm, n, w, r=()):
+        return op("G", lambda: g.iota(out, pat, base, cm, allow_small_or_imprecise_dtypes=True), ("g", n), r, w)
 
-    def asel(out, a, pat, cm, n, r, w):
-        return op("G", lambda: g.affine_select(out, a, pat, A.is_equal, 0.0, 0, cm), ("g", n), r, w)
+    def mark(out, a, pat, c, base, n, w):
+        return op("G", lambda: g.affine_select(out, a, pat, A.not_equal, c, base, 1), ("g", n), ["Wz0"], w)
 
     def dma(q, sem, pairs, kb, r, w, after=()):
         e = g.sync if q == "Y" else S
@@ -124,391 +126,337 @@ def build(g, core, T, topo):
     mask = -1
     for p in peers:
         rid, pid, _se = topo.addr(T.cores[p])
-        dst[p] = (rid, pid)
+        dst[p] = DstId(rid=rid, pnc=pid)
         mask &= topo.mask(core, T.cores[p])
-    neng = bin(mask).count("1")
+    engs = [e for e in topo.engines(core, T.cores[peers[0]]) if mask >> e & 1]
+    neng = len(engs)
+    halves = [sum(1 << e for e in engs[:neng // 2]), sum(1 << e for e in engs[neng // 2:])]
     sent = [0]
-    r8 = lambda t, a=0, b=128: t[0:8, a:b]
-    r16 = lambda t, a=0, b=128: t[0:16, a:b]
+
+    def send(transfers, r):
+        def fn():
+            g.remote_dma_fused([RemoteDMATransfer(dst_ids=[dst[q] for q in to], dma_engine_mask=m, remote_sem=T.sem[sem], srcs=[src],
+                                                  dsts=land, alu_op=0) for to, m, sem, src, land in transfers],
+                               local_sem=T.sem.sent)
+        sent[0] += neng
+        return op("G", fn, ("r",), r, (), sem="none")
 
     dma("Y", "dL", [(T.L[:], T.lens[:])], 256, (), ["L"])
-    dma("S", "dP", [(r8(T.Pi, 0, 6), T.pose[:])], 0, (), ["Pi"])
+    dma("S", "dP", [(T.Pi[0:8, 0:6], T.pose[:])], 0, (), ["Pi"])
     dma("Y", "dC3", [(T.C3[0:2, :], T.cam[0:2, :]), (T.C3[2:3, :], T.cam[15:16, :])], 48, (), ["C3"])
 
     zn = ["Wz%d" % k for k in range(NP)]
-    fill(T.W1[:, 0:PIECE], 0.0, PIECE // 2, [zn[0]])
-    iota(T.ones[:], [[0, 128]], 1, 0, 128, ["ones"])
-    asel(r8(T.GO), r8(T.ones), [[1, 8], [0, 16]], -1, 128, ["ones"], ["GO"])
-    for k in range(1, NP):
-        piece = T.W1[:, k * PIECE:(k + 1) * PIECE]
-        if k <= CFG["ZS"]:
-            act(piece, T.W1[:, 0:PIECE], PIECE, [zn[0]], [zn[k]])
-        elif k <= CFG["ZS"] + CFG["ZG"]:
-            iota(piece, [[0, PIECE]], 0, 0, PIECE, [zn[k]])
+    piece = lambda k: T.W1[:, k * PIECE:(k + 1) * PIECE]
+    ZS, ZG = CFG["ZS"], CFG["ZG"]
+    fill(piece(0), 0.0, PIECE // 2, [zn[0]])
+    fill(T.ones[:], 1.0, 64, ["ones"])
+    fill(T.mask[:], 0.0, 64, ["mask"])
+    fill(T.LAB[0:8], 0.0, 128, ["LAB"])
+    fill(T.mask[0:8, :], 1.0, 64, ["mask"])
+    for k in range(1, 1 + ZS):
+        act(piece(k), piece(0), PIECE, [zn[0]], [zn[k]])
+    for k in range(1 + ZS, 1 + ZS + ZG):
+        iota(piece(k), [[0, PIECE]], 0, 0, PIECE, [zn[k]])
+    for k in range(1 + ZS + ZG, NP - 3):
+        fill(piece(k), 0.0, PIECE // 2, [zn[k]])
+    zero = T.W1[:, 0:128]
+    mark(T.GO[0:8, :], zero[0:8], [[-1, 8], [0, 16]], 1.0, 0, 128, ["GO"])
+    mark(T.mask[:], T.mask[:], [[-2, 8], [0, 8], [-1, 2]], 1.0, -64, 128, ["mask"])
+    mark(T.GO2[0:8, :], zero[0:8], [[0, 8], [-1, 8], [0, 2]], 0.25, 0, 128, ["GO2"])
+    mark(T.mask[:], T.mask[:], [[-2, 8], [0, 8], [-1, 2]], 1.0, -96, 128, ["mask"])
+    mark(T.hcol[0:8, 0:1], T.W1[0:8, 0:1], [[0, 1]], 32.0, 0, 1, ["hcol"])
+    for rows, pt in ((5, [[8, 4], [0, 32]]), (4, [[0, 64], [8, 2]]), (3, [[0, 4], [256, 2], [0, 16]])):
+        iota(T.mask[0:rows, :], pt, 0, 0, 128, ["mask"])
+
+    LAB = T.LAB
+
+    def pieces(k, blk, col, r):
+        two = T.Pi[0:8, 2 + 2 * k:4 + 2 * k]
+        cpy(LAB[0:8, blk::8, col], two, 2, ["Pi"] + r, ["LABhi%d" % k])
+        if k:
+            fill(piece(NP - 3), 0.0, PIECE // 2, [zn[NP - 3]])
         else:
-            fill(piece, 0.0, PIECE // 2, [zn[k]])
+            fill(T.SP0[:], 0.0, 68, ["SP0z"])
+        tt(LAB[0:8, blk::8, col + 1], two, LAB[0:8, blk::8, col], A.subtract, 4, ["Pi", "LABhi%d" % k], ["LABlo%d" % k])
+    pieces(1, 7, 1, ["LAB"])
+    cpy(T.Pf[0:8, 0:2], T.Pi[0:8, 0:2], 2, ["Pi"], ["Pf"])
+    for k in range(NP - 2, NP):
+        fill(piece(k), 0.0, PIECE // 2, [zn[k]])
+    mm([(T.psB1[:, 0, 0:2], T.GO[0:8, :], LAB[0:8, 7, 1:3], True, False),
+        (T.psB1[:, 0, 0:2], T.GO[0:8, :], LAB[0:8, 7, 2:4], False, True)], 128, ["GO", "LABhi1", "LABlo1"], "B1")
+    act(T.hc[:, 0:2], T.psB1[:, 0, 0:2], 2, (), ["hc"], "B1", scale=1.0 / 4096)
+    act(T.Pf[0:8, 2:3], T.Pf[0:8, 1:2], 1, ["Pf"], ["Pfn"], scale=-1.0)
+    lab = ["LABhi0", "LABlo0", "LABhi1", "LABlo1"]
+    for blk, col, c in ((15, 0, 1.0 / 2048), (15, 3, 0.5)):
+        lab.append("LABc%d_%d" % (blk, col))
+        sfill(LAB[0:8, blk, col:col + 1], c, 1, lab[-1:], ["LAB"], 8)
 
-    iota(r8(T.KX), [[0, 16], [64, 8]], 0, 0, 128, ["KX"])
-    iota(r8(T.KY), [[64, 4], [8, 4], [0, 8]], 0, 0, 128, ["KY"])
-    iota(r8(T.Qr), [[0, 8], [1, 16]], 0, 0, 128, ["Qr"])
-    asel(r8(T.GOq), r8(T.Qr), [[1, 8], [0, 16]], -1, 128, ["Qr"], ["GOq"])
-    asel(T.I32[:], T.ones[:], [[-1, 128]], 1, 128, ["ones"], ["I32"])
-    GT, GTc = T.GO[0:8, ::2], T.GOq[0:8, ::2]
-
-    Pf = r8(T.Pf, 0, 6)
-    cpy(Pf, r8(T.Pi, 0, 6), 6, ["Pi"], ["Pf"])
-    mm([(T.psB1[:, 128:134], r8(T.GO), Pf, True, True)], 256, ["GO", "Pf"], "B1")
-    act(T.hc[:, 0:6], T.psB1[:, 128:134], 6, (), ["hc"], "B1", scale=1.0 / 4096)
-
+    dma("Y", "dC", [(T.W1[16 * a:16 * a + 3, PAD:PAD + HW], T.C3[0:3, :]) for a in range(8)], 384, zn + ["C3"], ["Wc"])
     cpy(T.psA1[:], T.L[:], 512, ["L"], (), "A1")
-    act(T.Lv[:], T.psA1[:], 512, ["hc"], ["Lv"], "A1", scale=T.hc[:, 4:5], bias=191.5 + 1.0 / 8192)
+    act(T.Lv[:], T.psA1[:], 512, ["hc"], ["Lv"], "A1", scale=T.hc[:, 0:1], bias=191.5 + 1.0 / 8192)
     cpy(T.Lhi[:], T.L[:], 512, ["L"], ["Lhi"])
     tt(T.Llo[:], T.psA1[:], T.Lhi[:], A.subtract, 512, ["Lhi"], ["Llo"], "A1")
     dma("Y", "dHi", [(T.W1[3::16, PAD:PAD + HW], T.Lhi[:])], 128, zn + ["Lhi"], ["Whi"])
     dma("S", "dV", [(T.W1[5::16, PAD:PAD + HW], T.Lv[:])], 128, zn + ["Lv"], ["Wv"])
     dma("Y", "dLo", [(T.W1[4::16, PAD:PAD + HW], T.Llo[:])], 128, zn + ["Llo"], ["Wlo"])
-    dma("Y", "dC", [(T.W1[16 * a:16 * a + 3, PAD:PAD + HW], T.C3[0:3, :]) for a in range(8)], 384, zn + ["C3"], ["Wc"])
     win1 = zn + ["Whi", "Wlo", "Wv", "Wc"]
 
-    act(r8(T.S4, 0, 6), Pf, 6, ["Pf"], ["S4"], scale=0.25)
-    act(r8(T.S32, 0, 6), Pf, 6, ["Pf"], ["S32"], scale=1.0 / 32)
-    act(r8(T.S8, 0, 6), Pf, 6, ["Pf"], ["S8"], scale=8.0)
-    act(r8(T.Ta), r8(T.KY), 128, ["KY", "S4"], ["Ta"], scale=r8(T.S4, 0, 1), bias=r8(T.S4, 3, 4))
-    ts(r8(T.Tb), r8(T.KX), r8(T.S4, 1, 2), -(PAD - 0.375), A.mult, A.add, 128, ["KX", "S4"], ["Tb"])
-    tt(r8(T.RZ0), r8(T.Ta), r8(T.Tb), A.subtract, 256, ["Ta", "Tb"], ["RZ0"])
-    act(r8(T.RZ1), r8(T.RZ0), 128, ["RZ0", "S8"], ["RZ1"], bias=r8(T.S8, 0, 1))
-    ts(r8(T.NB2, 0, 64), r8(T.ones, 0, 64), r8(T.Pf, 1, 2), -2.0, A.mult, A.mult, 64, ["ones", "Pf"], ["NB2"])
-    act(r8(T.Tc), r8(T.KX), 128, ["KX", "S32"], ["Tc"], scale=r8(T.S32, 0, 1), bias=r8(T.S32, 2, 3))
-    ts(r8(T.Td), r8(T.KY), r8(T.S32, 1, 2), -31.0 / 64, A.mult, A.add, 128, ["KY", "S32"], ["Td"])
-    tt(r8(T.RX0), r8(T.Tc), r8(T.Td), A.add, 256, ["Tc", "Td"], ["RX0"])
-    act(r8(T.RX1), r8(T.RX0), 128, ["RX0", "Pf"], ["RX1"], bias=r8(T.Pf, 1, 2))
-    ts(r8(T.NB), r8(T.ones), r8(T.Pf, 1, 2), -1.0, A.mult, A.mult, 128, ["ones", "Pf"], ["NB"])
-    ts(r8(T.A8), r8(T.ones), r8(T.Pf, 0, 1), 0.125, A.mult, A.mult, 128, ["ones", "Pf"], ["A8"])
-    act(r8(T.c1, 0, 6), Pf, 6, ["Pf"], ["c1"], scale=-1.0, bias=-(PAD + 0.5))
-    act(r8(T.c2, 0, 6), Pf, 6, ["Pf"], ["c2"], bias=-(PAD - 0.5))
+    for b0, cx, cy, c in ((8, 2, 0, -1.5), (0, 0, 1, -15.5)):
+        for nm, out, n, k, r in (("x", LAB[0:8, b0:b0 + 5:4, :], 32, cx, "LAB"), ("y", LAB[0:8, b0 + 6, :], 16, cy, "LAB"),
+                                 ("u", LAB[0:8, b0, 0:5:4], 2, cy, "LABx%d" % b0)):
+            lab.append("LAB%s%d" % (nm, b0))
+            act(out, T.ones[0:8, 0:n], n, ["Pf", "Pfn", "ones", r], lab[-1:], scale=T.Pf[0:8, k:k + 1])
+        lab.append("LABk%d" % b0)
+        sfill(LAB[0:8, b0, 5:6], c, 1, lab[-1:], ["LABx%d" % b0], 8)
+    fill(T.SP1[:], 0.0, 68, ["SP1z"])
+    fill(T.WZ[:], 0.0, 136, ["WZ"])
+    fill(T.PC[0:2], 0.0, 96, ["PCz"])
+    pieces(0, 0, 6, ["LABx0", "LABx8"])
+    ps = T.psB0
+    mm([(ps[0:KR, 0:16, :], LAB[0:8, 8:15, :], T.GO2[0:8, :], True, True),
+        (ps[0:KR, 16:32, :], LAB[0:8, 0:7, :], T.GO2[0:8, :], True, True),
+        (ps[0:4, 32:48, :], LAB[0:8, 15, 0:4], T.GO2[0:8, :], True, True)], 384, lab + ["GO2"], "B0")
 
-    cpy(T.Ib[:], T.I32[:], 128, ["I32"], ["Ib"])
-    act(T.I128[:], T.I32[:], 128, ["I32"], ["I128"], scale=128.0)
-    tt(T.stmp[:], T.I32[:, 3::16], T.I32[:, 4::16], A.add, 16, ["I32"], ["stmp"])
-    ts(T.SEL1[:, 0:8], T.stmp[:], 1.0 / 4096, None, A.mult, None, 8, ["stmp"], ["SEL1a"])
-    act(T.SEL1[:, 8:16], T.I32[:, 5::16], 8, ["I32"], ["SEL1b"])
-    act(T.SEL2[:, 0:8], T.I32[:, 2::16], 8, ["I32"], ["SEL2a"], scale=-32.0)
-    act(T.SEL2[:, 8:16], T.I32[:, 2::16], 8, ["I32"], ["SEL2b"], scale=32.0)
-    act(T.SEL2[:, 16:24], T.I32[:, 0::16], 8, ["I32"], ["SEL2c"])
-    act(T.SEL2[:, 24:32], T.I32[:, 1::16], 8, ["I32"], ["SEL2d"])
-    sel2 = ["SEL2a", "SEL2b", "SEL2c", "SEL2d"]
-    fill(r16(T.ZR, 0, 256), 0.0, 128, ["ZR"])
-    for nm in ("Bu0", "Bv0", "Bu1", "Bv1"):
-        fill(T[nm][:], 0.0, 68, [nm])
+    def places(nm, val, gx, gy):
+        act(val(T[nm + "0"][0:8]), T.ones[0:8, 0:64], 64, [nm + "0z", "ones"], [nm + "0c"])
+        iota(val(T[nm + "0"][0:2]), gx, 0, 0, 64, [nm + "0c"])
+        iota(val(T[nm + "0"][0:1]), gy, 0, 0, 64, [nm + "0c"])
+        return lambda: act(val(T[nm + "1"][0:8]), val(T[nm + "0"][0:8]), 64, [nm + "0c", nm + "1z", "hcol"], [nm + "1c"],
+                           bias=T.hcol[0:8, 0:1])
+    sp1 = places("SP", lambda t: t[:, 1::2, :], [[16, 8], [0, 4], [128, 2]], [[0, 8], [64, 4], [0, 2]])
+    mark(T.Ib[:], zero, [[-1, 128]], 1.0, 0, 128, ["Ib"])
+    fill(T.PC[0:2, :, 1], 1.0 / 8192, 32, ["PC1"], ["PCz"])
+    fill(T.SQ0[:], 0.0, 32, ["SQ0z"])
+    fill(T.PC[0:1, :, 1], -0.5, 32, ["PC1"])
+    act(T.mask[0:2, :], T.ones[0:2, :], 128, ["ones"], ["mask"])
+    fill(T.PAT[0:4], 0.0, 160, ["PATz"])
+    fill(T.SQ1[:], 0.0, 32, ["SQ1z"])
+    fill(T.PAT[0:4, :, 0:2], 4.0, 64, ["PAT0"], ["PATz"])
+    for h in (0, 1):
+        sfill(T["DX%d" % h][:, 0::3], 0.0, 64, ["DXa%d" % h])
+        sfill(T["DX%d" % h][:, 2::3], 1.0, 64, ["DXb%d" % h])
+    sq1 = places("SQ", lambda t: t[:], [[0, 4], [128, 2], [16, 8]], [[64, 4], [0, 16]])
+    tt(T.WK[0:KR, :], ps[0:KR, 0:16, :], T.mask[0:KR, :], A.mult, 128, ["mask"], ["WK"], "B0")
+    tt(T.WX[0:KR, :], ps[0:KR, 16:32, :], T.mask[0:KR, :], A.mult, 128, ["mask"], ["WX"], "B0")
+    wz = ["WZ%d" % c for c in range(8)]
+    for c in range(8):
+        (cpy if c % 2 else act)(T.WZ[0:KR, 1::2, 2 * c:2 * c + 2], T.WK[0:KR, 16 * c:16 * c + 16], 16, ["WK", "WZ"], [wz[c]])
+    sp1()
+    cpy(T.WT[0:4, :], ps[0:4, 32:48, :], 128, (), ["WT"], "B0")
+    mark(T.Ineg[:], zero, [[-8, 2], [-1, 8], [-16, 8]], -32768.0, 0, 128, ["Ineg"])
+    mark(T.Pr[:], zero, [[-64, 2], [-1, 8], [-8, 8]], 1.0, 0, 128, ["Pr"])
+    mark(T.Pm[:], zero, [[-1, 16], [-16, 8]], 1.0, 0, 128, ["Pm"])
+    tt(T.stmp[:], T.Ib[:, 3::16], T.Ib[:, 4::16], A.add, 16, ["Ib"], ["stmp"])
+    sfill(T.PC[0:1, :, 2], MAGIC, 64, ["PC2"], ["PCz"], 1)
+    sfill(T.SEL1[:, :, 1], 0.0, 8, ["SEL11"])
+    act(T.SEL1[:, :, 2], T.Ib[:, 5::16], 8, ["Ib"], ["SEL12"], scale=128.0)
+    act(T.SEL1[:, :, 0], T.stmp[:], 8, ["stmp"], ["SEL10"], scale=1.0 / 32768)
+    pat = ["PAT0", "PAT2", "PAT3", "PAT4"]
+    sel2 = ["SEL2%d" % k for k in range(5)]
 
-    def late_setup():
-        iota(r16(T.mi), [[0, 8], [-1, 16]], 16, 1, 128, ["mi"], False)
-        ts(r16(T.mj), r16(T.mi), 7, None, A.bitwise_and, None, 128, ["mi"], ["mj"])
-        ts(r16(T.M0), r16(T.mj), 0.0, 0.25, A.is_equal, A.mult, 128, ["mj"], ["M0"])
-        act(r16(T.MT, 0, 64), r16(T.M0, 0, 64), 64, ["M0"], ["MT"])
-        iota(r16(T.mk), [[0, 8], [1, 2], [0, 8]], 0, 0, 128, ["mk"])
-        tt(r16(T.M1), r16(T.M0), r16(T.mk), A.mult, 256, ["M0", "mk"], ["M1"])
-        tt(r16(T.M0), r16(T.M0), r16(T.M1), A.subtract, 256, ["M1"], ["M0"])
-        act(r8(T.LAB, 0, 8), r8(T.NB, 0, 8), 8, ["NB"], ["LABa"])
-        act(r8(T.LAB, 8, 16), r8(T.A8, 0, 8), 8, ["A8"], ["LABb"], scale=8.0)
-        act(r8(T.LAB, 16, 24), r8(T.NB, 0, 8), 8, ["NB"], ["LABc"], scale=-1.0)
-        ps, MT = T.psB0, r16(T.MT, 0, 64)
-        mm([(r16(ps, 128, 256), r8(T.LAB, 0, 16), r8(T.GO), True, True),
-            (r16(ps, 256, 320), r8(T.LAB, 8, 24), GT, True, True)], 768, ["LABa", "LABb", "LABc", "GO"], "B0")
-        tt(r16(T.WZ0), r16(ps, 128, 256), r16(T.M0), A.mult, 128, ["M0"], ["WZ0"], "B0")
-        tt(r16(T.WZ1), r16(ps, 128, 256), r16(T.M1), A.mult, 128, ["M1"], ["WZ1"], "B0")
-        tt(r16(T.WD, 0, 64), ps[0:16, 128:256:2], MT, A.mult, 64, ["MT"], ["WDa"], "B0")
-        tt(r16(T.wtmp, 0, 64), r16(ps, 256, 320), MT, A.mult, 64, ["MT"], ["wtmp"], "B0")
-        act(r16(T.WX, 0, 64), r16(T.wtmp, 0, 64), 64, ["wtmp"], ["WX"], scale=0.125)
-        act(r16(T.WD, 64, 128), r16(T.WD, 0, 64), 64, ["WDa"], ["WDb"], scale=-1.0)
+    def for_offsets():
+        fill(T.RZ[:], 0.0, 272, ["RZ"])
+
+    def for_sides():
+        for k, c in ((2, 512.0), (3, 256.0), (4, 128.0)):
+            sfill(T.PAT[0:1, :, k], c, 64, ["PAT%d" % k], ["PATz"], 1)
+        act(T.WN[0:KR, :], T.WK[0:KR, :], 128, ["WK"], ["WN"], scale=-1.0)
+
+    def for_turn2():
+        for k, (row, c) in enumerate(((2, 32.0), (2, -32.0), (0, 1.0 / 2048), (1, 1.0 / 2048), (0, 0.0))):
+            act(T.SEL2[:, :, k], T.Ib[:, row::16], 8, ["Ib"], ["SEL2%d" % k], scale=c)
+
+    def for_test():
+        fill(T.D5[:], 0.0, 160, ["D5z"])
+        fill(T.Rs[:], 0.0, 96, ["Rs"])
+        fill(T.D5[:, 0::5], 1.0, 32, ["D5"], ["D5z"])
+
+    def for_write():
+        mm([(T.psA0[:, 0:16], T.mask[64:80, :], T.Ib[64:80, 64:80], True, True)], 64, ["mask", "Ib"], "A0")
+        act(T.GSEL[:], T.psA0[:, 0:16], 16, (), ["GSEL"], "A0")
+        act(T.GSEL4[:], T.psA0[:, 0:16], 16, (), ["GSEL4"], "A0", scale=-4.0)
+        act(T.GSEL2[:], T.psA0[:, 0:16], 16, (), ["GSEL2"], "A0", scale=-2.0)
+    once = dict(O=for_offsets, K=for_sides, Q=sq1, R=for_turn2, S=for_test, W=for_write)
 
     def last_setup():
+        fill(T.LAND[:, :, 48:80], 0.0, 64, ["LANDz"])
         fill(T.W2[:, 0:PAD], 0.0, 64, ["W2a"])
         fill(T.W2[:, PAD + HW:WC], 0.0, 64, ["W2b"])
-        act(T.Ibig[:], T.I32[:], 128, ["I32"], ["Ibig"], scale=BIG)
-        cpy(T.I16[:], T.I32[:], 128, ["I32"], ["I16"])
-        iota(T.gi[:], [[-1, 16]], 16, 1, 16, ["gi"], False)
-        ts(T.gj[:], T.gi[:], 15, None, A.bitwise_and, None, 16, ["gi"], ["gj"])
-        ts(T.GSEL[:], T.gj[:], 0.0, None, A.is_equal, None, 16, ["gj"], ["GSEL"])
-        for nm in ("Bd0", "Bd1"):
-            fill(T[nm][:], 0.0, 68, [nm])
+        fill(T.D3[:], 0.0, 96, ["D3z"])
+        act(T.I17[:], T.Ineg[:], 128, ["Ineg"], ["I17"], scale=-1.0 / (1 << 32))
+        act(T.SEL3[:, :, 0:2], T.SEL2[:, :, 0:2], 16, sel2, ["SEL3a"])
+        sfill(T.SEL3[:, :, 2], 0.0, 8, ["SEL3b"])
+        fill(T.D3[:, 0::3], 1.0, 32, ["D3"], ["D3z"])
+        for h in (0, 1):
+            sfill(T["OF%d" % h][:, 0:130:2], 0.0, 65, ["OFz%d" % h])
 
     arrived = {}
     senders = peers[::-1]
 
     def half_pass(p, h):
-        cur[0] = h
         n = lambda s: "%s%d" % (s, h)
         B = lambda s: T[n(s)]
         pA, pB, pC, pD = B("psA"), B("psB"), B("psC"), B("psD")
         bA, bB, bC, bD = n("A"), n("B"), n("C"), n("D")
-        G = B("G")
-        psZ, psX = pB[:, 0:64], pC[:, 0:64]
-        mm([(psZ, r8(T.GO), B("RZ")[0:8, ::2], True, False),
-            (psZ, r8(T.GOq), r8(T.NB2, 0, 64), False, p == 0)], 512, ["GO", "GOq", n("RZ"), "NB2"], bB)
+        G, SP, SQ, O1, P5, H, OF, Fo = B("G"), B("SP"), B("SQ"), B("O1"), B("P5"), B("H"), B("OF"), B("Fo")
+        sp = [n("SP") + x for x in ("zcs" if p else "zc")]
+        sq = [n("SQ") + x for x in ("zcs" if p else "zc")]
+        GL, GI = CFG["GL"][p][h], CFG["GI"][p][h]
+        ns = 3 if p == 2 else 5
+        slot = lambda k: pD[:, k:64 * ns:ns]
+        R1, R2 = T.RZ[:, 2 * h, :], T.RZ[:, 2 * h + 1, :]
+        s = 2 * p + h
+        part = lambda t, q: t[:, 32 * (N * h + q):32 * (N * h + q) + 32]
+        mine = rank // 2
+
+        def add(j):
+            x = lambda w: T.Rs[:, s - 2, 0:w] if j < 0 else T.LAND[:, s - 2, 16 * j:16 * j + w]
+            w = 48 if j in (-1, 2) else 16
+            for ps, turn, nm, bk in ((lambda a, b: pB[a:b, 16:24, :], T.Pr, "Pr", bB), (lambda a, b: pA[a:b, 0:64], T.Ib, "Ib", bA)):
+                two = [(ps(64, 64 + w), x(w), turn[:, 0:64], j < 0, j == 2), (ps(96, 112), x(16), turn[:, 64:128], False, False)]
+                mm(two[::-1] if j == 2 else two, 128, [nm, "Rs%d" % (s - 2), "LANDz"], bk, [arrived[s - 2][j]] if j >= 0 else ())
+
+        def clamp():
+            add(2)
+            ts(SP[64:112, 1::2, :], pB[64:112, 16:24, :], -31.0, 31.0, A.max, A.min, 64, (), [sp[2]], bB)
+            ts(SQ[64:112, :], pA[64:112, 0:64], -31.0, 31.0, A.max, A.min, 64, (), [sq[2]], bA)
+
+        def distance():
+            mm([(pB[:, 0:8, 4 * b:4 * b + 4], T.WZ[0:KR, 1 - e:17 - e, b::2], SP[0:KR, 1::2, e::2], e == 0, e == 1)
+                for b in (0, 1) for e in (0, 1)], 256, sp + wz, bB)
+            ts(B("zoff")[:], pB[:, 0:8, :], float(PAD), float(WC - 1), A.add, A.min, 64, (), [n("zoff")], bB)
+
+        def both(offs, k):
+            gather("V", G[:, 0:16 * k], T.W1, B(offs)[:, 0:k], k, win1 + [n(offs)], [n("Ga")])
+            gather("S", G[:, 16 * k:1024], T.W1, B(offs)[:, k:64], 64 - k, win1 + [n(offs)], [n("Gb")])
+
+        def floor_x():
+            psX = pB[:, 8:16, :]
+            mm([(psX, SP[0:KR, 1 - b:17 - b, :], T.WX[0:KR, b::2], b == 0, b == 1) for b in (0, 1)], 128, sp + ["WX"], bB)
+            ts(B("DX")[:, 1::3], psX, MAGIC8, -MAGIC8, A.add, A.add, 64, (), [n("x")], bB)
+
+        def constants():
+            if p == 2 and h == 0:
+                sfill(T.PAT[0:1, :, 2], 0.0, 64, ["PAT2"], (), 1)
+            mm([(pC[:, 0:192], T.ones[0:2, :], T.PC[0:2], True, False)], 192, ["ones", "PC1", "PC2"], bC)
+            mm([(pD[:, 0:64 * ns], T.WT[0:4, :], T.PAT[0:4, :, 0:ns], True, False)], 64 * ns, ["WT"] + pat, bD)
+
+        def sides():
+            mm([(slot(0), T.WN[0:KR, :], SQ[0:KR, :], False, False), (slot(1), T.WK[0:KR, :], SQ[0:KR, :], False, False)],
+               128, sq + ["WK", "WN"], bD)
+
+        def turn1():
+            mm([(pC[:, 24 * c:24 * c + 24], G[:, c::8], T.SEL1[:], False, c == 7) for c in range(8)], 512,
+               [n("Ga"), n("Gb"), "SEL10", "SEL11", "SEL12"], bC)
+
+        def pixel():
+            scan(O1[:], B("DX")[:], pC[:, 0:192], A.mult, A.add, 192, [n("x"), n("DXa"), n("DXb")], [n("O1")], bC)
+            ts(B("off")[:], O1[:, 2::3], -COL0, float(WC - 1), A.add, A.min, 64, [n("O1")], [n("off")])
+            act(R1[:, 1:129:2], O1[:, 1::3], 64, [n("O1"), "RZ"], [n("R1")], scale=8192.0, bias=-63.5 * 8192, f=F.Relu)
+            act(R2[:, 1:129:2], O1[:, 1::3], 64, [n("O1"), "RZ"], [n("R2")], scale=-8192.0, bias=-64.5 * 8192, f=F.Relu)
+            if p == 2:
+                act(OF[:, 1:129:2], O1[:, 2::3], 64, [n("O1"), n("OFz")], [n("OF")], bias=-COL0)
+
+        def off_image():
+            mm([(slot(0), R[:, 1 - b:129 - b], T.Ineg[:, 64 * b:64 * b + 64], False, False) for R in (R1, R2) for b in (0, 1)], 256,
+               [n("R1"), n("R2"), "Ineg"], bD)
+            if p == 2:
+                mm([(slot(2), OF[:, 1 - b:129 - b], T.I17[:, 64 * b:64 * b + 64], False, False) for b in (0, 1)], 512, [n("OF"), "I17"], bD)
+
+        def turn2():
+            sel, seln = (T.SEL3, ["SEL3a", "SEL3b"]) if p == 2 else (T.SEL2, sel2)
+            mm([(pD[:, 8 * ns * e:8 * ns * (e + 1)], G[:, e::8], sel[:], False, e == 7) for e in range(8)], 512,
+               [n("Ga"), n("Gb")] + seln, bD)
+
+        def test():
+            if p < 2:
+                scan(P5[:], T.D5[:], pD[:, 0:320], A.max, A.min, 320, ["D5"], [n("P5")], bD)
+            else:
+                scan(B("O3")[:], T.D3[:], pD[:, 0:192], A.max, A.min, 192, ["D3"], [n("O3")], bD)
+                ts(B("offb")[:], B("O3")[:, 2::3], float(1 << 17), float(WC - 1), A.mult, A.min, 64, [n("O3")], [n("offb")])
+
+        def write():
+            mm([(pA[0:64, 128:144], P5[:, 4::5], T.GSEL4[:], True, False), (pA[0:64, 128:144], P5[:, 2::5], T.GSEL[:], False, True),
+                (pA[64:128, 128:144], P5[:, 4::5], T.GSEL2[:], True, False), (pA[64:128, 128:144], P5[:, 3::5], T.GSEL[:], False, True)],
+               256, [n("P5"), "GSEL", "GSEL4", "GSEL2"], bA)
+            src = T.Rs[:, s, 0:16]
+            act(src, pA[:, 128:144], 16, ["Rs"], ["Rs%d" % s], bA, scale=2048.0)
+            k = send([(peers, mask, "arr%d_%d" % (s, rank), src, [T.LAND[:, s, 16 * j:16 * j + 16] for j in range(3)])], ["Rs%d" % s])
+            arrived[s] = [op("-", None, ("c", j + 1), after=[k], sem="arr%d_%d" % (s, q), val=neng) for j, q in enumerate(senders)]
+
+        def fetch(j):
+            pair = mine if j else 1 - mine
+            for eng, q in (("V", 2 * pair), ("S", 2 * pair + 1)):
+                gather(eng, H[:, 256 * q:256 * q + 256], T.W2, B("offb")[:, 16 * q:16 * q + 16], 16,
+                       ["W2a", "W2b", "W20", "W21", "W22", n("offb")], [n("H%d%s" % (j, eng))])
+
+        def give(j):
+            pair = mine if j else 1 - mine
+            ps, bk = (pA, bA) if j else (pC, bC)
+            mm([(ps[:, 256 + b:320:2], T.Pm[:], H[:, 512 * pair + 2 * a + b:512 * pair + 512:16], a == 0, a == 7)
+                for b in (0, 1) for a in range(8)], 1024, [n("H%dV" % j), n("H%dS" % j), "Pm"], bk)
+            y0 = 32 * (N * h + 2 * pair)
+            cpy(T.Ys[:, y0:y0 + 64], ps[:, 256:320], 64, (), [n("Ys%d_" % j)], bk)
+            to = [q for q in (2 * pair, 2 * pair + 1) if q != rank]
+            ms = halves if len(to) == 2 else [mask]
+            k = send([([q], m, "arr%d_%d" % (s, rank), part(T.Ys, q), [part(T.LY, rank)]) for q, m in zip(to, ms)], [n("Ys%d_" % j)])
+            arrived.setdefault(s, []).extend(
+                (q, op("-", None, ("c", len(to)), after=[k], sem="arr%d_%d" % (s, q), val=neng // len(to))) for q in to)
+
+        def first_parts():
+            arr = arrived[s]
+            tt(Fo[:, 0:32], part(T.LY, arr[0][0]), part(T.LY, arr[1][0]), A.add, 64, (), [n("Fa")], None, [arr[0][1], arr[1][1]])
+            tt(Fo[:, 32:64], Fo[:, 0:32], part(T.Ys, rank), A.add, 64, [n("Fa"), n("Ys1_")], [n("Fb")])
+
+        def store():
+            arr = arrived[s]
+            tt(Fo[:, 64:96], Fo[:, 32:64], part(T.LY, arr[2][0]), A.add, 64, [n("Fb")], [n("Fo")], None, [arr[2][1]])
+            dma("Y", n("dY"), [(T.y[:, 256 * h:256 * h + 256], Fo[:, 64:96])], 16, [n("Fo")], ())
+        return dict(a=lambda: add(-1), b=lambda: add(0), c=lambda: add(1), d=clamp, z=distance, l=lambda: both("zoff", GL),
+                    x=floor_x, k=constants, m=sides, t=turn1, n=pixel, i=lambda: both("off", GI), u=off_image, r=turn2,
+                    s=test, w=write, f=lambda: fetch(0), g=lambda: give(0), F=lambda: fetch(1), G=lambda: give(1),
+                    e=first_parts, E=store)
+
+    def load_w2(k, r, after):
+        a0 = sum(CFG["W2"][:k])
+        dma("Y", "dW%d" % k, [(T.W2[16 * a:16 * a + 16, PAD:PAD + HW], T.cam[:]) for a in range(a0, a0 + CFG["W2"][k])],
+            256 * CFG["W2"][k], r, ["W2%d" % k], after)
+
+    load_w2(0, win1, ())
+    for p in range(3):
+        steps = [half_pass(p, 0), half_pass(p, 1)]
+        for name in ORDER[p].split():
+            (steps[int(name[1])][name[0]] if name[1:] else once[name])()
         if p == 0:
-            mm([(psX, r8(B("RX")), GT, True, False), (psX, r8(T.A8), GTc, False, True)], 512,
-               ["GO", "GOq", n("RX"), "A8"], bC)
-            cpy(B("xi")[:], psX, 64, (), [n("xi")], bC)
-            act(B("X0")[:], psX, 64, (), [n("X0")], bC)
-            act(r8(B("RDa")), r8(B("RZ")), 128, [n("RZ"), "c1"], [n("RDa")], bias=r8(T.c1, 5, 6))
-            act(r8(B("RDb")), r8(B("RZ")), 128, [n("RZ"), "c2"], [n("RDb")], bias=r8(T.c2, 5, 6))
-            mm([(pD[:, 256:320], r8(B("RDa")), GT, True, False), (pD[:, 256:320], r8(T.NB), GTc, False, True),
-                (pD[:, 320:384], r8(B("RDb")), GT, True, False), (pD[:, 320:384], r8(T.NB), GTc, False, True)],
-               1024, ["GO", "GOq", n("RDa"), n("RDb"), "NB"], bD)
-            act(B("D0")[:, 0:64], pD[:, 256:320], 64, (), [n("D0a")], bD)
-            act(B("D0")[:, 64:128], pD[:, 320:384], 64, (), [n("D0b")], bD, scale=-1.0)
-        mm([(pD[:, 0:256], r16(T.ZR), r16(T.ZR, 0, 256), True, False)], 256, ["ZR"], bD)
-        mm([(pD[:, 0:128], T.I32[:], B("D0")[:], False, False)], 512, ["I32", n("D0a"), n("D0b")], bD)
-        if p > 0:
-            s = 2 * (p - 1) + h
-            psS = r16(pA)
-            if CFG["FOLD"]:
-                P = B("Pp" if p == 1 else "Pq")
-                mm([(psS, P[:, a, :, :], T.Ib[:], a == 0, False) for a in range(8)], 1024, ["Pa%d" % s, "Pb%d" % s, "Ib"], bA)
-            else:
-                mm([(psS, T.Rs[:, 16 * s:16 * s + 16], T.Ib[:], True, False)], 128, ["Rs%d" % s, "Ib"], bA)
-            for j, q in enumerate(senders):
-                mm([(psS, T.LAND[:, 16 * (N * s + q):16 * (N * s + q) + 16], T.Ib[:], False, j == 2)],
-                   128, ["Ib"], bA, [arrived[(p - 1, h)][j]])
-            SP = B("SP")
-            ts(r16(SP), psS, -31.0, 31.0, A.max, A.min, 128, (), [n("SP")], bA)
-            mm([(psZ, r16(T.WZ0), SP[0:16, 0::2], False, False), (psZ, r16(T.WZ1), SP[0:16, 1::2], False, True)],
-               128, ["WZ0", "WZ1", n("SP")], bB)
-            mm([(psX, r16(SP), r16(T.WX, 0, 64), True, True)], 64, ["WX", n("SP")], bC)
-            tt(B("xi")[:], psX, B("X0")[:], A.add, 64, [n("X0")], [n("xi")], bC)
-            mm([(pD[:, 0:128], r16(SP), r16(T.WD), False, False)], 128, ["WDa", "WDb", n("SP")], bD)
-
-        ts(B("zoff")[:], psZ, 0.0, float(WC - 1), A.max, A.min, 64, (), [n("zoff")], bB)
-        gather("V", G[:, 0:16 * GV], T.W1, B("zoff")[:, 0:GV], GV, win1 + [n("zoff")], [n("Ga")])
-        gather("S", G[:, 16 * GV:1024], T.W1, B("zoff")[:, GV:64], 64 - GV, win1 + [n("zoff")], [n("Gb")])
-        mm([(pC[:, 128 + c:256:8], G[:, c::8], T.SEL1[:], True, True) for c in range(8)], 512,
-           [n("Ga"), n("Gb"), "SEL1a", "SEL1b"], bC)
-        tt(B("t")[:], pC[:, 128:192], B("xi")[:], A.mult, 64, [n("xi")], [n("t")], bC)
-        act(B("Bv")[:, 1::2, :], pC[:, 192:256], 64, (), [n("Bv")], bC, bias=-160.0)
-        ts(B("Bu")[:, 1::2, :], B("t")[:], 191.5 + 1.0 / 8192, 128.0, A.add, A.max, 64, [n("t")], [n("Bu")])
-
-        def turn(ps, buf, ident, first, last):
-            return [(ps, buf[:, 1:17, :], ident[:, 0::2], first, False), (ps, buf[:, 0:16, :], ident[:, 1::2], False, last)]
-        psO = pA[:, 128:192]
-        mm(turn(psO, B("Bu"), T.Ib, True, False) + turn(psO, B("Bv"), T.I128, False, True), 256,
-           [n("Bu"), n("Bv"), "Ib", "I128"], bA)
-        ts(B("off")[:], psO, 0.0, float(WC - 1), A.max, A.min, 64, (), [n("off")], bA)
-        gather("V", G[:, 0:16 * GV], T.W1, B("off")[:, 0:GV], GV, win1 + [n("off")], [n("Ga")])
-        act(B("au")[:], B("t")[:], 64, [n("t")], [n("au")], bias=1.0 / 8192, f=F.Abs)
-        act(B("pen")[:], B("au")[:], 64, [n("au")], [n("pen")], scale=float(1 << 23), bias=-float(1 << 29), f=F.Relu)
-        gather("S", G[:, 16 * GV:1024], T.W1, B("off")[:, GV:64], 64 - GV, win1 + [n("off")], [n("Gb")])
-        mm([(pD[:, 0:64], T.I128[:], B("pen")[:], False, False)], 64, ["I128", n("pen")], bD)
-        if p == 2:
-            psO2 = pA[:, 256:320]
-            mm(turn(psO2, B("Bu"), T.Ib, True, False) + turn(psO2, B("Bv"), T.I128, False, False), 256,
-               [n("Bu"), n("Bv"), "Ib", "I128"], bA)
-        wd = 128 if p == 2 else 256
-        mm([(pD[:, c:wd:8], G[:, c::8], T.SEL2[:, 0:wd // 8], False, c == 7) for c in range(8)], 512,
-           [n("Ga"), n("Gb")] + sel2, bD)
-        ts(B("Xk")[:], pD[:, 0:64], 0.0, -1.0e9, A.is_gt, A.mult, 64, (), [n("Xk")], bD)
-        if p < 2:
-            s = 2 * p + h
-            tt(B("keep")[:], pD[:, 64:128], B("Xk")[:], A.is_le, 64, [n("Xk")], [n("keep")], bD)
-            P = B("Pp" if p == 0 else "Pq")
-            pa, pb = "Pa%d" % s, "Pb%d" % s
-            tt(P[:, :, 0, :], pD[:, 128:192], B("keep")[:], A.mult, 64, [n("keep")], [pa], bD)
-            tt(P[:, :, 1, :], pD[:, 192:256], B("keep")[:], A.mult, 64, [n("keep")], [pb], bD)
-            if CFG["FOLD"]:
-                srcs, alu, rd = [P[:, a, :, :] for a in range(8)], 1, [pa, pb]
-            else:
-                psR = pA[:, 192:208]
-                mm([(psR, T.Ib[:], P[:, a, :, :], a == 0, a == 7) for a in range(8)], 512, [pa, pb, "Ib"], bA)
-                srcs, alu, rd = [T.Rs[:, 16 * s:16 * s + 16]], 0, ["Rs%d" % s]
-                act(srcs[0], psR, 16, (), rd, bA)
-            c0 = 16 * (N * s + rank)
-
-            def send():
-                g.remote_dma_fused([RemoteDMATransfer(
-                    dst_ids=[DstId(rid=dst[q][0], pnc=dst[q][1]) for q in peers], dma_engine_mask=mask,
-                    remote_sem=T.sem["arr%d_%d" % (s, rank)], srcs=srcs, dsts=[T.LAND[:, c0:c0 + 16] for q in peers],
-                    alu_op=alu)], local_sem=T.sem.sent)
-            sent[0] += neng
-            k = op("G", send, ("r",), rd, (), sem="none")
-            arrived[(p, h)] = [op("-", None, ("c", j + 1), after=[k], sem="arr%d_%d" % (s, q), val=neng)
-                               for j, q in enumerate(senders)]
-            return
-        tt(B("Bd")[:, 1::2, :], pD[:, 64:128], B("Xk")[:], A.is_gt, 64, [n("Xk")], [n("Bd")], bD)
-        mm(turn(psO2, B("Bd"), T.Ibig, False, True), 128, [n("Bd"), "Ibig"], bA)
-        ts(B("offb")[:], psO2, 0.0, float(WC - 1), A.max, A.min, 64, (), [n("offb")], bA)
-        win2 = ["W2a", "W2b", "W2c", "W2d", n("offb"), n("Gz")]
-        s = 4 + h
-        arr = []
-        plan = [(peers[0], "V", pC, 256, bC), (peers[1], "S", pB, 64, bB), (peers[2], "V", pD, 384, bD), (rank, "S", pA, 320, bA)]
-        op("-", None, ("c", 0), (), [n("Ga"), n("Gb"), n("Gz")])
-        for j, (q, eng, pb, c0, bk) in enumerate(plan):
-            gather(eng, G[:, 256 * q:256 * q + 256], T.W2, B("offb")[:, 16 * q:16 * q + 16], 16, win2, [n("Gq%d" % q)])
-            mm([(pb[:, c0 + 16 * e:c0 + 16 * e + 16], G[:, 256 * q + 128 * e:256 * q + 128 * e + 128], T.GSEL[:], True, True)
-                for e in range(2)], 128, [n("Gq%d" % q), "GSEL"], bk)
-            y0 = 32 * (N * h + q)
-            cpy(T.Ys[:, y0:y0 + 32], pb[:, c0:c0 + 32], 32, (), [n("Ys%d_" % q)], bk)
-            if q != rank:
-                l0 = 32 * (N * h + rank)
-
-                def send1(q=q, y0=y0, l0=l0):
-                    g.remote_dma(T.LY[:, l0:l0 + 32], T.Ys[:, y0:y0 + 32], T.sem["arr%d_%d" % (s, rank)], T.sem.sent,
-                                 dst[q][1], dst[q][0], mask)
-                sent[0] += neng
-                k = op("G", send1, ("r",), [n("Ys%d_" % q)], (), sem="none")
-                arr.append(op("-", None, ("c", 1), after=[k], sem="arr%d_%d" % (s, senders[j]), val=neng))
-        psF = pA[0:32, 384:512]
-        y0 = 32 * (N * h + rank)
-        mm([(psF, T.Ys[:, y0:y0 + 32], T.I16[:], True, False)], 128, [n("Ys%d_" % rank), "I16"], bA)
-        for j, q in enumerate(senders):
-            mm([(psF, T.LY[:, 32 * (N * h + q):32 * (N * h + q) + 32], T.I16[:], False, j == 2)], 128, ["I16"], bA, [arr[j]])
-        cpy(B("Fo")[0:32, :], psF, 128, (), [n("Fo")], bA)
-        dma("Y", n("dYa"), [(T.y[:, 256 * h:256 * h + 128], B("Fo")[0:16, :])], 8, [n("Fo")], ())
-        dma("S", n("dYb"), [(T.y[:, 256 * h + 128:256 * h + 256], B("Fo")[16:32, :])], 8, [n("Fo")], ())
-
-    half_pass(0, 0)
-    half_pass(0, 1)
-    cur[0] = 0
-    dma("Y", "dWa", [(T.W2[16 * a:16 * a + 16, PAD:PAD + HW], T.cam[:]) for a in range(4)], 1024, win1, ["W2c"])
-    late_setup()
-    half_pass(1, 0)
-    half_pass(1, 1)
-    cur[0] = 0
-    dma("Y", "dWb", [(T.W2[16 * a:16 * a + 16, PAD:PAD + HW], T.cam[:]) for a in range(4, 8)], 1024, (), ["W2d"],
-        [arrived[(0, 1)][2]])
-    last_setup()
-    half_pass(2, 0)
-    half_pass(2, 1)
+            last_setup()
+            load_w2(1, (), [arrived[1][2]])
+        if p == 1:
+            load_w2(2, (), [arrived[2][2]])
     return ops, sent[0]
-
-
-PLANS = [
-    dict(hop=0.09, cyc=0.00104, gat=1.56, pe=0.0006, dl=2.0, dk=0.004, ri=0.5, rl=2.4, rr=0.7),
-    dict(hop=0.05, cyc=0.00085, gat=1.1, pe=0.00045, dl=1.5, dk=0.003, ri=0.3, rl=1.6, rr=0.4),
-    dict(hop=0.15, cyc=0.0012, gat=2.0, pe=0.001, dl=2.3, dk=0.005, ri=0.8, rl=3.0, rr=1.1),
-    dict(hop=0.15, cyc=0.0009, gat=1.2, pe=0.0008, dl=2.0, dk=0.004, ri=0.8, rl=3.0, rr=1.0),
-    dict(hop=0.06, cyc=0.0012, gat=2.0, pe=0.0005, dl=1.8, dk=0.004, ri=0.4, rl=1.8, rr=0.5),
-]
-
-
-def price(ops, q):
-    out = []
-    for o in ops:
-        c = o["cost"]
-        out.append({"v": lambda: (0.04 + max(c[1], 64) * q["cyc"], 0.0), "i": lambda: (0.06 + c[1] * q["gat"] * q["cyc"], 0.0),
-                    "p": lambda: (0.03 + c[1] * q["pe"], 0.0), "g": lambda: (0.17 + 2 * c[1] * q["cyc"], 0.0),
-                    "d": lambda: (0.1 * c[1], q["dl"] + c[2] * q["dk"]), "r": lambda: (q["ri"], 0.0),
-                    "c": lambda: (0.0, q["rl"] + c[1] * q["rr"] if c[1] else 0.0)}[c[0]]())
-    return out
-
-
-def replay(ops, order, cost, hop):
-    done, start, free = [0.0] * len(ops), [0.0] * len(ops), {}
-    for k in order:
-        e = ops[k]["eng"]
-        t = 0.0 if e == "-" else free.get(e, 0.0)
-        for d in ops[k]["deps"]:
-            t = max(t, done[d] + (0.0 if e == "-" or ops[d]["eng"] == e == "P" else hop))
-        start[k] = t
-        free[e] = t + cost[k][0]
-        done[k] = t + cost[k][0] + cost[k][1]
-    return max(done), start, done
-
-
-def lay_once(ops, kids, cost, hop, bias, look, noise):
-    n = len(ops)
-    tail = [0.0] * n
-    for k in range(n - 1, -1, -1):
-        tail[k] = cost[k][0] + cost[k][1] + max([hop + tail[c] for c in kids[k]] + [0.0])
-    tail = [tail[k] - bias * ops[k]["half"] + noise[k] for k in range(n)]
-    left = [len(o["deps"]) for o in ops]
-    ready = [k for k in range(n) if left[k] == 0]
-    done, free, order, at = [0.0] * n, {}, [], {k: 0.0 for k in ready}
-    while ready:
-        e = {k: at[k] if ops[k]["eng"] == "-" else max(at[k], free.get(ops[k]["eng"], 0.0)) for k in ready}
-        k0 = min(ready, key=lambda k: (e[k], -tail[k]))
-        near = [k for k in ready if ops[k]["eng"] == ops[k0]["eng"] and e[k] <= e[k0] + look * cost[k0][0]]
-        k = max(near, key=lambda j: tail[j])
-        ready.remove(k)
-        eng = ops[k]["eng"]
-        free[eng] = e[k] + cost[k][0]
-        done[k] = free[eng] + cost[k][1]
-        order.append(k)
-        for c in kids[k]:
-            left[c] -= 1
-            if left[c] == 0:
-                ec = ops[c]["eng"]
-                at[c] = max(done[d] + (0.0 if ec == "-" or ops[d]["eng"] == ec == "P" else hop) for d in ops[c]["deps"])
-                ready.append(c)
-    return order
-
-
-LAID = {}
-
-
-def lay_out(ops):
-    if "order" in LAID:
-        return LAID["order"]
-    n = len(ops)
-    kids = [[] for _ in range(n)]
-    for k, o in enumerate(ops):
-        for d in o["deps"]:
-            kids[d].append(k)
-    costs = [price(ops, q) for q in PLANS]
-    state = [CFG["SEED"]]
-
-    def rnd():
-        state[0] = (state[0] * 6364136223846793005 + 1442695040888963407) % (1 << 64)
-        return (state[0] >> 11) / float(1 << 53)
-    best = None
-    for it in range(CFG["TRIES"]):
-        if best is None or it < CFG["TRIES"] // 5:
-            amp = 0.6 * rnd()
-            par = (0 if rnd() < 0.5 else int(rnd() * len(PLANS)), 5.0 * rnd(), 1.2 * rnd(), [amp * rnd() for _k in range(n)])
-        else:
-            p0, share = best[3], 0.15 * rnd()
-            par = (p0[0], max(0.0, p0[1] + 0.3 * (rnd() - 0.5)), max(0.0, p0[2] + 0.1 * (rnd() - 0.5)),
-                   [x + 1.5 * (rnd() - 0.5) if rnd() < share else x for x in p0[3]])
-        order = lay_once(ops, kids, costs[par[0]], PLANS[par[0]]["hop"], par[1], par[2], par[3])
-        ends = [replay(ops, order, costs[j], q["hop"])[0] for j, q in enumerate(PLANS)]
-        score = sum(ends) + ends[0]
-        if best is None or score <= best[0]:
-            best = (score, order, ends, par)
-    LAID["order"], LAID["ends"] = best[1], best[2]
-    return best[1]
 
 
 def rank_program(g, core, T, topo):
     if T.rank_of(core) is None:
         return
     ops, sent = build(g, core, T, topo)
-    order = lay_out(ops)
     queue = {"V": g.vector, "S": g.scalar, "P": g.tensor, "G": g, "Y": g.sync}
     count = {"sV": 0, "sS": 0, "sP": 0, "sG": 0}
     token, waited, totals = {}, {}, {}
 
-    def needs(k, eng):
-        out = []
-        for d in ops[k]["deps"]:
-            od = ops[d]
-            if od["eng"] == "-" and od["sem"] is None:
-                out += needs(d, eng)
-            elif not (od["eng"] == eng == "P" or od["sem"] == "none"):
-                out.append(d)
-        return out
+    def needs(o):
+        return [d for d in o["deps"] if not (ops[d]["eng"] == o["eng"] == "P" or ops[d]["sem"] == "none")]
     wanted = set()
-    for k in order:
-        if ops[k]["eng"] != "-":
-            wanted.update(needs(k, ops[k]["eng"]))
-    for k in order:
-        o = ops[k]
+    for o in ops:
+        if o["eng"] != "-":
+            wanted.update(needs(o))
+    for k, o in enumerate(ops):
         eng = o["eng"]
         if eng == "-":
-            if o["sem"] is not None:
-                token[k] = (o["sem"], o["val"])
-                totals[o["sem"]] = o["val"]
+            token[k] = (o["sem"], o["val"])
+            totals[o["sem"]] = o["val"]
             continue
         want = {}
-        for d in needs(k, eng):
+        for d in needs(o):
             s, v = token[d]
             want[s] = max(want.get(s, 0), v)
         for s in sorted(want):

@@ -6,31 +6,31 @@ HW = 8192
 PAD = 128
 WC = HW + 2 * PAD
 NP = 16
-PIECE = WC // NP
-KR = 112
+PIECE = HW // NP
+KR, KT = 96, 100
 MAGIC = 1.5 * (1 << 23)
 COL0 = MAGIC + 128 * 160 - 64 - PAD
 MAGIC8 = 8 * MAGIC
 ORDER = [
-    "O z0 z1 R x0 x1 K l0 k0 k1 t0 l1 m0 n0 i0 t1 S Q W n1 u0 r0 s0 i1 m1 w0 u1 r1 s1 w1",
-    "a0 b0 c0 d0 a1 z0 k0 l0 x0 b1 c1 t0 n0 d1 m0 i0 z1 k1 u0 l1 r0 s0 x1 t1 w0 n1 m1 i1 u1 r1 s1 w1",
-    "a0 b0 c0 d0 a1 z0 k0 k1 l0 b1 x0 t0 c1 n0 d1 m0 i0 z1 u0 r0 l1 s0 x1 t1 f0 m1 n1 i1 g0 F0 u1 r1 s1 f1 G0 F1 g1 G1 e0 E0 e1 E1",
+    "z0 z1 K l0 x0 l1 k0 t0 n0 k1 x1 m0 i0 t1 n1 Q u0 r0 s0 W m1 w0 P i1 u1 r1 s1 w1",
+    "a0 b0 k0 c0 d0 a1 z0 l0 b1 c1 x0 d1 k1 m0 t0 n0 z1 u0 i0 r0 l1 s0 x1 m1 t1 w0 n1 i1 u1 r1 s1 w1",
+    "a0 b0 c0 d0 a1 z0 l0 x0 t0 b1 c1 n0 d1 m0 i0 z1 m1 l1 u0 x1 r0 t1 s0 n1 u1 i1 f0 r1 F0 s1 f1 g0 G0 F1 g1 G1 e0 E0 e1 E1",
 ]
-CFG = dict(GL=((34, 24), (32, 34), (32, 24)), GI=((28, 44), (24, 32), (28, 34)), ZS=5, ZG=2, W2=(3, 3, 2))
+CFG = dict(GL=((32, 22), (32, 36), (32, 40)), GI=((32, 36), (28, 32), (18, 36)), GF=(20, 32), ZS=6, ZG=1, W2=(3, 3, 2))
 b16, f32, f16, i32, u16 = "bfloat16", "float32", "float16", "int32", "uint16"
 
 SCRATCH = {}
 for _d, _w, _names in (
     (b16, WC, "W1 W2"), (b16, HW, "C3"), (i32, 512, "L"), (b16, 512, "Lhi Llo Lv"), (i32, 8, "Pi"),
-    (f32, 8, "Pf hc stmp hcol"), (b16, 128, "ones mask GO GO2 Ib Pr Pm Ineg WK WN WX WT"), (f32, 128, "I17"),
-    (b16, 16, "GSEL GSEL4 GSEL2"), (b16, 192, "D3"), (f16, 256, "LY Ys"), (b16, 320, "D5 P50 P51"),
+    (f32, 8, "Pf hc hcol"), (b16, 128, "ones mask GO GO2 Ib Pr Pm Ineg WK WN WX"), (f32, 128, "I17"),
+    (b16, 16, "GSEL GSEL3 GSEL2"), (b16, 192, "D3"), (f16, 256, "LY Ys"), (b16, 320, "D5 P50 P51"),
     (f32, 96, "Fo0 Fo1"), (f32, 136, "OF0 OF1"), (u16, 64, "zoff0 zoff1 off0 off1 offb0 offb1"), (b16, 1024, "G0 G1 H0 H1"),
-    (b16, 64, "SQ0 SQ1"), (f32, 192, "DX0 DX1 O10 O11 O30 O31"),
+    (b16, 64, "SQ0 SQ1"), (f32, 192, "O10 O11 O30 O31"), (f32, 384, "DX"),
 ):
     for _n in _names.split():
         SCRATCH[_n] = ("sbuf", [128, _w], _d)
-for _n, _s in (("LAB", [16, 16]), ("SEL1", [8, 3]), ("SEL2", [8, 5]), ("SEL3", [8, 3]), ("PAT", [64, 5]), ("PC", [64, 3]),
-               ("RZ", [4, 136]), ("WZ", [17, 16]), ("SP0", [17, 8]), ("SP1", [17, 8]), ("Rs", [4, 48]), ("LAND", [4, 80])):
+for _n, _s in (("LAB", [16, 16]), ("SEL1", [8, 3]), ("SEL2", [8, 5]), ("SEL3", [8, 3]), ("RZ", [4, 136]), ("WZ", [17, 16]),
+               ("SP0", [17, 8]), ("SP1", [17, 8]), ("Rs", [4, 32]), ("LAND", [12, 32])):
     SCRATCH[_n] = ("sbuf", [128] + _s, b16)
 for _h in "01":
     SCRATCH["psA" + _h] = ("psum", [128, 512], f32)
@@ -38,7 +38,7 @@ for _h in "01":
     SCRATCH["psC" + _h] = ("psum", [128, 512], f32)
     SCRATCH["psD" + _h] = ("psum", [128, 512], f32)
 
-DMAS = ["dL", "dP", "dC3", "dC", "dHi", "dLo", "dV", "dW0", "dW1", "dW2", "dY0", "dY1"]
+DMAS = ["dL", "dP", "dC3", "dC0", "dC1", "dHi", "dLo", "dV", "dW0", "dW1", "dW2", "dY0", "dY1"]
 SEMAPHORES = ["sV", "sS", "sP", "sG", "sent"] + ["arr%d_%d" % (k, r) for k in range(6) for r in range(N)] + DMAS
 
 
@@ -90,8 +90,8 @@ def build(g, core, T, topo):
     def act(out, a, n, r, w, b=None, bias=0.0, scale=1.0, f=F.Identity):
         return op("S", lambda: S.activation(out, a, f, bias=bias, scale=scale), ("v", n), r, w, b)
 
-    def sfill(out, c, n, w, r=(), p1=128):
-        return act(out, T.W1[0:p1, 0:n], n, ["Wz0"] + list(r), w, bias=c)
+    def sfill(out, c, n, w, r=(), p0=0, p1=128):
+        return act(out, T.W1[p0:p1, 0:n], n, ["zero"] + list(r), w, bias=c)
 
     def mm(lst, cyc, r, b, after=()):
         def fn():
@@ -104,8 +104,8 @@ def build(g, core, T, topo):
     def iota(out, pat, base, cm, n, w, r=()):
         return op("G", lambda: g.iota(out, pat, base, cm, allow_small_or_imprecise_dtypes=True), ("g", n), r, w)
 
-    def mark(out, a, pat, c, base, n, w):
-        return op("G", lambda: g.affine_select(out, a, pat, A.not_equal, c, base, 1), ("g", n), ["Wz0"], w)
+    def mark(out, a, pat, c, base, n, w, how=A.not_equal, cm=1):
+        return op("G", lambda: g.affine_select(out, a, pat, how, c, base, cm), ("g", n), ["zero"], w)
 
     def dma(q, sem, pairs, kb, r, w, after=()):
         e = g.sync if q == "Y" else S
@@ -146,143 +146,154 @@ def build(g, core, T, topo):
     dma("Y", "dC3", [(T.C3[0:2, :], T.cam[0:2, :]), (T.C3[2:3, :], T.cam[15:16, :])], 48, (), ["C3"])
 
     zn = ["Wz%d" % k for k in range(NP)]
-    piece = lambda k: T.W1[:, k * PIECE:(k + 1) * PIECE]
+    piece = lambda k: T.W1[:, PAD + k * PIECE:PAD + (k + 1) * PIECE]
     ZS, ZG = CFG["ZS"], CFG["ZG"]
-    fill(piece(0), 0.0, PIECE // 2, [zn[0]])
-    fill(T.ones[:], 1.0, 64, ["ones"])
-    fill(T.mask[:], 0.0, 64, ["mask"])
+    zero = T.W1[:, 0:PAD]
+    fill(piece(NP - 1), 1.0, PIECE // 2, [zn[-1]])
+    fill(T.mask[:], 0.0, 64, ["maskz"])
+    fill(zero, 0.0, 64, ["zero"])
     fill(T.LAB[0:8], 0.0, 128, ["LAB"])
-    fill(T.mask[0:8, :], 1.0, 64, ["mask"])
-    for k in range(1, 1 + ZS):
-        act(piece(k), piece(0), PIECE, [zn[0]], [zn[k]])
-    for k in range(1 + ZS, 1 + ZS + ZG):
-        iota(piece(k), [[0, PIECE]], 0, 0, PIECE, [zn[k]])
-    for k in range(1 + ZS + ZG, NP - 3):
-        fill(piece(k), 0.0, PIECE // 2, [zn[k]])
-    zero = T.W1[:, 0:128]
+    fill(T.mask[0:8, :], 1.0, 64, ["mask"], ["maskz"])
+    fill(T.mask[KR:KT, :], 4.0, 64, ["mask4"], ["maskz"])
+    by_s = [0, 1, 2] + list(range(8, 5 + ZS))
+    by_g = list(range(3, 3 + ZG))
+    by_v = [k for k in range(NP - 1) if k not in by_s + by_g]
+    for k in by_s:
+        act(piece(k), piece(NP - 1), PIECE, [zn[-1]], [zn[k]])
+    for k in by_g:
+        iota(piece(k), [[0, PIECE]], 1, 0, PIECE, [zn[k]])
+    for k in by_v[:-4]:
+        fill(piece(k), 1.0, PIECE // 2, [zn[k]])
+
+    def image_rows(k):
+        c0, c1 = k * HW // 2, (k + 1) * HW // 2
+        dma("Y", "dC%d" % k, [(T.W1[16 * a:16 * a + 3, PAD + c0:PAD + c1], T.C3[0:3, c0:c1]) for a in range(8)], 192,
+            ["C3"] + zn[8 * k:8 * k + 8], ["Wc%d" % k])
+    image_rows(0)
+    s1 = lambda k, row, c, first: mark(T.SEL1[:, :, k], zero[:, 0:8] if first else T.SEL1[:, :, k], [[-16, 8]], c, -row, 8, ["SEL1%d" % k])
     mark(T.GO[0:8, :], zero[0:8], [[-1, 8], [0, 16]], 1.0, 0, 128, ["GO"])
-    mark(T.mask[:], T.mask[:], [[-2, 8], [0, 8], [-1, 2]], 1.0, -64, 128, ["mask"])
+    mark(T.mask[:], T.mask[:], [[-2, 8], [0, 8], [-1, 2]], 1.0, -64, 128, ["mask", "mask4"])
     mark(T.GO2[0:8, :], zero[0:8], [[0, 8], [-1, 8], [0, 2]], 0.25, 0, 128, ["GO2"])
-    mark(T.mask[:], T.mask[:], [[-2, 8], [0, 8], [-1, 2]], 1.0, -96, 128, ["mask"])
-    mark(T.hcol[0:8, 0:1], T.W1[0:8, 0:1], [[0, 1]], 32.0, 0, 1, ["hcol"])
-    for rows, pt in ((5, [[8, 4], [0, 32]]), (4, [[0, 64], [8, 2]]), (3, [[0, 4], [256, 2], [0, 16]])):
+    mark(T.mask[:], T.mask[:], [[-2, 8], [0, 8], [-1, 2]], 1.0, -80, 128, ["mask"])
+    mark(T.hcol[:, 0:1], zero[:, 0:1], [[0, 1]], 32.0, 0, 1, ["hcol"])
+    for k, (rows, pt, row, c) in enumerate(((5, [[8, 4], [0, 32]], 3, 1.0 / 32768), (4, [[0, 64], [8, 2]], 6, -0.5),
+                                            (3, [[0, 4], [256, 2], [0, 16]], 5, 128.0))):
         iota(T.mask[0:rows, :], pt, 0, 0, 128, ["mask"])
+        s1(k, row, c, True)
+    iota(T.mask[0:2, :], [[0, 128]], 1, 0, 128, ["mask"])
 
     LAB = T.LAB
 
-    def pieces(k, blk, col, r):
+    def pieces(k, blk, col, r, between):
         two = T.Pi[0:8, 2 + 2 * k:4 + 2 * k]
         cpy(LAB[0:8, blk::8, col], two, 2, ["Pi"] + r, ["LABhi%d" % k])
-        if k:
-            fill(piece(NP - 3), 0.0, PIECE // 2, [zn[NP - 3]])
-        else:
-            fill(T.SP0[:], 0.0, 68, ["SP0z"])
+        between()
         tt(LAB[0:8, blk::8, col + 1], two, LAB[0:8, blk::8, col], A.subtract, 4, ["Pi", "LABhi%d" % k], ["LABlo%d" % k])
-    pieces(1, 7, 1, ["LAB"])
+    pieces(1, 6, 0, ["LAB"], lambda: fill(piece(by_v[-4]), 1.0, PIECE // 2, [zn[by_v[-4]]]))
     cpy(T.Pf[0:8, 0:2], T.Pi[0:8, 0:2], 2, ["Pi"], ["Pf"])
-    for k in range(NP - 2, NP):
-        fill(piece(k), 0.0, PIECE // 2, [zn[k]])
-    mm([(T.psB1[:, 0, 0:2], T.GO[0:8, :], LAB[0:8, 7, 1:3], True, False),
-        (T.psB1[:, 0, 0:2], T.GO[0:8, :], LAB[0:8, 7, 2:4], False, True)], 128, ["GO", "LABhi1", "LABlo1"], "B1")
+    fill(piece(by_v[-3]), 1.0, PIECE // 2, [zn[by_v[-3]]])
+    mm([(T.psB1[:, 0, 0:2], T.GO[0:8, :], LAB[0:8, 6, 0:2], True, False),
+        (T.psB1[:, 0, 0:2], T.GO[0:8, :], LAB[0:8, 6, 1:3], False, True)], 128, ["GO", "LABhi1", "LABlo1"], "B1")
     act(T.hc[:, 0:2], T.psB1[:, 0, 0:2], 2, (), ["hc"], "B1", scale=1.0 / 4096)
-    act(T.Pf[0:8, 2:3], T.Pf[0:8, 1:2], 1, ["Pf"], ["Pfn"], scale=-1.0)
+
+    col = lambda t, k: t[:, 256 * k:256 * k + 256]
+    m32 = [T.psA0[:, 0:256], T.psA1[:, 0:256]]
+    for k in (0, 1):
+        cpy(m32[k], col(T.L, k), 256, ["L"], (), "A%d" % k)
+    for k in by_v[-2:]:
+        fill(piece(k), 1.0, PIECE // 2, [zn[k]])
+    image_rows(1)
+    for k in (0, 1):
+        act(col(T.Lhi, k), m32[k], 256, (), ["Lhi%d" % k], "A%d" % k)
+    for k in (0, 1):
+        tt(col(T.Llo, k), m32[k], col(T.Lhi, k), A.subtract, 256, ["Lhi%d" % k], ["Llo%d" % k], "A%d" % k)
+        if k == 0:
+            fill(T.ones[0:8, 0:16], 1.0, 8, ["ones"])
+            fill(T.SP0[:], 0.0, 68, ["SP0z"])
+        act(col(T.Lv, 1 - k), m32[1 - k], 256, ["hc"], ["Lv%d" % (1 - k)], "A%d" % (1 - k), scale=T.hc[:, 0:1], bias=191.5 + 1.0 / 8192)
+    dma("Y", "dHi", [(T.W1[3::16, PAD:PAD + HW], T.Lhi[:])], 128, zn + ["Lhi0", "Lhi1"], ["Whi"])
+    dma("Y", "dLo", [(T.W1[4::16, PAD:PAD + HW], T.Llo[:])], 128, zn + ["Llo0", "Llo1"], ["Wlo"])
+    dma("Y", "dV", [(T.W1[5::16, PAD:PAD + HW], T.Lv[:])], 128, zn + ["Lv0", "Lv1"], ["Wv"])
+    win1 = zn + ["zero", "zero2", "Whi", "Wlo", "Wv", "Wc0", "Wc1"]
+
     lab = ["LABhi0", "LABlo0", "LABhi1", "LABlo1"]
-    for blk, col, c in ((15, 0, 1.0 / 2048), (15, 3, 0.5)):
-        lab.append("LABc%d_%d" % (blk, col))
-        sfill(LAB[0:8, blk, col:col + 1], c, 1, lab[-1:], ["LAB"], 8)
 
-    dma("Y", "dC", [(T.W1[16 * a:16 * a + 3, PAD:PAD + HW], T.C3[0:3, :]) for a in range(8)], 384, zn + ["C3"], ["Wc"])
-    cpy(T.psA1[:], T.L[:], 512, ["L"], (), "A1")
-    act(T.Lv[:], T.psA1[:], 512, ["hc"], ["Lv"], "A1", scale=T.hc[:, 0:1], bias=191.5 + 1.0 / 8192)
-    cpy(T.Lhi[:], T.L[:], 512, ["L"], ["Lhi"])
-    tt(T.Llo[:], T.psA1[:], T.Lhi[:], A.subtract, 512, ["Lhi"], ["Llo"], "A1")
-    dma("Y", "dHi", [(T.W1[3::16, PAD:PAD + HW], T.Lhi[:])], 128, zn + ["Lhi"], ["Whi"])
-    dma("S", "dV", [(T.W1[5::16, PAD:PAD + HW], T.Lv[:])], 128, zn + ["Lv"], ["Wv"])
-    dma("Y", "dLo", [(T.W1[4::16, PAD:PAD + HW], T.Llo[:])], 128, zn + ["Llo"], ["Wlo"])
-    win1 = zn + ["Whi", "Wlo", "Wv", "Wc"]
-
-    for b0, cx, cy, c in ((8, 2, 0, -1.5), (0, 0, 1, -15.5)):
-        for nm, out, n, k, r in (("x", LAB[0:8, b0:b0 + 5:4, :], 32, cx, "LAB"), ("y", LAB[0:8, b0 + 6, :], 16, cy, "LAB"),
-                                 ("u", LAB[0:8, b0, 0:5:4], 2, cy, "LABx%d" % b0)):
-            lab.append("LAB%s%d" % (nm, b0))
-            act(out, T.ones[0:8, 0:n], n, ["Pf", "Pfn", "ones", r], lab[-1:], scale=T.Pf[0:8, k:k + 1])
-        lab.append("LABk%d" % b0)
-        sfill(LAB[0:8, b0, 5:6], c, 1, lab[-1:], ["LABx%d" % b0], 8)
-    fill(T.SP1[:], 0.0, 68, ["SP1z"])
+    def factor(b0, j):
+        out, n = ((LAB[0:8, b0, 1:4], 3), (LAB[0:8, b0 + 4, :], 16), (LAB[0:8, b0, 0:5:4], 2), (LAB[0:8, b0 + 5, :], 16))[j]
+        lab.append("LABf%d_%d" % (b0, j))
+        if b0:
+            ts(out, T.ones[0:8, 0:n], T.Pf[0:8, 1 - j // 2:2 - j // 2], 1.0 if j // 2 else -1.0, A.mult, A.mult, n,
+               ["Pf", "ones", "LAB"], lab[-1:])
+        else:
+            act(out, T.ones[0:8, 0:n], n, ["Pf", "ones", "LAB"], lab[-1:], scale=T.Pf[0:8, j // 2:j // 2 + 1])
+    for blk, k, c in ((8, 5, -1.5), (14, 2, 0.5), (0, 5, -15.5)):
+        lab.append("LABk%d" % blk)
+        sfill(LAB[0:8, blk, k:k + 1], c, 1, lab[-1:], ["LAB"], 0, 8)
+    pieces(0, 0, 6, ["LAB"], lambda: [factor(8, j) for j in range(3)])
+    factor(8, 3)
+    fill(T.SP0[0:8, 1::2, :], 1.0, 32, ["SP0c"], ["SP0z"])
+    for j in range(4):
+        factor(0, j)
     fill(T.WZ[:], 0.0, 136, ["WZ"])
-    fill(T.PC[0:2], 0.0, 96, ["PCz"])
-    pieces(0, 0, 6, ["LABx0", "LABx8"])
-    ps = T.psB0
-    mm([(ps[0:KR, 0:16, :], LAB[0:8, 8:15, :], T.GO2[0:8, :], True, True),
-        (ps[0:KR, 16:32, :], LAB[0:8, 0:7, :], T.GO2[0:8, :], True, True),
-        (ps[0:4, 32:48, :], LAB[0:8, 15, 0:4], T.GO2[0:8, :], True, True)], 384, lab + ["GO2"], "B0")
-
-    def places(nm, val, gx, gy):
-        act(val(T[nm + "0"][0:8]), T.ones[0:8, 0:64], 64, [nm + "0z", "ones"], [nm + "0c"])
-        iota(val(T[nm + "0"][0:2]), gx, 0, 0, 64, [nm + "0c"])
-        iota(val(T[nm + "0"][0:1]), gy, 0, 0, 64, [nm + "0c"])
-        return lambda: act(val(T[nm + "1"][0:8]), val(T[nm + "0"][0:8]), 64, [nm + "0c", nm + "1z", "hcol"], [nm + "1c"],
-                           bias=T.hcol[0:8, 0:1])
-    sp1 = places("SP", lambda t: t[:, 1::2, :], [[16, 8], [0, 4], [128, 2]], [[0, 8], [64, 4], [0, 2]])
-    mark(T.Ib[:], zero, [[-1, 128]], 1.0, 0, 128, ["Ib"])
-    fill(T.PC[0:2, :, 1], 1.0 / 8192, 32, ["PC1"], ["PCz"])
     fill(T.SQ0[:], 0.0, 32, ["SQ0z"])
-    fill(T.PC[0:1, :, 1], -0.5, 32, ["PC1"])
-    act(T.mask[0:2, :], T.ones[0:2, :], 128, ["ones"], ["mask"])
-    fill(T.PAT[0:4], 0.0, 160, ["PATz"])
-    fill(T.SQ1[:], 0.0, 32, ["SQ1z"])
-    fill(T.PAT[0:4, :, 0:2], 4.0, 64, ["PAT0"], ["PATz"])
-    for h in (0, 1):
-        sfill(T["DX%d" % h][:, 0::3], 0.0, 64, ["DXa%d" % h])
-        sfill(T["DX%d" % h][:, 2::3], 1.0, 64, ["DXb%d" % h])
-    sq1 = places("SQ", lambda t: t[:], [[0, 4], [128, 2], [16, 8]], [[64, 4], [0, 16]])
-    tt(T.WK[0:KR, :], ps[0:KR, 0:16, :], T.mask[0:KR, :], A.mult, 128, ["mask"], ["WK"], "B0")
-    tt(T.WX[0:KR, :], ps[0:KR, 16:32, :], T.mask[0:KR, :], A.mult, 128, ["mask"], ["WX"], "B0")
+    fill(T.W1[:, PAD + HW:WC], 0.0, 64, ["zero2"])
+    ps = T.psB0
+    dist = [x for x in lab if not x.startswith("LABf0") and x != "LABk0"]
+    mm([(ps[0:112, 0:16, :], LAB[0:8, 8:15, :], T.GO2[0:8, :], True, True)], 128, dist + ["GO2"], "B0")
+    mm([(T.psB1[0:KR, 16:32, :], LAB[0:8, 0:6, :], T.GO2[0:8, :], True, True)], 128, lab + ["GO2"], "B1")
+
+    def places(nm, val, gx, gy, between):
+        iota(val[0:2], gx, 0, 0, 64, [nm])
+        between()
+        iota(val[0:1], gy, 0, 0, 64, [nm])
+    places("SP0c", T.SP0[:, 1::2, :], [[16, 8], [0, 4], [128, 2]], [[0, 8], [64, 4], [0, 2]], lambda: s1(0, 4, 1.0 / 32768, False))
+    s1(1, 7, 1.0 / 8192, False)
+    s1(2, 6, MAGIC, False)
+    tt(T.WK[0:KT, :], ps[0:KT, 0:16, :], T.mask[0:KT, :], A.mult, 128, ["mask"], ["WK"], "B0")
+    fill(T.SP1[:], 0.0, 68, ["SP1z"])
+    fill(T.SQ0[0:8], 1.0, 32, ["SQ0c"], ["SQ0z"])
     wz = ["WZ%d" % c for c in range(8)]
     for c in range(8):
         (cpy if c % 2 else act)(T.WZ[0:KR, 1::2, 2 * c:2 * c + 2], T.WK[0:KR, 16 * c:16 * c + 16], 16, ["WK", "WZ"], [wz[c]])
-    sp1()
-    cpy(T.WT[0:4, :], ps[0:4, 32:48, :], 128, (), ["WT"], "B0")
+    act(T.SP1[0:8, 1::2, :], T.SP0[0:8, 1::2, :], 64, ["SP0c", "SP1z", "hcol"], ["SP1c"], bias=T.hcol[0:8, 0:1])
+    tt(T.WX[0:KR, :], T.psB1[0:KR, 16:32, :], T.mask[0:KR, :], A.mult, 128, ["mask"], ["WX"], "B1")
+    fill(T.SQ0[KR:KT], 1.0, 32, ["SQ0t"], ["SQ0z"])
+    sfill(T.DX[:, 0::3], 0.0, 128, ["DXa"])
+    sfill(T.DX[:, 2::3], 1.0, 128, ["DXb"])
+    places("SQ0c", T.SQ0[:], [[0, 4], [128, 2], [16, 8]], [[64, 4], [0, 16]],
+           lambda: mark(T.SEL2[:, :, 2:5], zero[:, 0:24], [[16, 8], [0, 3]], 1.0 / 32, 6, 24, ["SEL22"], A.is_gt, -1))
+    iota(T.RZ[:, :, 0:130:2], [[0, 260]], 0, 0, 260, ["RZ"])
+    mark(T.SEL2[:, :, 2:5], T.SEL2[:, :, 2:5], [[16, 8], [-1, 3]], 0.0, 9, 24, ["SEL22"], A.is_gt, -1)
     mark(T.Ineg[:], zero, [[-8, 2], [-1, 8], [-16, 8]], -32768.0, 0, 128, ["Ineg"])
-    mark(T.Pr[:], zero, [[-64, 2], [-1, 8], [-8, 8]], 1.0, 0, 128, ["Pr"])
-    mark(T.Pm[:], zero, [[-1, 16], [-16, 8]], 1.0, 0, 128, ["Pm"])
-    tt(T.stmp[:], T.Ib[:, 3::16], T.Ib[:, 4::16], A.add, 16, ["Ib"], ["stmp"])
-    sfill(T.PC[0:1, :, 2], MAGIC, 64, ["PC2"], ["PCz"], 1)
-    sfill(T.SEL1[:, :, 1], 0.0, 8, ["SEL11"])
-    act(T.SEL1[:, :, 2], T.Ib[:, 5::16], 8, ["Ib"], ["SEL12"], scale=128.0)
-    act(T.SEL1[:, :, 0], T.stmp[:], 8, ["stmp"], ["SEL10"], scale=1.0 / 32768)
-    pat = ["PAT0", "PAT2", "PAT3", "PAT4"]
-    sel2 = ["SEL2%d" % k for k in range(5)]
-
-    def for_offsets():
-        fill(T.RZ[:], 0.0, 272, ["RZ"])
+    mark(T.SEL2[:, :, 2:4], T.SEL2[:, :, 2:4], [[-16, 8], [-1, 2]], 1.0 / 2048, 0, 16, ["SEL22"])
+    for k, c in ((0, 32.0), (1, -32.0)):
+        mark(T.SEL2[:, :, k], zero[:, 0:8], [[-16, 8]], c, -2, 8, ["SEL2%d" % k])
+    iota(T.D5[:], [[0, 320]], 0, 0, 320, ["D5z"])
+    mark(T.Ib[:], zero, [[-1, 128]], 1.0, 0, 128, ["Ib"])
+    iota(T.D5[:, 0::5], [[0, 64]], 1, 0, 64, ["D5"], ["D5z"])
+    iota(T.Rs[:], [[0, 128]], 0, 0, 128, ["Rs"])
+    sel2 = ["SEL20", "SEL21", "SEL22"]
 
     def for_sides():
-        for k, c in ((2, 512.0), (3, 256.0), (4, 128.0)):
-            sfill(T.PAT[0:1, :, k], c, 64, ["PAT%d" % k], ["PATz"], 1)
-        act(T.WN[0:KR, :], T.WK[0:KR, :], 128, ["WK"], ["WN"], scale=-1.0)
+        act(T.WN[0:KR, :], T.WK[0:KR, :], 128, ["WK"], ["WNa"], scale=-1.0)
+        act(T.WN[KR:KT, :], T.WK[KR:KT, :], 128, ["WK"], ["WNb"])
 
-    def for_turn2():
-        for k, (row, c) in enumerate(((2, 32.0), (2, -32.0), (0, 1.0 / 2048), (1, 1.0 / 2048), (0, 0.0))):
-            act(T.SEL2[:, :, k], T.Ib[:, row::16], 8, ["Ib"], ["SEL2%d" % k], scale=c)
-
-    def for_test():
-        fill(T.D5[:], 0.0, 160, ["D5z"])
-        fill(T.Rs[:], 0.0, 96, ["Rs"])
-        fill(T.D5[:, 0::5], 1.0, 32, ["D5"], ["D5z"])
+    def second_half():
+        act(T.SQ1[0:KT, :], T.SQ0[0:KT, :], 64, ["SQ0c", "SQ0t", "hcol"], ["SQ1z", "SQ1c", "SQ1t"], bias=T.hcol[0:KT, 0:1])
 
     def for_write():
         mm([(T.psA0[:, 0:16], T.mask[64:80, :], T.Ib[64:80, 64:80], True, True)], 64, ["mask", "Ib"], "A0")
         act(T.GSEL[:], T.psA0[:, 0:16], 16, (), ["GSEL"], "A0")
-        act(T.GSEL4[:], T.psA0[:, 0:16], 16, (), ["GSEL4"], "A0", scale=-4.0)
+        act(T.GSEL3[:], T.psA0[:, 0:16], 16, (), ["GSEL3"], "A0", scale=-3.0)
         act(T.GSEL2[:], T.psA0[:, 0:16], 16, (), ["GSEL2"], "A0", scale=-2.0)
-    once = dict(O=for_offsets, K=for_sides, Q=sq1, R=for_turn2, S=for_test, W=for_write)
+    once = dict(K=for_sides, Q=second_half, W=for_write,
+                P=lambda: mark(T.Pr[0:64, 0:64], zero[0:64, 0:64], [[-1, 8], [-8, 8]], 1.0, 0, 64, ["Pr"]))
 
     def last_setup():
-        fill(T.LAND[:, :, 48:80], 0.0, 64, ["LANDz"])
         fill(T.W2[:, 0:PAD], 0.0, 64, ["W2a"])
         fill(T.W2[:, PAD + HW:WC], 0.0, 64, ["W2b"])
         fill(T.D3[:], 0.0, 96, ["D3z"])
+        mark(T.Pm[:], zero, [[-1, 16], [-16, 8]], 1.0, 0, 128, ["Pm"])
         act(T.I17[:], T.Ineg[:], 128, ["Ineg"], ["I17"], scale=-1.0 / (1 << 32))
         act(T.SEL3[:, :, 0:2], T.SEL2[:, :, 0:2], 16, sel2, ["SEL3a"])
         sfill(T.SEL3[:, :, 2], 0.0, 8, ["SEL3b"])
@@ -300,7 +311,7 @@ def build(g, core, T, topo):
         bA, bB, bC, bD = n("A"), n("B"), n("C"), n("D")
         G, SP, SQ, O1, P5, H, OF, Fo = B("G"), B("SP"), B("SQ"), B("O1"), B("P5"), B("H"), B("OF"), B("Fo")
         sp = [n("SP") + x for x in ("zcs" if p else "zc")]
-        sq = [n("SQ") + x for x in ("zcs" if p else "zc")]
+        sq = [n("SQ") + x for x in ("zcts" if p else "zct")]
         GL, GI = CFG["GL"][p][h], CFG["GI"][p][h]
         ns = 3 if p == 2 else 5
         slot = lambda k: pD[:, k:64 * ns:ns]
@@ -310,47 +321,42 @@ def build(g, core, T, topo):
         mine = rank // 2
 
         def add(j):
-            x = lambda w: T.Rs[:, s - 2, 0:w] if j < 0 else T.LAND[:, s - 2, 16 * j:16 * j + w]
-            w = 48 if j in (-1, 2) else 16
-            for ps, turn, nm, bk in ((lambda a, b: pB[a:b, 16:24, :], T.Pr, "Pr", bB), (lambda a, b: pA[a:b, 0:64], T.Ib, "Ib", bA)):
-                two = [(ps(64, 64 + w), x(w), turn[:, 0:64], j < 0, j == 2), (ps(96, 112), x(16), turn[:, 64:128], False, False)]
-                mm(two[::-1] if j == 2 else two, 128, [nm, "Rs%d" % (s - 2), "LANDz"], bk, [arrived[s - 2][j]] if j >= 0 else ())
+            x = T.Rs[0:64, s - 2, :] if j < 0 else T.LAND[0:64, 3 * (s - 2) + j, :]
+            for ps, turn, nm, bk in ((pB[64:KR, 16:24, :], T.Pr, "Pr", bB), (pA[64:KR, 0:64], T.Ib, "Ib", bA)):
+                mm([(ps, x, turn[0:64, 0:64], j < 0, j == 2)], 64, [nm, "Rs%d" % (s - 2)], bk, [arrived[s - 2][j]] if j >= 0 else ())
 
         def clamp():
             add(2)
-            ts(SP[64:112, 1::2, :], pB[64:112, 16:24, :], -31.0, 31.0, A.max, A.min, 64, (), [sp[2]], bB)
-            ts(SQ[64:112, :], pA[64:112, 0:64], -31.0, 31.0, A.max, A.min, 64, (), [sq[2]], bA)
+            ts(SP[64:KR, 1::2, :], pB[64:KR, 16:24, :], -31.0, 31.0, A.max, A.min, 64, (), [n("SP") + "s"], bB)
+            ts(SQ[64:KR, :], pA[64:KR, 0:64], -31.0, 31.0, A.max, A.min, 64, (), [n("SQ") + "s"], bA)
 
         def distance():
             mm([(pB[:, 0:8, 4 * b:4 * b + 4], T.WZ[0:KR, 1 - e:17 - e, b::2], SP[0:KR, 1::2, e::2], e == 0, e == 1)
                 for b in (0, 1) for e in (0, 1)], 256, sp + wz, bB)
             ts(B("zoff")[:], pB[:, 0:8, :], float(PAD), float(WC - 1), A.add, A.min, 64, (), [n("zoff")], bB)
 
-        def both(offs, k):
-            gather("V", G[:, 0:16 * k], T.W1, B(offs)[:, 0:k], k, win1 + [n(offs)], [n("Ga")])
-            gather("S", G[:, 16 * k:1024], T.W1, B(offs)[:, k:64], 64 - k, win1 + [n(offs)], [n("Gb")])
+        def both(out, win, offs, k, r, w):
+            gather("V", out[:, 0:16 * k], win, B(offs)[:, 0:k], k, r + [n(offs)], [n(w + "a")])
+            gather("S", out[:, 16 * k:1024], win, B(offs)[:, k:64], 64 - k, r + [n(offs)], [n(w + "b")])
 
         def floor_x():
             psX = pB[:, 8:16, :]
             mm([(psX, SP[0:KR, 1 - b:17 - b, :], T.WX[0:KR, b::2], b == 0, b == 1) for b in (0, 1)], 128, sp + ["WX"], bB)
-            ts(B("DX")[:, 1::3], psX, MAGIC8, -MAGIC8, A.add, A.add, 64, (), [n("x")], bB)
-
-        def constants():
-            if p == 2 and h == 0:
-                sfill(T.PAT[0:1, :, 2], 0.0, 64, ["PAT2"], (), 1)
-            mm([(pC[:, 0:192], T.ones[0:2, :], T.PC[0:2], True, False)], 192, ["ones", "PC1", "PC2"], bC)
-            mm([(pD[:, 0:64 * ns], T.WT[0:4, :], T.PAT[0:4, :, 0:ns], True, False)], 64 * ns, ["WT"] + pat, bD)
+            ts(T.DX[:, 192 * h + 1:192 * h + 192:3], psX, MAGIC8, -MAGIC8, A.add, A.add, 64, (), [n("x")], bB)
 
         def sides():
-            mm([(slot(0), T.WN[0:KR, :], SQ[0:KR, :], False, False), (slot(1), T.WK[0:KR, :], SQ[0:KR, :], False, False)],
-               128, sq + ["WK", "WN"], bD)
+            mm([(slot(0), T.WN[0:KT, :], SQ[0:KT, :], p == 2, False), (slot(1), T.WK[0:KT, :], SQ[0:KT, :], False, False)],
+               128, sq + ["WK", "WNa", "WNb"], bD)
+
+        def clear():
+            mm([(slot(k), zero[0:1, :], zero[0:1, 0:64], k == 2, False) for k in (2, 3, 4)], 192, ["zero"], bD)
 
         def turn1():
-            mm([(pC[:, 24 * c:24 * c + 24], G[:, c::8], T.SEL1[:], False, c == 7) for c in range(8)], 512,
+            mm([(pC[:, 24 * c:24 * c + 24], G[:, c::8], T.SEL1[:], True, True) for c in range(8)], 512,
                [n("Ga"), n("Gb"), "SEL10", "SEL11", "SEL12"], bC)
 
         def pixel():
-            scan(O1[:], B("DX")[:], pC[:, 0:192], A.mult, A.add, 192, [n("x"), n("DXa"), n("DXb")], [n("O1")], bC)
+            scan(O1[:], T.DX[:, 192 * h:192 * h + 192], pC[:, 0:192], A.mult, A.add, 192, [n("x"), "DXa", "DXb"], [n("O1")], bC)
             ts(B("off")[:], O1[:, 2::3], -COL0, float(WC - 1), A.add, A.min, 64, [n("O1")], [n("off")])
             act(R1[:, 1:129:2], O1[:, 1::3], 64, [n("O1"), "RZ"], [n("R1")], scale=8192.0, bias=-63.5 * 8192, f=F.Relu)
             act(R2[:, 1:129:2], O1[:, 1::3], 64, [n("O1"), "RZ"], [n("R2")], scale=-8192.0, bias=-64.5 * 8192, f=F.Relu)
@@ -376,18 +382,17 @@ def build(g, core, T, topo):
                 ts(B("offb")[:], B("O3")[:, 2::3], float(1 << 17), float(WC - 1), A.mult, A.min, 64, [n("O3")], [n("offb")])
 
         def write():
-            mm([(pA[0:64, 128:144], P5[:, 4::5], T.GSEL4[:], True, False), (pA[0:64, 128:144], P5[:, 2::5], T.GSEL[:], False, True),
-                (pA[64:128, 128:144], P5[:, 4::5], T.GSEL2[:], True, False), (pA[64:128, 128:144], P5[:, 3::5], T.GSEL[:], False, True)],
-               256, [n("P5"), "GSEL", "GSEL4", "GSEL2"], bA)
-            src = T.Rs[:, s, 0:16]
-            act(src, pA[:, 128:144], 16, ["Rs"], ["Rs%d" % s], bA, scale=2048.0)
-            k = send([(peers, mask, "arr%d_%d" % (s, rank), src, [T.LAND[:, s, 16 * j:16 * j + 16] for j in range(3)])], ["Rs%d" % s])
+            mm([(pA[0:64, 128:144], P5[:, 4::5], T.GSEL3[:], True, False), (pA[0:64, 128:144], P5[:, 2::5], T.GSEL[:], False, True),
+                (pA[0:64, 144:160], P5[:, 4::5], T.GSEL2[:], True, False), (pA[0:64, 144:160], P5[:, 3::5], T.GSEL[:], False, True)],
+               256, [n("P5"), "GSEL", "GSEL3", "GSEL2"], bA)
+            act(T.Rs[0:64, s, :], pA[0:64, 128:160], 32, ["Rs"], ["Rs%d" % s], bA, scale=2048.0)
+            k = send([(peers, mask, "arr%d_%d" % (s, rank), T.Rs[:, s, :], [T.LAND[:, 3 * s + j, :] for j in range(3)])], ["Rs", "Rs%d" % s])
             arrived[s] = [op("-", None, ("c", j + 1), after=[k], sem="arr%d_%d" % (s, q), val=neng) for j, q in enumerate(senders)]
 
         def fetch(j):
-            pair = mine if j else 1 - mine
-            for eng, q in (("V", 2 * pair), ("S", 2 * pair + 1)):
-                gather(eng, H[:, 256 * q:256 * q + 256], T.W2, B("offb")[:, 16 * q:16 * q + 16], 16,
+            c0, k = 32 * (mine if j else 1 - mine), CFG["GF"][h] // 2
+            for eng, a, b in (("V", c0, c0 + k), ("S", c0 + k, c0 + 32)):
+                gather(eng, H[:, 16 * a:16 * b], T.W2, B("offb")[:, a:b], b - a,
                        ["W2a", "W2b", "W20", "W21", "W22", n("offb")], [n("H%d%s" % (j, eng))])
 
         def give(j):
@@ -412,9 +417,10 @@ def build(g, core, T, topo):
             arr = arrived[s]
             tt(Fo[:, 64:96], Fo[:, 32:64], part(T.LY, arr[2][0]), A.add, 64, [n("Fb")], [n("Fo")], None, [arr[2][1]])
             dma("Y", n("dY"), [(T.y[:, 256 * h:256 * h + 256], Fo[:, 64:96])], 16, [n("Fo")], ())
-        return dict(a=lambda: add(-1), b=lambda: add(0), c=lambda: add(1), d=clamp, z=distance, l=lambda: both("zoff", GL),
-                    x=floor_x, k=constants, m=sides, t=turn1, n=pixel, i=lambda: both("off", GI), u=off_image, r=turn2,
-                    s=test, w=write, f=lambda: fetch(0), g=lambda: give(0), F=lambda: fetch(1), G=lambda: give(1),
+        return dict(a=lambda: add(-1), b=lambda: add(0), c=lambda: add(1), d=clamp, z=distance,
+                    l=lambda: both(G, T.W1, "zoff", GL, win1, "G"), x=floor_x, k=clear, m=sides, t=turn1, n=pixel,
+                    i=lambda: both(G, T.W1, "off", GI, win1, "G"), u=off_image, r=turn2, s=test, w=write,
+                    f=lambda: fetch(0), g=lambda: give(0), F=lambda: fetch(1), G=lambda: give(1),
                     e=first_parts, E=store)
 
     def load_w2(k, r, after):
@@ -431,7 +437,7 @@ def build(g, core, T, topo):
             last_setup()
             load_w2(1, (), [arrived[1][2]])
         if p == 1:
-            load_w2(2, (), [arrived[2][2]])
+            load_w2(2, (), [arrived[3][2]])
     return ops, sent[0]
 
 

@@ -12,19 +12,26 @@ MAGIC = 1.5 * (1 << 23)
 COL0 = MAGIC + 128 * 160 - 64 - PAD
 MAGIC8 = 8 * MAGIC
 ORDER = [
-    "z0 z1 K l0 x0 l1 k0 t0 n0 k1 x1 m0 i0 t1 n1 Q u0 r0 s0 W m1 w0 P i1 u1 r1 s1 w1",
-    "a0 b0 k0 c0 d0 a1 z0 l0 b1 c1 x0 d1 k1 m0 t0 n0 z1 u0 i0 r0 l1 s0 x1 m1 t1 w0 n1 i1 u1 r1 s1 w1",
-    "a0 b0 c0 d0 a1 z0 l0 x0 t0 b1 c1 n0 d1 m0 i0 z1 m1 l1 u0 x1 r0 t1 s0 n1 u1 i1 f0 r1 F0 s1 f1 g0 G0 F1 g1 G1 e0 E0 e1 E1",
+    "zero maskz LAB W15 W06 W03 SQz mask4 ones mask8 SPz maskx s10 W05 W08 masky W04 W07 W00 W02 k1 GO2 W14 hi0 W01 mask5 Pf m0f "
+    "m1f GO Lhi0 maskb hi1 dZ s12 mask3 W12 Lhi1 SP1s dC0 lo1 Llo0 f82 Llo1 f83 lo0 SPx f03 mask2 f81 f01 SP1z SPy hc dHi f80 SQ1s "
+    "k8 s11 WZz hcol e2a dLo k14 Lv1 dC1 dC2 mmK Lv0 SQx s11b SQt f02 f00 WK k0c k0 c3 c7 c1c mmX c6 WX dV DXb e21 zero2 c4 c0 SQy "
+    "c2 c5 dW0 D5z SP1c s10b s12b z0 DXa e20 z1 e2b WN l0 x0 l1 j0 t0 RZ j1 n0 p0 x1 Ineg i0 m0 t1 Ib h0 n1 u0 GSEL e2c D5 r0 s0 "
+    "Pr SQ1 Rs i1 h1 m1 w0 p1 H1 u1 r1 s1 w1",
+    "k0 a1 a0 b0 c0 d0 q0 z0 b1 J0 c1 L0 m0 d1 l0 j0 z1 x0 l1 t0 k1 n0 j1 x1 p0 t1 i0 n1 u0 h0 q1 r0 p1 i1 s0 h1 m1 u1 w0 I1 r1 s1 w1",
+    "a0 b0 c0 a1 d0 z0 b1 c1 J0 l0 d1 L0 j0 q0 x0 z1 q1 L1 t0 n0 l1 j1 m0 x1 p0 i0 t1 m1 h0 u0 n1 i1 r0 s0 I1 p1 h1 u1 f0 r1 F0 s1 "
+    "f1 F1 g0 G0 g1 G1 E1",
 ]
-CFG = dict(GL=((32, 22), (32, 36), (32, 40)), GI=((32, 36), (28, 32), (18, 36)), GF=(20, 32), ZS=6, ZG=1, W2=(3, 3, 2))
+CFG = dict(GL=(((32, 32, 64), (22, 22, 64)), ((18, 26, 44), (18, 18, 64)), ((12, 20, 48), (2, 18, 64))),
+           GI=(((32, 32, 64), (32, 32, 58)), ((28, 28, 64), (10, 24, 64)), ((30, 30, 64), (14, 20, 64))), GF=(24, 32),
+           FILL="SVSGVVVVSDDDVDS", ON_S="mask8 c5 c0 c4 c2 SP1s maskz SQz k8 DXa ones k14 f82 f01 SQt f02 DXb k0c", W2=(4, 2, 2))
 b16, f32, f16, i32, u16 = "bfloat16", "float32", "float16", "int32", "uint16"
 
 SCRATCH = {}
 for _d, _w, _names in (
     (b16, WC, "W1 W2"), (b16, HW, "C3"), (i32, 512, "L"), (b16, 512, "Lhi Llo Lv"), (i32, 8, "Pi"),
     (f32, 8, "Pf hc hcol"), (b16, 128, "ones mask GO GO2 Ib Pr Pm Ineg WK WN WX"), (f32, 128, "I17"),
-    (b16, 16, "GSEL GSEL3 GSEL2"), (b16, 192, "D3"), (f16, 256, "LY Ys"), (b16, 320, "D5 P50 P51"),
-    (f32, 96, "Fo0 Fo1"), (f32, 136, "OF0 OF1"), (u16, 64, "zoff0 zoff1 off0 off1 offb0 offb1"), (b16, 1024, "G0 G1 H0 H1"),
+    (b16, 16, "GSEL"), (b16, 32, "GSELF"), (b16, 192, "D3"), (f16, 128, "I16"), (b16, 320, "D5 P50 P51"),
+    (f32, 64, "Fo"), (f32, 136, "OF0 OF1"), (u16, 64, "zoff0 zoff1 off0 off1 offb0 offb1"), (b16, 1024, "G0 G1 H0 H1"),
     (b16, 64, "SQ0 SQ1"), (f32, 192, "O10 O11 O30 O31"), (f32, 384, "DX"),
 ):
     for _n in _names.split():
@@ -32,14 +39,16 @@ for _d, _w, _names in (
 for _n, _s in (("LAB", [16, 16]), ("SEL1", [8, 3]), ("SEL2", [8, 5]), ("SEL3", [8, 3]), ("RZ", [4, 136]), ("WZ", [17, 16]),
                ("SP0", [17, 8]), ("SP1", [17, 8]), ("Rs", [4, 32]), ("LAND", [12, 32])):
     SCRATCH[_n] = ("sbuf", [128] + _s, b16)
+for _n in ("LY", "Ys"):
+    SCRATCH[_n] = ("sbuf", [128, N, 64], f16)
 for _h in "01":
     SCRATCH["psA" + _h] = ("psum", [128, 512], f32)
     SCRATCH["psB" + _h] = ("psum", [128, 64, 8], f32)
     SCRATCH["psC" + _h] = ("psum", [128, 512], f32)
     SCRATCH["psD" + _h] = ("psum", [128, 512], f32)
 
-DMAS = ["dL", "dP", "dC3", "dC0", "dC1", "dHi", "dLo", "dV", "dW0", "dW1", "dW2", "dY0", "dY1"]
-SEMAPHORES = ["sV", "sS", "sP", "sG", "sent"] + ["arr%d_%d" % (k, r) for k in range(6) for r in range(N)] + DMAS
+DMAS = ["dL", "dP", "dC3", "dZ", "dC0", "dC1", "dC2", "dHi", "dLo", "dV", "dW0", "dW1", "dW2", "dY"]
+SEMAPHORES = ["sV", "sS", "sP", "sG", "sent"] + ["arr%d_%d" % (k, r) for k in range(5) for r in range(N)] + DMAS
 
 
 def build(g, core, T, topo):
@@ -93,19 +102,19 @@ def build(g, core, T, topo):
     def sfill(out, c, n, w, r=(), p0=0, p1=128):
         return act(out, T.W1[p0:p1, 0:n], n, ["zero"] + list(r), w, bias=c)
 
-    def mm(lst, cyc, r, b, after=()):
+    def mm(lst, cyc, r, b, after=(), w=()):
         def fn():
             last = None
             for o, l, x, st, sp in lst:
                 last = PE.matmul(o, l, x, st, sp)
             return last
-        return op("P", fn, ("p", cyc), r, (), b, after)
+        return op("P", fn, ("p", cyc), r, w, b, after)
 
-    def iota(out, pat, base, cm, n, w, r=()):
-        return op("G", lambda: g.iota(out, pat, base, cm, allow_small_or_imprecise_dtypes=True), ("g", n), r, w)
+    def iota(out, pat, base, n, w, r=()):
+        return op("G", lambda: g.iota(out, pat, base, 0, allow_small_or_imprecise_dtypes=True), ("g", n), r, w)
 
-    def mark(out, a, pat, c, base, n, w, how=A.not_equal, cm=1):
-        return op("G", lambda: g.affine_select(out, a, pat, how, c, base, cm), ("g", n), ["zero"], w)
+    def mark(out, a, pat, c, base, n, w, r=("zero",), how=A.not_equal, cm=1):
+        return op("G", lambda: g.affine_select(out, a, pat, how, c, base, cm), ("g", n), r, w)
 
     def dma(q, sem, pairs, kb, r, w, after=()):
         e = g.sync if q == "Y" else S
@@ -121,7 +130,9 @@ def build(g, core, T, topo):
             return op("V", lambda: V.tensor_copy(out, src), ("i", 16 * cols), r, w)
         return op("S", lambda: S.activation(out, src, F.Copy), ("i", 16 * cols), r, w)
 
-    peers = [(rank + d) % N for d in (1, 2, 3)]
+    here = topo.chip(core)
+    way = lambda q: 2 if topo.mates(here, topo.chip(T.cores[q])) else 1 if topo.same_plane(here, topo.chip(T.cores[q])) else 0
+    peers = sorted((q for q in range(N) if q != rank), key=way)
     dst = {}
     mask = -1
     for p in peers:
@@ -145,154 +156,136 @@ def build(g, core, T, topo):
     dma("S", "dP", [(T.Pi[0:8, 0:6], T.pose[:])], 0, (), ["Pi"])
     dma("Y", "dC3", [(T.C3[0:2, :], T.cam[0:2, :]), (T.C3[2:3, :], T.cam[15:16, :])], 48, (), ["C3"])
 
-    zn = ["Wz%d" % k for k in range(NP)]
-    piece = lambda k: T.W1[:, PAD + k * PIECE:PAD + (k + 1) * PIECE]
-    ZS, ZG = CFG["ZS"], CFG["ZG"]
-    zero = T.W1[:, 0:PAD]
-    fill(piece(NP - 1), 1.0, PIECE // 2, [zn[-1]])
-    fill(T.mask[:], 0.0, 64, ["maskz"])
-    fill(zero, 0.0, 64, ["zero"])
-    fill(T.LAB[0:8], 0.0, 128, ["LAB"])
-    fill(T.mask[0:8, :], 1.0, 64, ["mask"], ["maskz"])
-    fill(T.mask[KR:KT, :], 4.0, 64, ["mask4"], ["maskz"])
-    by_s = [0, 1, 2] + list(range(8, 5 + ZS))
-    by_g = list(range(3, 3 + ZG))
-    by_v = [k for k in range(NP - 1) if k not in by_s + by_g]
-    for k in by_s:
-        act(piece(k), piece(NP - 1), PIECE, [zn[-1]], [zn[k]])
-    for k in by_g:
-        iota(piece(k), [[0, PIECE]], 1, 0, PIECE, [zn[k]])
-    for k in by_v[:-4]:
-        fill(piece(k), 1.0, PIECE // 2, [zn[k]])
+    once = {}
+    on_s = CFG["ON_S"].split()
 
-    def image_rows(k):
+    def const(nm, out, c, n, two, r=(), p0=0, p1=128):
+        once[nm] = (lambda: sfill(out, c, n, [nm], r, p0, p1)) if nm in on_s else (lambda: fill(out, c, n // 2 if two else n, [nm], r))
+
+    zn = ["W%02d" % k for k in range(NP)]
+    piece = lambda k: T.W1[:, PAD + k * PIECE:PAD + (k + 1) * PIECE]
+    zero = T.W1[:, 0:PAD]
+    by_d = [k for k in range(NP - 1) if CFG["FILL"][k] == "D"]
+    for k, who in enumerate(CFG["FILL"] + "V"):
+        once[zn[k]] = {"V": lambda k=k: fill(piece(k), 1.0, PIECE // 2, [zn[k]]),
+                       "S": lambda k=k: act(piece(k), piece(NP - 1), PIECE, [zn[-1]], [zn[k]]),
+                       "G": lambda k=k: iota(piece(k), [[0, PIECE]], 1, PIECE, [zn[k]]), "D": lambda: None}[who]
+    once["dZ"] = lambda: by_d and dma("Y", "dZ", [(piece(k), piece(NP - 1)) for k in by_d], 128 * len(by_d), [zn[-1]], [zn[k] for k in by_d])
+    once["zero"] = lambda: fill(zero, 0.0, 64, ["zero"])
+    const("zero2", T.W1[:, PAD + HW:WC], 0.0, 128, True)
+    for nm, k, groups in (("dC0", 0, range(8)), ("dC1", 1, range(4)), ("dC2", 1, range(4, 8))):
         c0, c1 = k * HW // 2, (k + 1) * HW // 2
-        dma("Y", "dC%d" % k, [(T.W1[16 * a:16 * a + 3, PAD + c0:PAD + c1], T.C3[0:3, c0:c1]) for a in range(8)], 192,
-            ["C3"] + zn[8 * k:8 * k + 8], ["Wc%d" % k])
-    image_rows(0)
-    s1 = lambda k, row, c, first: mark(T.SEL1[:, :, k], zero[:, 0:8] if first else T.SEL1[:, :, k], [[-16, 8]], c, -row, 8, ["SEL1%d" % k])
-    mark(T.GO[0:8, :], zero[0:8], [[-1, 8], [0, 16]], 1.0, 0, 128, ["GO"])
-    mark(T.mask[:], T.mask[:], [[-2, 8], [0, 8], [-1, 2]], 1.0, -64, 128, ["mask", "mask4"])
-    mark(T.GO2[0:8, :], zero[0:8], [[0, 8], [-1, 8], [0, 2]], 0.25, 0, 128, ["GO2"])
-    mark(T.mask[:], T.mask[:], [[-2, 8], [0, 8], [-1, 2]], 1.0, -80, 128, ["mask"])
-    mark(T.hcol[:, 0:1], zero[:, 0:1], [[0, 1]], 32.0, 0, 1, ["hcol"])
-    for k, (rows, pt, row, c) in enumerate(((5, [[8, 4], [0, 32]], 3, 1.0 / 32768), (4, [[0, 64], [8, 2]], 6, -0.5),
-                                            (3, [[0, 4], [256, 2], [0, 16]], 5, 128.0))):
-        iota(T.mask[0:rows, :], pt, 0, 0, 128, ["mask"])
-        s1(k, row, c, True)
-    iota(T.mask[0:2, :], [[0, 128]], 1, 0, 128, ["mask"])
+        once[nm] = lambda nm=nm, k=k, groups=groups, c0=c0, c1=c1: dma(
+            "Y", nm, [(T.W1[16 * a:16 * a + 3, PAD + c0:PAD + c1], T.C3[0:3, c0:c1]) for a in groups], 24 * len(groups),
+            ["C3"] + zn[8 * k:8 * k + 8] + ([x for x, who in zip(zn, CFG["FILL"]) if who in "SD"] if k else []), [nm])
 
     LAB = T.LAB
-
-    def pieces(k, blk, col, r, between):
+    once["LAB"] = lambda: fill(LAB[0:8], 0.0, 128, ["LAB"])
+    for k, blk, c in ((0, 0, 6), (1, 6, 0)):
         two = T.Pi[0:8, 2 + 2 * k:4 + 2 * k]
-        cpy(LAB[0:8, blk::8, col], two, 2, ["Pi"] + r, ["LABhi%d" % k])
-        between()
-        tt(LAB[0:8, blk::8, col + 1], two, LAB[0:8, blk::8, col], A.subtract, 4, ["Pi", "LABhi%d" % k], ["LABlo%d" % k])
-    pieces(1, 6, 0, ["LAB"], lambda: fill(piece(by_v[-4]), 1.0, PIECE // 2, [zn[by_v[-4]]]))
-    cpy(T.Pf[0:8, 0:2], T.Pi[0:8, 0:2], 2, ["Pi"], ["Pf"])
-    fill(piece(by_v[-3]), 1.0, PIECE // 2, [zn[by_v[-3]]])
-    mm([(T.psB1[:, 0, 0:2], T.GO[0:8, :], LAB[0:8, 6, 0:2], True, False),
-        (T.psB1[:, 0, 0:2], T.GO[0:8, :], LAB[0:8, 6, 1:3], False, True)], 128, ["GO", "LABhi1", "LABlo1"], "B1")
-    act(T.hc[:, 0:2], T.psB1[:, 0, 0:2], 2, (), ["hc"], "B1", scale=1.0 / 4096)
+        once["hi%d" % k] = lambda k=k, blk=blk, c=c, two=two: cpy(LAB[0:8, blk::8, c], two, 2, ["Pi", "LAB"], ["hi%d" % k])
+        once["lo%d" % k] = lambda k=k, blk=blk, c=c, two=two: tt(LAB[0:8, blk::8, c + 1], two, LAB[0:8, blk::8, c], A.subtract, 4,
+                                                                  ["Pi", "hi%d" % k], ["lo%d" % k])
+    once["Pf"] = lambda: [cpy(T.Pf[0:8, 0:2], T.Pi[0:8, 0:2], 2, ["Pi"], ["Pf"])]
+    once["GO"] = lambda: mark(T.GO[0:8, :], zero[0:8], [[-1, 8], [0, 16]], 1.0, 0, 128, ["GO"])
+    once["hc"] = lambda: [
+        mm([(T.psB1[:, 0, 0:2], T.GO[0:8, :], LAB[0:8, 6, 0:2], True, False), (T.psB1[:, 0, 0:2], T.GO[0:8, :], LAB[0:8, 6, 1:3], False, True)],
+           128, ["GO", "hi1", "lo1"], "B1"), act(T.hc[:, 0:2], T.psB1[:, 0, 0:2], 2, (), ["hc"], "B1", scale=1.0 / 4096)]
 
     col = lambda t, k: t[:, 256 * k:256 * k + 256]
-    m32 = [T.psA0[:, 0:256], T.psA1[:, 0:256]]
     for k in (0, 1):
-        cpy(m32[k], col(T.L, k), 256, ["L"], (), "A%d" % k)
-    for k in by_v[-2:]:
-        fill(piece(k), 1.0, PIECE // 2, [zn[k]])
-    image_rows(1)
-    for k in (0, 1):
-        act(col(T.Lhi, k), m32[k], 256, (), ["Lhi%d" % k], "A%d" % k)
-    for k in (0, 1):
-        tt(col(T.Llo, k), m32[k], col(T.Lhi, k), A.subtract, 256, ["Lhi%d" % k], ["Llo%d" % k], "A%d" % k)
-        if k == 0:
-            fill(T.ones[0:8, 0:16], 1.0, 8, ["ones"])
-            fill(T.SP0[:], 0.0, 68, ["SP0z"])
-        act(col(T.Lv, 1 - k), m32[1 - k], 256, ["hc"], ["Lv%d" % (1 - k)], "A%d" % (1 - k), scale=T.hc[:, 0:1], bias=191.5 + 1.0 / 8192)
-    dma("Y", "dHi", [(T.W1[3::16, PAD:PAD + HW], T.Lhi[:])], 128, zn + ["Lhi0", "Lhi1"], ["Whi"])
-    dma("Y", "dLo", [(T.W1[4::16, PAD:PAD + HW], T.Llo[:])], 128, zn + ["Llo0", "Llo1"], ["Wlo"])
-    dma("Y", "dV", [(T.W1[5::16, PAD:PAD + HW], T.Lv[:])], 128, zn + ["Lv0", "Lv1"], ["Wv"])
-    win1 = zn + ["zero", "zero2", "Whi", "Wlo", "Wv", "Wc0", "Wc1"]
+        m32, bk, nm = T["psA%d" % k][:, 0:256], "A%d" % k, "m%df" % k
+        once[nm] = lambda k=k, m32=m32, bk=bk, nm=nm: cpy(m32, col(T.L, k), 256, ["L"], [nm], bk)
+        once["Lhi%d" % k] = lambda k=k, m32=m32, bk=bk, nm=nm: act(col(T.Lhi, k), m32, 256, [nm], ["Lhi%d" % k], bk)
+        once["Llo%d" % k] = lambda k=k, m32=m32, bk=bk: tt(col(T.Llo, k), m32, col(T.Lhi, k), A.subtract, 256, ["Lhi%d" % k], ["Llo%d" % k], bk)
+        once["Lv%d" % k] = lambda k=k, m32=m32, bk=bk, nm=nm: act(col(T.Lv, k), m32, 256, ["hc", nm], ["Lv%d" % k], bk,
+                                                                   scale=T.hc[:, 0:1], bias=191.5 + 1.0 / 8192)
+    for nm, q, row, src in (("dHi", "Y", 3, "Lhi"), ("dLo", "Y", 4, "Llo"), ("dV", "S", 5, "Lv")):
+        once[nm] = lambda nm=nm, q=q, row=row, src=src: dma(q, nm, [(T.W1[row::16, PAD:PAD + HW], T[src][:])], 128,
+                                                             zn + [src + "0", src + "1"], [nm])
+    win1 = zn + ["zero", "zero2", "dHi", "dLo", "dV", "dC0", "dC1", "dC2"]
 
-    lab = ["LABhi0", "LABlo0", "LABhi1", "LABlo1"]
+    const("ones", T.ones[0:8, 0:16], 1.0, 16, True, (), 0, 8)
+    for b0 in (0, 8):
+        for j, (out, n) in enumerate(((LAB[0:8, b0, 1:4:2], 2), (LAB[0:8, b0 + 4, :], 16), (LAB[0:8, b0, 0:5:2], 3), (LAB[0:8, b0 + 5, :], 16))):
+            nm, k, sign = "f%d%d" % (b0, j), (j // 2) ^ (b0 // 8), -1.0 if b0 and j < 2 else 1.0
+            a, num, r = T.ones[0:8, 0:n], T.Pf[0:8, k:k + 1], ["Pf", "ones", "LAB"]
+            once[nm] = (lambda out=out, a=a, n=n, r=r, nm=nm, num=num: act(out, a, n, r, [nm], scale=num)) if nm in on_s else (
+                lambda out=out, a=a, n=n, r=r, nm=nm, num=num, sign=sign: ts(out, a, num, sign, A.mult, A.mult, n, r, [nm]))
+    for nm, blk, k, c in (("k8", 8, 5, -1.5), ("k14", 14, 2, 0.5), ("k0c", 0, 5, -15.5)):
+        const(nm, LAB[0:8, blk, k:k + 1], c, 1, True, ["LAB"], 0, 8)
+    once["GO2"] = lambda: mark(T.GO2[0:8, :], zero[0:8], [[0, 8], [-1, 8], [0, 2]], 0.25, 0, 128, ["GO2"])
+    psK, psX = T.psB0[:, 0:16, :], T.psB1[:, 16:32, :]
+    once["mmK"] = lambda: mm([(psK[0:112], LAB[0:8, 8:15, :], T.GO2[0:8, :], True, True)], 128,
+                             ["hi0", "lo0", "hi1", "lo1", "k8", "k14", "f80", "f81", "f82", "f83", "GO2"], "B0", w=["mmK"])
+    once["mmX"] = lambda: mm([(psX[0:KR], LAB[0:8, 0:6, :], T.GO2[0:8, :], True, True)], 128,
+                             ["hi0", "lo0", "k0c", "f00", "f01", "f02", "f03", "GO2"], "B1", w=["mmX"])
+    const("maskz", T.mask[:], 0.0, 128, True)
+    const("mask8", T.mask[0:8, :], 1.0, 128, True, ["maskz"], 0, 8)
+    const("mask4", T.mask[KR:KT, :], 4.0, 128, True, ["maskz"], KR, KT)
+    rowis = [[-2, 8], [0, 8], [-1, 2]]
+    once["maskx"] = lambda: mark(T.mask[:], T.mask[:], rowis, 1.0, -64, 128, ["maskx"], ["mask8", "mask4"])
+    once["masky"] = lambda: mark(T.mask[:], T.mask[:], rowis, 1.0, -80, 128, ["masky"], ["maskx"])
+    for nm, rows, pt, base, r in (("mask5", 5, [[32, 2], [0, 64]], 0, "masky"), ("maskb", 4, [[0, 64], [8, 2]], 0, "mask5"),
+                                  ("mask3", 3, [[0, 2], [8, 4], [0, 16]], 0, "maskb"), ("mask2", 2, [[0, 128]], 1, "mask3")):
+        once[nm] = lambda nm=nm, rows=rows, pt=pt, base=base, r=r: iota(T.mask[0:rows, :], pt, base, 128, [nm], [r])
+    once["WK"] = lambda: tt(T.WK[0:KT, :], psK[0:KT], T.mask[0:KT, :], A.mult, 128, ["mask2", "mmK"], ["WK"], "B0")
+    once["WX"] = lambda: tt(T.WX[0:KR, :], psX[0:KR], T.mask[0:KR, :], A.mult, 128, ["mask2", "mmX"], ["WX"], "B1")
+    once["WN"] = lambda: [act(T.WN[0:KR, :], T.WK[0:KR, :], 128, ["WK"], ["WNa"], scale=-1.0),
+                          act(T.WN[KR:KT, :], T.WK[KR:KT, :], 128, ["WK"], ["WNb"])]
+    once["WZz"] = lambda: fill(T.WZ[:], 0.0, 136, ["WZz"])
+    wz = ["c0", "c1c", "c2", "c3", "c4", "c5", "c6", "c7"]
+    for c, nm in enumerate(wz):
+        once[nm] = lambda c=c, nm=nm: (act if nm in on_s else cpy)(T.WZ[0:KR, 1::2, 2 * c:2 * c + 2], T.WK[0:KR, 16 * c:16 * c + 16], 16,
+                                                                   ["WK", "WZz"], ["WZ" + nm])
+    wz = ["WZ" + nm for nm in wz]
 
-    def factor(b0, j):
-        out, n = ((LAB[0:8, b0, 1:4], 3), (LAB[0:8, b0 + 4, :], 16), (LAB[0:8, b0, 0:5:4], 2), (LAB[0:8, b0 + 5, :], 16))[j]
-        lab.append("LABf%d_%d" % (b0, j))
-        if b0:
-            ts(out, T.ones[0:8, 0:n], T.Pf[0:8, 1 - j // 2:2 - j // 2], 1.0 if j // 2 else -1.0, A.mult, A.mult, n,
-               ["Pf", "ones", "LAB"], lab[-1:])
-        else:
-            act(out, T.ones[0:8, 0:n], n, ["Pf", "ones", "LAB"], lab[-1:], scale=T.Pf[0:8, j // 2:j // 2 + 1])
-    for blk, k, c in ((8, 5, -1.5), (14, 2, 0.5), (0, 5, -15.5)):
-        lab.append("LABk%d" % blk)
-        sfill(LAB[0:8, blk, k:k + 1], c, 1, lab[-1:], ["LAB"], 0, 8)
-    pieces(0, 0, 6, ["LAB"], lambda: [factor(8, j) for j in range(3)])
-    factor(8, 3)
-    fill(T.SP0[0:8, 1::2, :], 1.0, 32, ["SP0c"], ["SP0z"])
-    for j in range(4):
-        factor(0, j)
-    fill(T.WZ[:], 0.0, 136, ["WZ"])
-    fill(T.SQ0[:], 0.0, 32, ["SQ0z"])
-    fill(T.W1[:, PAD + HW:WC], 0.0, 64, ["zero2"])
-    ps = T.psB0
-    dist = [x for x in lab if not x.startswith("LABf0") and x != "LABk0"]
-    mm([(ps[0:112, 0:16, :], LAB[0:8, 8:15, :], T.GO2[0:8, :], True, True)], 128, dist + ["GO2"], "B0")
-    mm([(T.psB1[0:KR, 16:32, :], LAB[0:8, 0:6, :], T.GO2[0:8, :], True, True)], 128, lab + ["GO2"], "B1")
+    once["SPz"] = lambda: fill(T.SP0[:], 0.0, 68, ["SPz"])
+    once["SP1z"] = lambda: fill(T.SP1[:], 0.0, 68, ["SP1z"])
+    const("SQz", T.SQ0[:], 0.0, 64, True)
+    const("SP1s", T.SP0[0:8, 1::2, :], 1.0, 64, True, ["SPz"], 0, 8)
+    const("SQ1s", T.SQ0[0:8], 1.0, 64, True, ["SQz"], 0, 8)
+    const("SQt", T.SQ0[KR:KT], 1.0, 64, True, ["SQz"], KR, KT)
+    for nm, val, gx, gy in (("SP", T.SP0[:, 1::2, :], [[16, 8], [0, 4], [128, 2]], [[0, 8], [64, 4], [0, 2]]),
+                            ("SQ", T.SQ0[:], [[0, 4], [128, 2], [16, 8]], [[64, 4], [0, 16]])):
+        once[nm + "x"] = lambda nm=nm, val=val, gx=gx: iota(val[0:2], gx, 0, 64, [nm + "x"], [nm + "1s"])
+        once[nm + "y"] = lambda nm=nm, val=val, gy=gy: iota(val[0:1], gy, 0, 64, [nm + "y"], [nm + "x"])
+    once["hcol"] = lambda: mark(T.hcol[:, 0:1], zero[:, 0:1], [[0, 1]], 256.0, -1, 1, ["hcol"])
+    once["SP1c"] = lambda: act(T.SP1[0:8, 1::2, :], T.SP0[0:8, 1::2, :], 64, ["SPy", "SP1z", "hcol"], ["SP1c"], bias=T.hcol[0:8, 0:1])
+    once["SQ1"] = lambda: act(T.SQ1[0:KT, :], T.SQ0[0:KT, :], 64, ["SQy", "SQt", "hcol"], ["SQ1"], bias=T.hcol[0:KT, 0:1])
+    places = dict(SP0=["SPy"], SP1=["SP1c"], SQ0=["SQy", "SQt"], SQ1=["SQ1"])
 
-    def places(nm, val, gx, gy, between):
-        iota(val[0:2], gx, 0, 0, 64, [nm])
-        between()
-        iota(val[0:1], gy, 0, 0, 64, [nm])
-    places("SP0c", T.SP0[:, 1::2, :], [[16, 8], [0, 4], [128, 2]], [[0, 8], [64, 4], [0, 2]], lambda: s1(0, 4, 1.0 / 32768, False))
-    s1(1, 7, 1.0 / 8192, False)
-    s1(2, 6, MAGIC, False)
-    tt(T.WK[0:KT, :], ps[0:KT, 0:16, :], T.mask[0:KT, :], A.mult, 128, ["mask"], ["WK"], "B0")
-    fill(T.SP1[:], 0.0, 68, ["SP1z"])
-    fill(T.SQ0[0:8], 1.0, 32, ["SQ0c"], ["SQ0z"])
-    wz = ["WZ%d" % c for c in range(8)]
-    for c in range(8):
-        (cpy if c % 2 else act)(T.WZ[0:KR, 1::2, 2 * c:2 * c + 2], T.WK[0:KR, 16 * c:16 * c + 16], 16, ["WK", "WZ"], [wz[c]])
-    act(T.SP1[0:8, 1::2, :], T.SP0[0:8, 1::2, :], 64, ["SP0c", "SP1z", "hcol"], ["SP1c"], bias=T.hcol[0:8, 0:1])
-    tt(T.WX[0:KR, :], T.psB1[0:KR, 16:32, :], T.mask[0:KR, :], A.mult, 128, ["mask"], ["WX"], "B1")
-    fill(T.SQ0[KR:KT], 1.0, 32, ["SQ0t"], ["SQ0z"])
-    sfill(T.DX[:, 0::3], 0.0, 128, ["DXa"])
-    sfill(T.DX[:, 2::3], 1.0, 128, ["DXb"])
-    places("SQ0c", T.SQ0[:], [[0, 4], [128, 2], [16, 8]], [[64, 4], [0, 16]],
-           lambda: mark(T.SEL2[:, :, 2:5], zero[:, 0:24], [[16, 8], [0, 3]], 1.0 / 32, 6, 24, ["SEL22"], A.is_gt, -1))
-    iota(T.RZ[:, :, 0:130:2], [[0, 260]], 0, 0, 260, ["RZ"])
-    mark(T.SEL2[:, :, 2:5], T.SEL2[:, :, 2:5], [[16, 8], [-1, 3]], 0.0, 9, 24, ["SEL22"], A.is_gt, -1)
-    mark(T.Ineg[:], zero, [[-8, 2], [-1, 8], [-16, 8]], -32768.0, 0, 128, ["Ineg"])
-    mark(T.SEL2[:, :, 2:4], T.SEL2[:, :, 2:4], [[-16, 8], [-1, 2]], 1.0 / 2048, 0, 16, ["SEL22"])
+    for k, (r0, c0, r1, c1) in enumerate(((3, 1.0 / 32768, 4, 1.0 / 32768), (6, -0.5, 7, 1.0 / 8192), (5, 128.0, 6, MAGIC))):
+        nm, out = "s1%d" % k, T.SEL1[:, :, k]
+        once[nm] = lambda nm=nm, out=out, r0=r0, c0=c0: mark(out, zero[:, 0:8], [[-16, 8]], c0, -r0, 8, [nm])
+        once[nm + "b"] = lambda nm=nm, out=out, r1=r1, c1=c1: mark(out, out, [[-16, 8]], c1, -r1, 8, [nm + "b"], [nm])
+    three = T.SEL2[:, :, 2:5]
+    once["e2a"] = lambda: mark(three, zero[:, 0:24], [[16, 8], [0, 3]], 1.0 / 32, 6, 24, ["e2a"], ["zero"], A.is_gt, -1)
+    once["e2b"] = lambda: mark(three, three, [[16, 8], [-1, 3]], 0.0, 9, 24, ["e2b"], ["e2a"], A.is_gt, -1)
+    once["e2c"] = lambda: mark(T.SEL2[:, :, 2:4], T.SEL2[:, :, 2:4], [[-16, 8], [-1, 2]], 1.0 / 2048, 0, 16, ["e2c"], ["e2b"])
     for k, c in ((0, 32.0), (1, -32.0)):
-        mark(T.SEL2[:, :, k], zero[:, 0:8], [[-16, 8]], c, -2, 8, ["SEL2%d" % k])
-    iota(T.D5[:], [[0, 320]], 0, 0, 320, ["D5z"])
-    mark(T.Ib[:], zero, [[-1, 128]], 1.0, 0, 128, ["Ib"])
-    iota(T.D5[:, 0::5], [[0, 64]], 1, 0, 64, ["D5"], ["D5z"])
-    iota(T.Rs[:], [[0, 128]], 0, 0, 128, ["Rs"])
-    sel2 = ["SEL20", "SEL21", "SEL22"]
-
-    def for_sides():
-        act(T.WN[0:KR, :], T.WK[0:KR, :], 128, ["WK"], ["WNa"], scale=-1.0)
-        act(T.WN[KR:KT, :], T.WK[KR:KT, :], 128, ["WK"], ["WNb"])
-
-    def second_half():
-        act(T.SQ1[0:KT, :], T.SQ0[0:KT, :], 64, ["SQ0c", "SQ0t", "hcol"], ["SQ1z", "SQ1c", "SQ1t"], bias=T.hcol[0:KT, 0:1])
-
-    def for_write():
-        mm([(T.psA0[:, 0:16], T.mask[64:80, :], T.Ib[64:80, 64:80], True, True)], 64, ["mask", "Ib"], "A0")
-        act(T.GSEL[:], T.psA0[:, 0:16], 16, (), ["GSEL"], "A0")
-        act(T.GSEL3[:], T.psA0[:, 0:16], 16, (), ["GSEL3"], "A0", scale=-3.0)
-        act(T.GSEL2[:], T.psA0[:, 0:16], 16, (), ["GSEL2"], "A0", scale=-2.0)
-    once = dict(K=for_sides, Q=second_half, W=for_write,
-                P=lambda: mark(T.Pr[0:64, 0:64], zero[0:64, 0:64], [[-1, 8], [-8, 8]], 1.0, 0, 64, ["Pr"]))
+        once["e2%d" % k] = lambda k=k, c=c: mark(T.SEL2[:, :, k], zero[:, 0:8], [[-16, 8]], c, -2, 8, ["e2%d" % k])
+    sel2 = ["e20", "e21", "e2c"]
+    once["Ineg"] = lambda: mark(T.Ineg[:], zero, [[-8, 2], [-1, 8], [-16, 8]], -32768.0, 0, 128, ["Ineg"])
+    once["Ib"] = lambda: mark(T.Ib[:], zero, [[-1, 128]], 1.0, 0, 128, ["Ib"])
+    once["Pr"] = lambda: mark(T.Pr[0:64, 0:64], zero[0:64, 0:64], [[-1, 8], [-8, 8]], 1.0, 0, 64, ["Pr"])
+    const("DXa", T.DX[:, 0::3], 0.0, 128, False)
+    const("DXb", T.DX[:, 2::3], 1.0, 128, False)
+    once["RZ"] = lambda: iota(T.RZ[:, :, 0:130:2], [[0, 260]], 0, 260, ["RZ"])
+    once["D5z"] = lambda: fill(T.D5[:], 0.0, 160, ["D5z"])
+    once["D5"] = lambda: iota(T.D5[:, 0::5], [[0, 64]], 1, 64, ["D5"], ["D5z"])
+    once["Rs"] = lambda: iota(T.Rs[:], [[0, 128]], 0, 128, ["Rs"])
+    once["GSEL"] = lambda: [
+        mm([(T.psA0[:, 256:272], T.mask[64:80, :], T.Ib[64:80, 64:80], True, True)], 64, ["mask2", "Ib"], "A0"),
+        act(T.GSEL[:], T.psA0[:, 256:272], 16, (), ["GSEL"], "A0"),
+        act(T.GSELF[:, 0:16], T.psA0[:, 256:272], 16, (), ["GSEL3"], "A0", scale=-3.0),
+        act(T.GSELF[:, 16:32], T.psA0[:, 256:272], 16, (), ["GSEL2"], "A0", scale=-2.0)]
 
     def last_setup():
         fill(T.W2[:, 0:PAD], 0.0, 64, ["W2a"])
         fill(T.W2[:, PAD + HW:WC], 0.0, 64, ["W2b"])
         fill(T.D3[:], 0.0, 96, ["D3z"])
+        cpy(T.I16[:], T.Ib[:], 64, ["Ib"], ["I16"])
         mark(T.Pm[:], zero, [[-1, 16], [-16, 8]], 1.0, 0, 128, ["Pm"])
         act(T.I17[:], T.Ineg[:], 128, ["Ineg"], ["I17"], scale=-1.0 / (1 << 32))
         act(T.SEL3[:, :, 0:2], T.SEL2[:, :, 0:2], 16, sel2, ["SEL3a"])
@@ -302,22 +295,21 @@ def build(g, core, T, topo):
             sfill(T["OF%d" % h][:, 0:130:2], 0.0, 65, ["OFz%d" % h])
 
     arrived = {}
-    senders = peers[::-1]
+    senders = peers
 
     def half_pass(p, h):
         n = lambda s: "%s%d" % (s, h)
         B = lambda s: T[n(s)]
         pA, pB, pC, pD = B("psA"), B("psB"), B("psC"), B("psD")
         bA, bB, bC, bD = n("A"), n("B"), n("C"), n("D")
-        G, SP, SQ, O1, P5, H, OF, Fo = B("G"), B("SP"), B("SQ"), B("O1"), B("P5"), B("H"), B("OF"), B("Fo")
-        sp = [n("SP") + x for x in ("zcs" if p else "zc")]
-        sq = [n("SQ") + x for x in ("zcts" if p else "zct")]
+        G, SP, SQ, O1, P5, H, OF = B("G"), B("SP"), B("SQ"), B("O1"), B("P5"), B("H"), B("OF")
+        sp = places[n("SP")] + ([n("SPs")] if p else [])
+        sq = places[n("SQ")] + ([n("SQs")] if p else [])
         GL, GI = CFG["GL"][p][h], CFG["GI"][p][h]
         ns = 3 if p == 2 else 5
         slot = lambda k: pD[:, k:64 * ns:ns]
         R1, R2 = T.RZ[:, 2 * h, :], T.RZ[:, 2 * h + 1, :]
         s = 2 * p + h
-        part = lambda t, q: t[:, 32 * (N * h + q):32 * (N * h + q) + 32]
         mine = rank // 2
 
         def add(j):
@@ -327,21 +319,25 @@ def build(g, core, T, topo):
 
         def clamp():
             add(2)
-            ts(SP[64:KR, 1::2, :], pB[64:KR, 16:24, :], -31.0, 31.0, A.max, A.min, 64, (), [n("SP") + "s"], bB)
-            ts(SQ[64:KR, :], pA[64:KR, 0:64], -31.0, 31.0, A.max, A.min, 64, (), [n("SQ") + "s"], bA)
+            ts(SP[64:KR, 1::2, :], pB[64:KR, 16:24, :], -31.0, 31.0, A.max, A.min, 64, (), [n("SPs")], bB)
+
+        def clamp2():
+            ts(SQ[64:KR, :], pA[64:KR, 0:64], -31.0, 31.0, A.max, A.min, 64, (), [n("SQs")], bA)
 
         def distance():
             mm([(pB[:, 0:8, 4 * b:4 * b + 4], T.WZ[0:KR, 1 - e:17 - e, b::2], SP[0:KR, 1::2, e::2], e == 0, e == 1)
-                for b in (0, 1) for e in (0, 1)], 256, sp + wz, bB)
+                for b in (0, 1) for e in (0, 1)], 256, sp + wz + ["hc"], bB, w=[] if p else [n("Gfree")])
             ts(B("zoff")[:], pB[:, 0:8, :], float(PAD), float(WC - 1), A.add, A.min, 64, (), [n("zoff")], bB)
 
-        def both(out, win, offs, k, r, w):
-            gather("V", out[:, 0:16 * k], win, B(offs)[:, 0:k], k, r + [n(offs)], [n(w + "a")])
-            gather("S", out[:, 16 * k:1024], win, B(offs)[:, k:64], 64 - k, r + [n(offs)], [n(w + "b")])
+        def look(offs, cuts, j):
+            a, b = ((0,) + tuple(cuts) + (64,))[j:j + 2]
+            if b > a:
+                gather("VVSS"[j], G[:, 16 * a:16 * b], T.W1, B(offs)[:, a:b], b - a, win1 + [n(offs), n("Gfree")], [n("G%d_" % j)])
+        gs = lambda cuts: [n("G%d_" % j) for j, (a, b) in enumerate(zip((0,) + tuple(cuts), tuple(cuts) + (64,))) if b > a]
 
         def floor_x():
             psX = pB[:, 8:16, :]
-            mm([(psX, SP[0:KR, 1 - b:17 - b, :], T.WX[0:KR, b::2], b == 0, b == 1) for b in (0, 1)], 128, sp + ["WX"], bB)
+            mm([(psX, SP[0:KR, 1 - b:17 - b, :], T.WX[0:KR, b::2], b == 0, b == 1) for b in (0, 1)], 128, sp + ["WX", "WK"], bB)
             ts(T.DX[:, 192 * h + 1:192 * h + 192:3], psX, MAGIC8, -MAGIC8, A.add, A.add, 64, (), [n("x")], bB)
 
         def sides():
@@ -353,11 +349,13 @@ def build(g, core, T, topo):
 
         def turn1():
             mm([(pC[:, 24 * c:24 * c + 24], G[:, c::8], T.SEL1[:], True, True) for c in range(8)], 512,
-               [n("Ga"), n("Gb"), "SEL10", "SEL11", "SEL12"], bC)
+               gs(GL) + ["s10b", "s11b", "s12b"], bC, w=[n("Gfree")])
 
         def pixel():
             scan(O1[:], T.DX[:, 192 * h:192 * h + 192], pC[:, 0:192], A.mult, A.add, 192, [n("x"), "DXa", "DXb"], [n("O1")], bC)
             ts(B("off")[:], O1[:, 2::3], -COL0, float(WC - 1), A.add, A.min, 64, [n("O1")], [n("off")])
+
+        def beyond():
             act(R1[:, 1:129:2], O1[:, 1::3], 64, [n("O1"), "RZ"], [n("R1")], scale=8192.0, bias=-63.5 * 8192, f=F.Relu)
             act(R2[:, 1:129:2], O1[:, 1::3], 64, [n("O1"), "RZ"], [n("R2")], scale=-8192.0, bias=-64.5 * 8192, f=F.Relu)
             if p == 2:
@@ -372,7 +370,7 @@ def build(g, core, T, topo):
         def turn2():
             sel, seln = (T.SEL3, ["SEL3a", "SEL3b"]) if p == 2 else (T.SEL2, sel2)
             mm([(pD[:, 8 * ns * e:8 * ns * (e + 1)], G[:, e::8], sel[:], False, e == 7) for e in range(8)], 512,
-               [n("Ga"), n("Gb")] + seln, bD)
+               gs(GI) + seln, bD, w=[n("Gfree")])
 
         def test():
             if p < 2:
@@ -382,9 +380,8 @@ def build(g, core, T, topo):
                 ts(B("offb")[:], B("O3")[:, 2::3], float(1 << 17), float(WC - 1), A.mult, A.min, 64, [n("O3")], [n("offb")])
 
         def write():
-            mm([(pA[0:64, 128:144], P5[:, 4::5], T.GSEL3[:], True, False), (pA[0:64, 128:144], P5[:, 2::5], T.GSEL[:], False, True),
-                (pA[0:64, 144:160], P5[:, 4::5], T.GSEL2[:], True, False), (pA[0:64, 144:160], P5[:, 3::5], T.GSEL[:], False, True)],
-               256, [n("P5"), "GSEL", "GSEL3", "GSEL2"], bA)
+            mm([(pA[0:64, 128:160], P5[:, 4::5], T.GSELF[:], True, False), (pA[0:64, 128:144], P5[:, 2::5], T.GSEL[:], False, False),
+                (pA[0:64, 144:160], P5[:, 3::5], T.GSEL[:], False, True)], 192, [n("P5"), "GSEL", "GSEL3", "GSEL2"], bA)
             act(T.Rs[0:64, s, :], pA[0:64, 128:160], 32, ["Rs"], ["Rs%d" % s], bA, scale=2048.0)
             k = send([(peers, mask, "arr%d_%d" % (s, rank), T.Rs[:, s, :], [T.LAND[:, 3 * s + j, :] for j in range(3)])], ["Rs", "Rs%d" % s])
             arrived[s] = [op("-", None, ("c", j + 1), after=[k], sem="arr%d_%d" % (s, q), val=neng) for j, q in enumerate(senders)]
@@ -400,39 +397,39 @@ def build(g, core, T, topo):
             ps, bk = (pA, bA) if j else (pC, bC)
             mm([(ps[:, 256 + b:320:2], T.Pm[:], H[:, 512 * pair + 2 * a + b:512 * pair + 512:16], a == 0, a == 7)
                 for b in (0, 1) for a in range(8)], 1024, [n("H%dV" % j), n("H%dS" % j), "Pm"], bk)
-            y0 = 32 * (N * h + 2 * pair)
-            cpy(T.Ys[:, y0:y0 + 64], ps[:, 256:320], 64, (), [n("Ys%d_" % j)], bk)
+            cpy(T.Ys[:, 2 * pair:2 * pair + 2, 32 * h:32 * h + 32], ps[:, 256:320], 64, (), [n("Ys%d_" % j)], bk)
+            if h == 0:
+                return
             to = [q for q in (2 * pair, 2 * pair + 1) if q != rank]
             ms = halves if len(to) == 2 else [mask]
-            k = send([([q], m, "arr%d_%d" % (s, rank), part(T.Ys, q), [part(T.LY, rank)]) for q, m in zip(to, ms)], [n("Ys%d_" % j)])
-            arrived.setdefault(s, []).extend(
-                (q, op("-", None, ("c", len(to)), after=[k], sem="arr%d_%d" % (s, q), val=neng // len(to))) for q in to)
-
-        def first_parts():
-            arr = arrived[s]
-            tt(Fo[:, 0:32], part(T.LY, arr[0][0]), part(T.LY, arr[1][0]), A.add, 64, (), [n("Fa")], None, [arr[0][1], arr[1][1]])
-            tt(Fo[:, 32:64], Fo[:, 0:32], part(T.Ys, rank), A.add, 64, [n("Fa"), n("Ys1_")], [n("Fb")])
+            k = send([([q], m, "arr4_%d" % rank, T.Ys[:, q, :], [T.LY[:, rank, :]]) for q, m in zip(to, ms)], ["Ys%d_0" % j, "Ys%d_1" % j])
+            arrived.setdefault(4, []).extend(
+                (q, op("-", None, ("c", len(to)), after=[k], sem="arr4_%d" % q, val=neng // len(to))) for q in to)
 
         def store():
-            arr = arrived[s]
-            tt(Fo[:, 64:96], Fo[:, 32:64], part(T.LY, arr[2][0]), A.add, 64, [n("Fb")], [n("Fo")], None, [arr[2][1]])
-            dma("Y", n("dY"), [(T.y[:, 256 * h:256 * h + 256], Fo[:, 64:96])], 16, [n("Fo")], ())
+            mm([(pB[:, 32:40, :], T.I16[:], T.Ys[:, rank, :], True, False)], 64, ["I16", "Ys1_0", "Ys1_1"], bB)
+            for j, (q, k) in enumerate(arrived[4][:2]):
+                mm([(pB[:, 32:40, :], T.I16[:], T.LY[:, q, :], False, j == 1)], 64, ["I16"], bB, [k])
+            q, k = arrived[4][2]
+            tt(T.Fo[:], pB[:, 32:40, :], T.LY[:, q, :], A.add, 64, (), ["Fo"], bB, [k])
+            dma("Y", "dY", [(T.y[:], T.Fo[:])], 16, ["Fo"], ())
         return dict(a=lambda: add(-1), b=lambda: add(0), c=lambda: add(1), d=clamp, z=distance,
-                    l=lambda: both(G, T.W1, "zoff", GL, win1, "G"), x=floor_x, k=clear, m=sides, t=turn1, n=pixel,
-                    i=lambda: both(G, T.W1, "off", GI, win1, "G"), u=off_image, r=turn2, s=test, w=write,
-                    f=lambda: fetch(0), g=lambda: give(0), F=lambda: fetch(1), G=lambda: give(1),
-                    e=first_parts, E=store)
+                    l=lambda: look("zoff", GL, 0), L=lambda: look("zoff", GL, 1), j=lambda: look("zoff", GL, 2),
+                    J=lambda: look("zoff", GL, 3), x=floor_x, k=clear, m=sides, t=turn1, n=pixel, q=clamp2, p=beyond,
+                    i=lambda: look("off", GI, 0), I=lambda: look("off", GI, 1), h=lambda: look("off", GI, 2),
+                    H=lambda: look("off", GI, 3), u=off_image, r=turn2, s=test, w=write,
+                    f=lambda: fetch(0), g=lambda: give(0), F=lambda: fetch(1), G=lambda: give(1), E=store)
 
     def load_w2(k, r, after):
         a0 = sum(CFG["W2"][:k])
         dma("Y", "dW%d" % k, [(T.W2[16 * a:16 * a + 16, PAD:PAD + HW], T.cam[:]) for a in range(a0, a0 + CFG["W2"][k])],
             256 * CFG["W2"][k], r, ["W2%d" % k], after)
 
-    load_w2(0, win1, ())
-    for p in range(3):
+    once["dW0"] = lambda: load_w2(0, win1, ())
+    for p in range(len(ORDER)):
         steps = [half_pass(p, 0), half_pass(p, 1)]
         for name in ORDER[p].split():
-            (steps[int(name[1])][name[0]] if name[1:] else once[name])()
+            (once[name] if p == 0 and name in once else steps[int(name[1])][name[0]])()
         if p == 0:
             last_setup()
             load_w2(1, (), [arrived[1][2]])

from concourse.bass import DstId, RemoteDMATransfer
from concourse.mybir import AluOpType as A, ActivationFunctionType as F

N = 4
HW = 8192
PAD = 128
WC = HW + 2 * PAD
NP = 16
PIECE = HW // NP
KR, KT = 96, 100
MAGIC = 1.5 * (1 << 23)
COL0 = MAGIC + 128 * 160 - 64 - PAD
MAGIC8 = 8 * MAGIC
ORDER = [
    "zero maskz LAB W15 W06 W03 SQz mask4 ones mask8 SPz maskx s10 W05 W08 masky W04 W07 W00 W02 k1 GO2 W14 hi0 W01 mask5 Pf m0f "
    "m1f GO Lhi0 maskb hi1 dZ s12 mask3 W12 Lhi1 SP1s dC0 lo1 Llo0 f82 Llo1 f83 lo0 SPx f03 mask2 f81 f01 SP1z SPy hc dHi f80 SQ1s "
    "k8 s11 WZz hcol e2a dLo k14 Lv1 dC1 dC2 mmK Lv0 SQx s11b SQt f02 f00 WK k0c k0 c3 c7 c1c mmX c6 WX dV DXb e21 zero2 c4 c0 SQy "
    "c2 c5 dW0 D5z SP1c s10b s12b z0 DXa e20 z1 e2b WN l0 x0 l1 j0 t0 RZ j1 n0 p0 x1 Ineg i0 m0 t1 Ib h0 n1 u0 GSEL e2c D5 r0 s0 "
    "Pr SQ1 Rs i1 h1 m1 w0 p1 H1 u1 r1 s1 w1",
    "k0 a1 a0 b0 c0 d0 q0 z0 b1 J0 c1 L0 m0 d1 l0 j0 z1 x0 l1 t0 k1 n0 j1 x1 p0 t1 i0 n1 u0 h0 q1 r0 p1 i1 s0 h1 m1 u1 w0 I1 r1 s1 w1",
    "a0 b0 c0 a1 d0 z0 b1 c1 J0 l0 d1 L0 j0 q0 x0 z1 q1 L1 t0 n0 l1 j1 m0 x1 p0 i0 t1 m1 h0 u0 n1 i1 r0 s0 I1 p1 h1 u1 f0 r1 F0 s1 "
    "f1 F1 g0 G0 g1 G1 E1",
]
CFG = dict(GL=(((32, 32, 64), (22, 22, 64)), ((18, 26, 44), (18, 18, 64)), ((12, 20, 48), (2, 18, 64))),
           GI=(((32, 32, 64), (32, 32, 58)), ((28, 28, 64), (10, 24, 64)), ((30, 30, 64), (14, 20, 64))), GF=(24, 32),
           FILL="SVSGVVVVSDDDVDS", ON_S="mask8 c5 c0 c4 c2 SP1s maskz SQz k8 DXa ones k14 f82 f01 SQt f02 DXb k0c", W2=(4, 2, 2))
b16, f32, f16, i32, u16 = "bfloat16", "float32", "float16", "int32", "uint16"

SCRATCH = {}
for _d, _w, _names in (
    (b16, WC, "W1 W2"), (b16, HW, "C3"), (i32, 512, "L"), (b16, 512, "Lhi Llo Lv"), (i32, 8, "Pi"),
    (f32, 8, "Pf hc hcol"), (b16, 128, "ones mask GO GO2 Ib Pr Pm Ineg WK WN WX"), (f32, 128, "I17"),
    (b16, 16, "GSEL"), (b16, 32, "GSELF"), (b16, 192, "D3"), (f16, 128, "I16"), (b16, 320, "D5 P50 P51"),
    (f32, 64, "Fo"), (f32, 136, "OF0 OF1"), (u16, 64, "zoff0 zoff1 off0 off1 offb0 offb1"), (b16, 1024, "G0 G1 H0 H1"),
    (b16, 64, "SQ0 SQ1"), (f32, 192, "O10 O11 O30 O31"), (f32, 384, "DX"),
):
    for _n in _names.split():
        SCRATCH[_n] = ("sbuf", [128, _w], _d)
for _n, _s in (("LAB", [16, 16]), ("SEL1", [8, 3]), ("SEL2", [8, 5]), ("SEL3", [8, 3]), ("RZ", [4, 136]), ("WZ", [17, 16]),
               ("SP0", [17, 8]), ("SP1", [17, 8]), ("Rs", [4, 32]), ("LAND", [12, 32])):
    SCRATCH[_n] = ("sbuf", [128] + _s, b16)
for _n in ("LY", "Ys"):
    SCRATCH[_n] = ("sbuf", [128, N, 64], f16)
for _h in "01":
    SCRATCH["psA" + _h] = ("psum", [128, 512], f32)
    SCRATCH["psB" + _h] = ("psum", [128, 64, 8], f32)
    SCRATCH["psC" + _h] = ("psum", [128, 512], f32)
    SCRATCH["psD" + _h] = ("psum", [128, 512], f32)

DMAS = ["dL", "dP", "dC3", "dZ", "dC0", "dC1", "dC2", "dHi", "dLo", "dV", "dW0", "dW1", "dW2", "dY"]
SEMAPHORES = ["sV", "sS", "sP", "sG", "sent"] + ["arr%d_%d" % (k, r) for k in range(5) for r in range(N)] + DMAS


def build(g, core, T, topo):
    rank = T.rank_of(core)
    ops, res, banks = [], {}, {}
    V, S, PE = g.vector, g.scalar, g.tensor

    def op(eng, fn, cost, r=(), w=(), b=None, after=(), sem=None, val=0):
        k = len(ops)
        deps = set(after)
        for x in r:
            deps.add(res[x][0])
        for x in w:
            if x in res:
                deps.add(res[x][0])
                deps.update(res[x][1])
        for x in r:
            res[x][1].append(k)
        for x in w:
            res[x] = [k, []]
        if b is not None:
            st = banks.setdefault(b, [None, [], []])
            if st[0] == eng:
                deps.update(st[2])
                st[1].append(k)
            else:
                deps.update(st[1])
                banks[b] = [eng, [k], st[1]]
        deps.discard(k)
        ops.append(dict(eng=eng, fn=fn, cost=cost, deps=deps, sem=sem, val=val, tag=(list(w) + [b])[0]))
        return k

    def ts(out, in0, s1, s2, o0, o1, n, r, w, b=None):
        return op("V", lambda: V.tensor_scalar(out, in0, s1, s2, o0, o1), ("v", n), r, w, b)

    def tt(out, a, c, o, n, r, w, b=None, after=()):
        return op("V", lambda: V.tensor_tensor(out, a, c, o), ("v", n), r, w, b, after)

    def cpy(out, a, n, r, w, b=None):
        return op("V", lambda: V.tensor_copy(out, a), ("v", n), r, w, b)

    def fill(ap, c, n, w, r=()):
        return op("V", lambda: V.memset(ap, c), ("v", n), r, w)

    def scan(out, d0, d1, o0, o1, n, r, w, b):
        return op("V", lambda: V.tensor_tensor_scan(out, d0, d1, 0.0, o0, o1), ("v", n), r, w, b)

    def act(out, a, n, r, w, b=None, bias=0.0, scale=1.0, f=F.Identity):
        return op("S", lambda: S.activation(out, a, f, bias=bias, scale=scale), ("v", n), r, w, b)

    def sfill(out, c, n, w, r=(), p0=0, p1=128):
        return act(out, T.W1[p0:p1, 0:n], n, ["zero"] + list(r), w, bias=c)

    def mm(lst, cyc, r, b, after=(), w=()):
        def fn():
            last = None
            for o, l, x, st, sp in lst:
                last = PE.matmul(o, l, x, st, sp)
            return last
        return op("P", fn, ("p", cyc), r, w, b, after)

    def iota(out, pat, base, n, w, r=()):
        return op("G", lambda: g.iota(out, pat, base, 0, allow_small_or_imprecise_dtypes=True), ("g", n), r, w)

    def mark(out, a, pat, c, base, n, w, r=("zero",), how=A.not_equal, cm=1):
        return op("G", lambda: g.affine_select(out, a, pat, how, c, base, cm), ("g", n), r, w)

    def dma(q, sem, pairs, kb, r, w, after=()):
        e = g.sync if q == "Y" else S

        def fn():
            for o, i in pairs:
                e.dma_start(o, i).then_inc(T.sem[sem], 16)
        return op(q, fn, ("d", len(pairs), kb), r, w, None, after, sem, 16 * len(pairs))

    def gather(eng, out, win, offs, cols, r, w):
        src = win[:, 0:WC].indirect(offs)
        if eng == "V":
            return op("V", lambda: V.tensor_copy(out, src), ("i", 16 * cols), r, w)
        return op("S", lambda: S.activation(out, src, F.Copy), ("i", 16 * cols), r, w)

    here = topo.chip(core)
    way = lambda q: 2 if topo.mates(here, topo.chip(T.cores[q])) else 1 if topo.same_plane(here, topo.chip(T.cores[q])) else 0
    peers = sorted((q for q in range(N) if q != rank), key=way)
    dst = {}
    mask = -1
    for p in peers:
        rid, pid, _se = topo.addr(T.cores[p])
        dst[p] = DstId(rid=rid, pnc=pid)
        mask &= topo.mask(core, T.cores[p])
    engs = [e for e in topo.engines(core, T.cores[peers[0]]) if mask >> e & 1]
    neng = len(engs)
    halves = [sum(1 << e for e in engs[:neng // 2]), sum(1 << e for e in engs[neng // 2:])]
    sent = [0]

    def send(transfers, r):
        def fn():
            g.remote_dma_fused([RemoteDMATransfer(dst_ids=[dst[q] for q in to], dma_engine_mask=m, remote_sem=T.sem[sem], srcs=[src],
                                                  dsts=land, alu_op=0) for to, m, sem, src, land in transfers],
                               local_sem=T.sem.sent)
        sent[0] += neng
        return op("G", fn, ("r",), r, (), sem="none")

    dma("Y", "dL", [(T.L[:], T.lens[:])], 256, (), ["L"])
    dma("S", "dP", [(T.Pi[0:8, 0:6], T.pose[:])], 0, (), ["Pi"])
    dma("Y", "dC3", [(T.C3[0:2, :], T.cam[0:2, :]), (T.C3[2:3, :], T.cam[15:16, :])], 48, (), ["C3"])

    once = {}
    on_s = CFG["ON_S"].split()

    def const(nm, out, c, n, two, r=(), p0=0, p1=128):
        once[nm] = (lambda: sfill(out, c, n, [nm], r, p0, p1)) if nm in on_s else (lambda: fill(out, c, n // 2 if two else n, [nm], r))

    zn = ["W%02d" % k for k in range(NP)]
    piece = lambda k: T.W1[:, PAD + k * PIECE:PAD + (k + 1) * PIECE]
    zero = T.W1[:, 0:PAD]
    by_d = [k for k in range(NP - 1) if CFG["FILL"][k] == "D"]
    for k, who in enumerate(CFG["FILL"] + "V"):
        once[zn[k]] = {"V": lambda k=k: fill(piece(k), 1.0, PIECE // 2, [zn[k]]),
                       "S": lambda k=k: act(piece(k), piece(NP - 1), PIECE, [zn[-1]], [zn[k]]),
                       "G": lambda k=k: iota(piece(k), [[0, PIECE]], 1, PIECE, [zn[k]]), "D": lambda: None}[who]
    once["dZ"] = lambda: by_d and dma("Y", "dZ", [(piece(k), piece(NP - 1)) for k in by_d], 128 * len(by_d), [zn[-1]], [zn[k] for k in by_d])
    once["zero"] = lambda: fill(zero, 0.0, 64, ["zero"])
    const("zero2", T.W1[:, PAD + HW:WC], 0.0, 128, True)
    for nm, k, groups in (("dC0", 0, range(8)), ("dC1", 1, range(4)), ("dC2", 1, range(4, 8))):
        c0, c1 = k * HW // 2, (k + 1) * HW // 2
        once[nm] = lambda nm=nm, k=k, groups=groups, c0=c0, c1=c1: dma(
            "Y", nm, [(T.W1[16 * a:16 * a + 3, PAD + c0:PAD + c1], T.C3[0:3, c0:c1]) for a in groups], 24 * len(groups),
            ["C3"] + zn[8 * k:8 * k + 8] + ([x for x, who in zip(zn, CFG["FILL"]) if who in "SD"] if k else []), [nm])

    LAB = T.LAB
    once["LAB"] = lambda: fill(LAB[0:8], 0.0, 128, ["LAB"])
    for k, blk, c in ((0, 0, 6), (1, 6, 0)):
        two = T.Pi[0:8, 2 + 2 * k:4 + 2 * k]
        once["hi%d" % k] = lambda k=k, blk=blk, c=c, two=two: cpy(LAB[0:8, blk::8, c], two, 2, ["Pi", "LAB"], ["hi%d" % k])
        once["lo%d" % k] = lambda k=k, blk=blk, c=c, two=two: tt(LAB[0:8, blk::8, c + 1], two, LAB[0:8, blk::8, c], A.subtract, 4,
                                                                  ["Pi", "hi%d" % k], ["lo%d" % k])
    once["Pf"] = lambda: [cpy(T.Pf[0:8, 0:2], T.Pi[0:8, 0:2], 2, ["Pi"], ["Pf"])]
    once["GO"] = lambda: mark(T.GO[0:8, :], zero[0:8], [[-1, 8], [0, 16]], 1.0, 0, 128, ["GO"])
    once["hc"] = lambda: [
        mm([(T.psB1[:, 0, 0:2], T.GO[0:8, :], LAB[0:8, 6, 0:2], True, False), (T.psB1[:, 0, 0:2], T.GO[0:8, :], LAB[0:8, 6, 1:3], False, True)],
           128, ["GO", "hi1", "lo1"], "B1"), act(T.hc[:, 0:2], T.psB1[:, 0, 0:2], 2, (), ["hc"], "B1", scale=1.0 / 4096)]

    col = lambda t, k: t[:, 256 * k:256 * k + 256]
    for k in (0, 1):
        m32, bk, nm = T["psA%d" % k][:, 0:256], "A%d" % k, "m%df" % k
        once[nm] = lambda k=k, m32=m32, bk=bk, nm=nm: cpy(m32, col(T.L, k), 256, ["L"], [nm], bk)
        once["Lhi%d" % k] = lambda k=k, m32=m32, bk=bk, nm=nm: act(col(T.Lhi, k), m32, 256, [nm], ["Lhi%d" % k], bk)
        once["Llo%d" % k] = lambda k=k, m32=m32, bk=bk: tt(col(T.Llo, k), m32, col(T.Lhi, k), A.subtract, 256, ["Lhi%d" % k], ["Llo%d" % k], bk)
        once["Lv%d" % k] = lambda k=k, m32=m32, bk=bk, nm=nm: act(col(T.Lv, k), m32, 256, ["hc", nm], ["Lv%d" % k], bk,
                                                                   scale=T.hc[:, 0:1], bias=191.5 + 1.0 / 8192)
    for nm, q, row, src in (("dHi", "Y", 3, "Lhi"), ("dLo", "Y", 4, "Llo"), ("dV", "S", 5, "Lv")):
        once[nm] = lambda nm=nm, q=q, row=row, src=src: dma(q, nm, [(T.W1[row::16, PAD:PAD + HW], T[src][:])], 128,
                                                             zn + [src + "0", src + "1"], [nm])
    win1 = zn + ["zero", "zero2", "dHi", "dLo", "dV", "dC0", "dC1", "dC2"]

    const("ones", T.ones[0:8, 0:16], 1.0, 16, True, (), 0, 8)
    for b0 in (0, 8):
        for j, (out, n) in enumerate(((LAB[0:8, b0, 1:4:2], 2), (LAB[0:8, b0 + 4, :], 16), (LAB[0:8, b0, 0:5:2], 3), (LAB[0:8, b0 + 5, :], 16))):
            nm, k, sign = "f%d%d" % (b0, j), (j // 2) ^ (b0 // 8), -1.0 if b0 and j < 2 else 1.0
            a, num, r = T.ones[0:8, 0:n], T.Pf[0:8, k:k + 1], ["Pf", "ones", "LAB"]
            once[nm] = (lambda out=out, a=a, n=n, r=r, nm=nm, num=num: act(out, a, n, r, [nm], scale=num)) if nm in on_s else (
                lambda out=out, a=a, n=n, r=r, nm=nm, num=num, sign=sign: ts(out, a, num, sign, A.mult, A.mult, n, r, [nm]))
    for nm, blk, k, c in (("k8", 8, 5, -1.5), ("k14", 14, 2, 0.5), ("k0c", 0, 5, -15.5)):
        const(nm, LAB[0:8, blk, k:k + 1], c, 1, True, ["LAB"], 0, 8)
    once["GO2"] = lambda: mark(T.GO2[0:8, :], zero[0:8], [[0, 8], [-1, 8], [0, 2]], 0.25, 0, 128, ["GO2"])
    psK, psX = T.psB0[:, 0:16, :], T.psB1[:, 16:32, :]
    once["mmK"] = lambda: mm([(psK[0:112], LAB[0:8, 8:15, :], T.GO2[0:8, :], True, True)], 128,
                             ["hi0", "lo0", "hi1", "lo1", "k8", "k14", "f80", "f81", "f82", "f83", "GO2"], "B0", w=["mmK"])
    once["mmX"] = lambda: mm([(psX[0:KR], LAB[0:8, 0:6, :], T.GO2[0:8, :], True, True)], 128,
                             ["hi0", "lo0", "k0c", "f00", "f01", "f02", "f03", "GO2"], "B1", w=["mmX"])
    const("maskz", T.mask[:], 0.0, 128, True)
    const("mask8", T.mask[0:8, :], 1.0, 128, True, ["maskz"], 0, 8)
    const("mask4", T.mask[KR:KT, :], 4.0, 128, True, ["maskz"], KR, KT)
    rowis = [[-2, 8], [0, 8], [-1, 2]]
    once["maskx"] = lambda: mark(T.mask[:], T.mask[:], rowis, 1.0, -64, 128, ["maskx"], ["mask8", "mask4"])
    once["masky"] = lambda: mark(T.mask[:], T.mask[:], rowis, 1.0, -80, 128, ["masky"], ["maskx"])
    for nm, rows, pt, base, r in (("mask5", 5, [[32, 2], [0, 64]], 0, "masky"), ("maskb", 4, [[0, 64], [8, 2]], 0, "mask5"),
                                  ("mask3", 3, [[0, 2], [8, 4], [0, 16]], 0, "maskb"), ("mask2", 2, [[0, 128]], 1, "mask3")):
        once[nm] = lambda nm=nm, rows=rows, pt=pt, base=base, r=r: iota(T.mask[0:rows, :], pt, base, 128, [nm], [r])
    once["WK"] = lambda: tt(T.WK[0:KT, :], psK[0:KT], T.mask[0:KT, :], A.mult, 128, ["mask2", "mmK"], ["WK"], "B0")
    once["WX"] = lambda: tt(T.WX[0:KR, :], psX[0:KR], T.mask[0:KR, :], A.mult, 128, ["mask2", "mmX"], ["WX"], "B1")
    once["WN"] = lambda: [act(T.WN[0:KR, :], T.WK[0:KR, :], 128, ["WK"], ["WNa"], scale=-1.0),
                          act(T.WN[KR:KT, :], T.WK[KR:KT, :], 128, ["WK"], ["WNb"])]
    once["WZz"] = lambda: fill(T.WZ[:], 0.0, 136, ["WZz"])
    wz = ["c0", "c1c", "c2", "c3", "c4", "c5", "c6", "c7"]
    for c, nm in enumerate(wz):
        once[nm] = lambda c=c, nm=nm: (act if nm in on_s else cpy)(T.WZ[0:KR, 1::2, 2 * c:2 * c + 2], T.WK[0:KR, 16 * c:16 * c + 16], 16,
                                                                   ["WK", "WZz"], ["WZ" + nm])
    wz = ["WZ" + nm for nm in wz]

    once["SPz"] = lambda: fill(T.SP0[:], 0.0, 68, ["SPz"])
    once["SP1z"] = lambda: fill(T.SP1[:], 0.0, 68, ["SP1z"])
    const("SQz", T.SQ0[:], 0.0, 64, True)
    const("SP1s", T.SP0[0:8, 1::2, :], 1.0, 64, True, ["SPz"], 0, 8)
    const("SQ1s", T.SQ0[0:8], 1.0, 64, True, ["SQz"], 0, 8)
    const("SQt", T.SQ0[KR:KT], 1.0, 64, True, ["SQz"], KR, KT)
    for nm, val, gx, gy in (("SP", T.SP0[:, 1::2, :], [[16, 8], [0, 4], [128, 2]], [[0, 8], [64, 4], [0, 2]]),
                            ("SQ", T.SQ0[:], [[0, 4], [128, 2], [16, 8]], [[64, 4], [0, 16]])):
        once[nm + "x"] = lambda nm=nm, val=val, gx=gx: iota(val[0:2], gx, 0, 64, [nm + "x"], [nm + "1s"])
        once[nm + "y"] = lambda nm=nm, val=val, gy=gy: iota(val[0:1], gy, 0, 64, [nm + "y"], [nm + "x"])
    once["hcol"] = lambda: mark(T.hcol[:, 0:1], zero[:, 0:1], [[0, 1]], 256.0, -1, 1, ["hcol"])
    once["SP1c"] = lambda: act(T.SP1[0:8, 1::2, :], T.SP0[0:8, 1::2, :], 64, ["SPy", "SP1z", "hcol"], ["SP1c"], bias=T.hcol[0:8, 0:1])
    once["SQ1"] = lambda: act(T.SQ1[0:KT, :], T.SQ0[0:KT, :], 64, ["SQy", "SQt", "hcol"], ["SQ1"], bias=T.hcol[0:KT, 0:1])
    places = dict(SP0=["SPy"], SP1=["SP1c"], SQ0=["SQy", "SQt"], SQ1=["SQ1"])

    for k, (r0, c0, r1, c1) in enumerate(((3, 1.0 / 32768, 4, 1.0 / 32768), (6, -0.5, 7, 1.0 / 8192), (5, 128.0, 6, MAGIC))):
        nm, out = "s1%d" % k, T.SEL1[:, :, k]
        once[nm] = lambda nm=nm, out=out, r0=r0, c0=c0: mark(out, zero[:, 0:8], [[-16, 8]], c0, -r0, 8, [nm])
        once[nm + "b"] = lambda nm=nm, out=out, r1=r1, c1=c1: mark(out, out, [[-16, 8]], c1, -r1, 8, [nm + "b"], [nm])
    three = T.SEL2[:, :, 2:5]
    once["e2a"] = lambda: mark(three, zero[:, 0:24], [[16, 8], [0, 3]], 1.0 / 32, 6, 24, ["e2a"], ["zero"], A.is_gt, -1)
    once["e2b"] = lambda: mark(three, three, [[16, 8], [-1, 3]], 0.0, 9, 24, ["e2b"], ["e2a"], A.is_gt, -1)
    once["e2c"] = lambda: mark(T.SEL2[:, :, 2:4], T.SEL2[:, :, 2:4], [[-16, 8], [-1, 2]], 1.0 / 2048, 0, 16, ["e2c"], ["e2b"])
    for k, c in ((0, 32.0), (1, -32.0)):
        once["e2%d" % k] = lambda k=k, c=c: mark(T.SEL2[:, :, k], zero[:, 0:8], [[-16, 8]], c, -2, 8, ["e2%d" % k])
    sel2 = ["e20", "e21", "e2c"]
    once["Ineg"] = lambda: mark(T.Ineg[:], zero, [[-8, 2], [-1, 8], [-16, 8]], -32768.0, 0, 128, ["Ineg"])
    once["Ib"] = lambda: mark(T.Ib[:], zero, [[-1, 128]], 1.0, 0, 128, ["Ib"])
    once["Pr"] = lambda: mark(T.Pr[0:64, 0:64], zero[0:64, 0:64], [[-1, 8], [-8, 8]], 1.0, 0, 64, ["Pr"])
    const("DXa", T.DX[:, 0::3], 0.0, 128, False)
    const("DXb", T.DX[:, 2::3], 1.0, 128, False)
    once["RZ"] = lambda: iota(T.RZ[:, :, 0:130:2], [[0, 260]], 0, 260, ["RZ"])
    once["D5z"] = lambda: fill(T.D5[:], 0.0, 160, ["D5z"])
    once["D5"] = lambda: iota(T.D5[:, 0::5], [[0, 64]], 1, 64, ["D5"], ["D5z"])
    once["Rs"] = lambda: iota(T.Rs[:], [[0, 128]], 0, 128, ["Rs"])
    once["GSEL"] = lambda: [
        mm([(T.psA0[:, 256:272], T.mask[64:80, :], T.Ib[64:80, 64:80], True, True)], 64, ["mask2", "Ib"], "A0"),
        act(T.GSEL[:], T.psA0[:, 256:272], 16, (), ["GSEL"], "A0"),
        act(T.GSELF[:, 0:16], T.psA0[:, 256:272], 16, (), ["GSEL3"], "A0", scale=-3.0),
        act(T.GSELF[:, 16:32], T.psA0[:, 256:272], 16, (), ["GSEL2"], "A0", scale=-2.0)]

    def last_setup():
        fill(T.W2[:, 0:PAD], 0.0, 64, ["W2a"])
        fill(T.W2[:, PAD + HW:WC], 0.0, 64, ["W2b"])
        fill(T.D3[:], 0.0, 96, ["D3z"])
        cpy(T.I16[:], T.Ib[:], 64, ["Ib"], ["I16"])
        mark(T.Pm[:], zero, [[-1, 16], [-16, 8]], 1.0, 0, 128, ["Pm"])
        act(T.I17[:], T.Ineg[:], 128, ["Ineg"], ["I17"], scale=-1.0 / (1 << 32))
        act(T.SEL3[:, :, 0:2], T.SEL2[:, :, 0:2], 16, sel2, ["SEL3a"])
        sfill(T.SEL3[:, :, 2], 0.0, 8, ["SEL3b"])
        fill(T.D3[:, 0::3], 1.0, 32, ["D3"], ["D3z"])
        for h in (0, 1):
            sfill(T["OF%d" % h][:, 0:130:2], 0.0, 65, ["OFz%d" % h])

    arrived = {}
    senders = peers

    def half_pass(p, h):
        n = lambda s: "%s%d" % (s, h)
        B = lambda s: T[n(s)]
        pA, pB, pC, pD = B("psA"), B("psB"), B("psC"), B("psD")
        bA, bB, bC, bD = n("A"), n("B"), n("C"), n("D")
        G, SP, SQ, O1, P5, H, OF = B("G"), B("SP"), B("SQ"), B("O1"), B("P5"), B("H"), B("OF")
        sp = places[n("SP")] + ([n("SPs")] if p else [])
        sq = places[n("SQ")] + ([n("SQs")] if p else [])
        GL, GI = CFG["GL"][p][h], CFG["GI"][p][h]
        ns = 3 if p == 2 else 5
        slot = lambda k: pD[:, k:64 * ns:ns]
        R1, R2 = T.RZ[:, 2 * h, :], T.RZ[:, 2 * h + 1, :]
        s = 2 * p + h
        mine = rank // 2

        def add(j):
            x = T.Rs[0:64, s - 2, :] if j < 0 else T.LAND[0:64, 3 * (s - 2) + j, :]
            for ps, turn, nm, bk in ((pB[64:KR, 16:24, :], T.Pr, "Pr", bB), (pA[64:KR, 0:64], T.Ib, "Ib", bA)):
                mm([(ps, x, turn[0:64, 0:64], j < 0, j == 2)], 64, [nm, "Rs%d" % (s - 2)], bk, [arrived[s - 2][j]] if j >= 0 else ())

        def clamp():
            add(2)
            ts(SP[64:KR, 1::2, :], pB[64:KR, 16:24, :], -31.0, 31.0, A.max, A.min, 64, (), [n("SPs")], bB)

        def clamp2():
            ts(SQ[64:KR, :], pA[64:KR, 0:64], -31.0, 31.0, A.max, A.min, 64, (), [n("SQs")], bA)

        def distance():
            mm([(pB[:, 0:8, 4 * b:4 * b + 4], T.WZ[0:KR, 1 - e:17 - e, b::2], SP[0:KR, 1::2, e::2], e == 0, e == 1)
                for b in (0, 1) for e in (0, 1)], 256, sp + wz + ["hc"], bB, w=[] if p else [n("Gfree")])
            ts(B("zoff")[:], pB[:, 0:8, :], float(PAD), float(WC - 1), A.add, A.min, 64, (), [n("zoff")], bB)

        def look(offs, cuts, j):
            a, b = ((0,) + tuple(cuts) + (64,))[j:j + 2]
            if b > a:
                gather("VVSS"[j], G[:, 16 * a:16 * b], T.W1, B(offs)[:, a:b], b - a, win1 + [n(offs), n("Gfree")], [n("G%d_" % j)])
        gs = lambda cuts: [n("G%d_" % j) for j, (a, b) in enumerate(zip((0,) + tuple(cuts), tuple(cuts) + (64,))) if b > a]

        def floor_x():
            psX = pB[:, 8:16, :]
            mm([(psX, SP[0:KR, 1 - b:17 - b, :], T.WX[0:KR, b::2], b == 0, b == 1) for b in (0, 1)], 128, sp + ["WX", "WK"], bB)
            ts(T.DX[:, 192 * h + 1:192 * h + 192:3], psX, MAGIC8, -MAGIC8, A.add, A.add, 64, (), [n("x")], bB)

        def sides():
            mm([(slot(0), T.WN[0:KT, :], SQ[0:KT, :], p == 2, False), (slot(1), T.WK[0:KT, :], SQ[0:KT, :], False, False)],
               128, sq + ["WK", "WNa", "WNb"], bD)

        def clear():
            mm([(slot(k), zero[0:1, :], zero[0:1, 0:64], k == 2, False) for k in (2, 3, 4)], 192, ["zero"], bD)

        def turn1():
            mm([(pC[:, 24 * c:24 * c + 24], G[:, c::8], T.SEL1[:], True, True) for c in range(8)], 512,
               gs(GL) + ["s10b", "s11b", "s12b"], bC, w=[n("Gfree")])

        def pixel():
            scan(O1[:], T.DX[:, 192 * h:192 * h + 192], pC[:, 0:192], A.mult, A.add, 192, [n("x"), "DXa", "DXb"], [n("O1")], bC)
            ts(B("off")[:], O1[:, 2::3], -COL0, float(WC - 1), A.add, A.min, 64, [n("O1")], [n("off")])

        def beyond():
            act(R1[:, 1:129:2], O1[:, 1::3], 64, [n("O1"), "RZ"], [n("R1")], scale=8192.0, bias=-63.5 * 8192, f=F.Relu)
            act(R2[:, 1:129:2], O1[:, 1::3], 64, [n("O1"), "RZ"], [n("R2")], scale=-8192.0, bias=-64.5 * 8192, f=F.Relu)
            if p == 2:
                act(OF[:, 1:129:2], O1[:, 2::3], 64, [n("O1"), n("OFz")], [n("OF")], bias=-COL0)

        def off_image():
            mm([(slot(0), R[:, 1 - b:129 - b], T.Ineg[:, 64 * b:64 * b + 64], False, False) for R in (R1, R2) for b in (0, 1)], 256,
               [n("R1"), n("R2"), "Ineg"], bD)
            if p == 2:
                mm([(slot(2), OF[:, 1 - b:129 - b], T.I17[:, 64 * b:64 * b + 64], False, False) for b in (0, 1)], 512, [n("OF"), "I17"], bD)

        def turn2():
            sel, seln = (T.SEL3, ["SEL3a", "SEL3b"]) if p == 2 else (T.SEL2, sel2)
            mm([(pD[:, 8 * ns * e:8 * ns * (e + 1)], G[:, e::8], sel[:], False, e == 7) for e in range(8)], 512,
               gs(GI) + seln, bD, w=[n("Gfree")])

        def test():
            if p < 2:
                scan(P5[:], T.D5[:], pD[:, 0:320], A.max, A.min, 320, ["D5"], [n("P5")], bD)
            else:
                scan(B("O3")[:], T.D3[:], pD[:, 0:192], A.max, A.min, 192, ["D3"], [n("O3")], bD)
                ts(B("offb")[:], B("O3")[:, 2::3], float(1 << 17), float(WC - 1), A.mult, A.min, 64, [n("O3")], [n("offb")])

        def write():
            mm([(pA[0:64, 128:160], P5[:, 4::5], T.GSELF[:], True, False), (pA[0:64, 128:144], P5[:, 2::5], T.GSEL[:], False, False),
                (pA[0:64, 144:160], P5[:, 3::5], T.GSEL[:], False, True)], 192, [n("P5"), "GSEL", "GSEL3", "GSEL2"], bA)
            act(T.Rs[0:64, s, :], pA[0:64, 128:160], 32, ["Rs"], ["Rs%d" % s], bA, scale=2048.0)
            k = send([(peers, mask, "arr%d_%d" % (s, rank), T.Rs[:, s, :], [T.LAND[:, 3 * s + j, :] for j in range(3)])], ["Rs", "Rs%d" % s])
            arrived[s] = [op("-", None, ("c", j + 1), after=[k], sem="arr%d_%d" % (s, q), val=neng) for j, q in enumerate(senders)]

        def fetch(j):
            c0, k = 32 * (mine if j else 1 - mine), CFG["GF"][h] // 2
            for eng, a, b in (("V", c0, c0 + k), ("S", c0 + k, c0 + 32)):
                gather(eng, H[:, 16 * a:16 * b], T.W2, B("offb")[:, a:b], b - a,
                       ["W2a", "W2b", "W20", "W21", "W22", n("offb")], [n("H%d%s" % (j, eng))])

        def give(j):
            pair = mine if j else 1 - mine
            ps, bk = (pA, bA) if j else (pC, bC)
            mm([(ps[:, 256 + b:320:2], T.Pm[:], H[:, 512 * pair + 2 * a + b:512 * pair + 512:16], a == 0, a == 7)
                for b in (0, 1) for a in range(8)], 1024, [n("H%dV" % j), n("H%dS" % j), "Pm"], bk)
            cpy(T.Ys[:, 2 * pair:2 * pair + 2, 32 * h:32 * h + 32], ps[:, 256:320], 64, (), [n("Ys%d_" % j)], bk)
            if h == 0:
                return
            to = [q for q in (2 * pair, 2 * pair + 1) if q != rank]
            ms = halves if len(to) == 2 else [mask]
            k = send([([q], m, "arr4_%d" % rank, T.Ys[:, q, :], [T.LY[:, rank, :]]) for q, m in zip(to, ms)], ["Ys%d_0" % j, "Ys%d_1" % j])
            arrived.setdefault(4, []).extend(
                (q, op("-", None, ("c", len(to)), after=[k], sem="arr4_%d" % q, val=neng // len(to))) for q in to)

        def store():
            mm([(pB[:, 32:40, :], T.I16[:], T.Ys[:, rank, :], True, False)], 64, ["I16", "Ys1_0", "Ys1_1"], bB)
            for j, (q, k) in enumerate(arrived[4][:2]):
                mm([(pB[:, 32:40, :], T.I16[:], T.LY[:, q, :], False, j == 1)], 64, ["I16"], bB, [k])
            q, k = arrived[4][2]
            tt(T.Fo[:], pB[:, 32:40, :], T.LY[:, q, :], A.add, 64, (), ["Fo"], bB, [k])
            dma("Y", "dY", [(T.y[:], T.Fo[:])], 16, ["Fo"], ())
        return dict(a=lambda: add(-1), b=lambda: add(0), c=lambda: add(1), d=clamp, z=distance,
                    l=lambda: look("zoff", GL, 0), L=lambda: look("zoff", GL, 1), j=lambda: look("zoff", GL, 2),
                    J=lambda: look("zoff", GL, 3), x=floor_x, k=clear, m=sides, t=turn1, n=pixel, q=clamp2, p=beyond,
                    i=lambda: look("off", GI, 0), I=lambda: look("off", GI, 1), h=lambda: look("off", GI, 2),
                    H=lambda: look("off", GI, 3), u=off_image, r=turn2, s=test, w=write,
                    f=lambda: fetch(0), g=lambda: give(0), F=lambda: fetch(1), G=lambda: give(1), E=store)

    def load_w2(k, r, after):
        a0 = sum(CFG["W2"][:k])
        dma("Y", "dW%d" % k, [(T.W2[16 * a:16 * a + 16, PAD:PAD + HW], T.cam[:]) for a in range(a0, a0 + CFG["W2"][k])],
            256 * CFG["W2"][k], r, ["W2%d" % k], after)

    once["dW0"] = lambda: load_w2(0, win1, ())
    for p in range(len(ORDER)):
        steps = [half_pass(p, 0), half_pass(p, 1)]
        for name in ORDER[p].split():
            (once[name] if p == 0 and name in once else steps[int(name[1])][name[0]])()
        if p == 0:
            last_setup()
            load_w2(1, (), [arrived[1][2]])
        if p == 1:
            load_w2(2, (), [arrived[3][2]])
    return ops, sent[0]


def rank_program(g, core, T, topo):
    if T.rank_of(core) is None:
        return
    ops, sent = build(g, core, T, topo)
    queue = {"V": g.vector, "S": g.scalar, "P": g.tensor, "G": g, "Y": g.sync}
    count = {"sV": 0, "sS": 0, "sP": 0, "sG": 0}
    token, waited, totals = {}, {}, {}

    def needs(o):
        return [d for d in o["deps"] if not (ops[d]["eng"] == o["eng"] == "P" or ops[d]["sem"] == "none")]
    wanted = set()
    for o in ops:
        if o["eng"] != "-":
            wanted.update(needs(o))
    for k, o in enumerate(ops):
        eng = o["eng"]
        if eng == "-":
            token[k] = (o["sem"], o["val"])
            totals[o["sem"]] = o["val"]
            continue
        want = {}
        for d in needs(o):
            s, v = token[d]
            want[s] = max(want.get(s, 0), v)
        for s in sorted(want):
            if waited.get((eng, s), 0) < want[s]:
                queue[eng].wait_ge(T.sem[s], want[s])
                waited[(eng, s)] = want[s]
        ins = o["fn"]()
        if o["sem"] is None:
            if k in wanted:
                s = "s" + eng
                count[s] += 1
                ins.then_inc(T.sem[s], 1)
                token[k] = (s, count[s])
        elif o["sem"] != "none":
            token[k] = (o["sem"], o["val"])
            totals[o["sem"]] = o["val"]
    totals.update(count)
    totals["sent"] = sent
    seen = {}
    for (e, s), v in waited.items():
        seen[s] = max(seen.get(s, 0), v)
    for s in totals:
        if totals[s] > seen.get(s, 0):
            g.wait_ge(T.sem[s], totals[s])
